import numpy as np, ml_dtypes
CORES = [6,15,38,47]
N = 4
BF = ml_dtypes.bfloat16
M, P, W, ST, SH, VM = 8192, 1024, 256, 4, 1, 1024
NB, VB = 8161, 1023
AIM = np.array([255] * 14 + [16, 1])
def spot(u):
    return ((u * 241) >> 6) & (P - 1)
def lanes(u):
    b = u % 255
    return np.array([min(15, max(0, u // 255 - 15 * i)) for i in range(14)] + [b // 16, b % 16])
def aim(rng, c):
    u = np.arange(53000); return lanes(int(rng.choice(u[spot(u) == c])))
def below(rng, n):
    return (rng.random((N, 8, 16, n.shape[3]), dtype=np.float32) * n.astype(np.float32)).astype(np.int32)
def names(rng, pool, share, n):
    z = (N, 8, 16, n); p = np.take_along_axis(np.broadcast_to(pool, (N,) + pool.shape), rng.integers(0, pool.shape[2], z), 3)
    return np.where(rng.random(z) < share, p, rng.integers(0, M, z))
def parts(rng):
    g = below(rng, rng.integers(5, 17, (N, 8, 1, M))); e = below(rng, rng.integers(4, 17, (N, 8, 1, M)))
    pool = rng.integers(0, M, (8, 16, 6)); asl = rng.random((N, 8, 16, W)) < 0.5
    nm = np.where(asl, names(rng, pool, 0.8, W), names(rng, pool, 0.0, W))
    k = np.where(rng.random((N, 8, 16, P)) < 0.7, names(rng, pool, 0.7, P), M)
    return {"g": g, "e": e, "y": below(rng, rng.integers(8, 17, (N, 8, 1, P))), "k": k, "x": rng.integers(0, 16, (N, 8, 16, W)), "nm": nm, "asl": asl,
            "d": rng.integers(4, 15, (N, 8, 16, ST)), "h": rng.integers(0, 256, (N, 8, 16, 1)), "th": rng.integers(50, 101, (N, 8, 1, 1))}
def pack(s):
    def fl(a, n): return np.ascontiguousarray(a.reshape(N, 128, n)).astype(np.float32).astype(BF)
    def wh(a, n): return np.ascontiguousarray(a.reshape(N, 128, n)).astype(np.int32)
    return {"fx": fl(s["g"] + 16 * s["e"], M), "y0": fl(s["y"], P), "k0": wh(s["k"], P), "x0": fl(s["x"], W), "t0": wh(s["nm"] + M * s["asl"].astype(np.int64), W),
            "dw": wh(s["d"], ST), "hw": wh(s["h"], 1), "th": wh(np.repeat(s["th"], 16, axis=2), 1)}
def setup_inputs(rng):
    return pack(parts(rng))
def setup_inputs_spread(rng):
    s = parts(rng)
    s["g"] = below(rng, np.exp2(4 * rng.random((N, 8, 1, M))).astype(np.int64) + 1); s["e"] = below(rng, np.exp2(4 * rng.random((N, 8, 1, M))).astype(np.int64) + 1)
    s["g"] = np.minimum(s["g"], 15); s["e"] = np.minimum(s["e"], 15)
    s["x"] = np.minimum(below(rng, np.exp2(1 + 3 * rng.random((N, 8, 1, W))).astype(np.int64) + 1), 15)
    s["y"] = np.minimum(below(rng, np.exp2(1 + 3 * rng.random((N, 8, 1, P))).astype(np.int64) + 1), 15)
    s["asl"] = rng.random((N, 8, 16, W)) < rng.random((N, 8, 1, W))
    uneven = np.minimum(np.exp2(np.log2(M) * rng.random((N, 8, 16, W))).astype(np.int64) - 1, M - 1)
    s["nm"] = np.where(rng.random((N, 8, 1, W)) < 0.5, uneven, s["nm"])
    s["k"] = np.where(rng.random((N, 8, 16, P)) < rng.random((N, 8, 1, P)), s["k"], M)
    s["h"] = np.minimum(np.exp2(8 * rng.random((N, 8, 16, 1))).astype(np.int64), 255)
    s["d"] = rng.integers(1, 17, (N, 8, 16, ST)); s["th"] = rng.integers(0, 241, (N, 8, 1, 1))
    return pack(s)
def setup_inputs_ends(rng):
    s = parts(rng); z = (N, 8, 16, W)
    f = np.where(rng.random((N, 8, 1, M)) < 0.8, 255 * rng.integers(0, 2, (N, 8, 16, M)), s["g"] + 16 * s["e"])
    f[..., 0] = 0; f[..., 1] = 48; f[..., NB] = 0; f[..., M - 1] = 255
    s["g"] = f & 15; s["e"] = f >> 4
    th = np.where((np.arange(N)[:, None] + np.arange(8)[None, :]) % 2 == 0, 240, 0).reshape(N, 8, 1, 1)
    th[::2, 6] = 239; th[1::2, 6] = 1; s["th"] = th
    r = rng.random((N, 8, 1, P)); s["y"] = np.where(r < 0.3, 15, np.where(r < 0.6, 0, 15 * rng.integers(0, 2, (N, 8, 16, P))))
    s["y"][..., spot(61200)] = np.where(th[..., 0] >= 239, 0, 15)
    for q in range(1, N, 2):
        b = (q >> 1) & 1; s["y"][q, 6, 15, spot(61200)] = 14 - b; s["y"][q, 6, :, 0] = 0; s["y"][q, 6, 15, 0] = 2 - b
    r = rng.random((N, 8, 16, P)); s["k"] = np.where(r < 0.4, 0, np.where(r < 0.8, M, np.where(r < 0.9, M - 1, s["k"])))
    kind = rng.choice(4, (N, 8, 1, W), p=[0.3, 0.2, 0.3, 0.2]); kind[..., W - 4:] = np.array([3, 2, 1, 0])
    x = np.where(kind == 0, 15, np.where(kind == 1, 0, np.where(kind == 2, 15 * rng.integers(0, 2, z), 7)))
    both = (2 * M - 1) * rng.integers(0, 2, z); r = rng.random(z)
    t = np.where((kind == 0) | (r < 0.75), both, np.where(r < 0.85, M - 1, np.where(r < 0.95, M, s["nm"] + M * s["asl"])))
    t = np.where(kind == 3, np.where((np.arange(16) % 2 == 0)[None, None, :, None], 1, 2 * M - 1), t)
    h = 255 * rng.integers(0, 2, (N, 8, 16, 1)); h[:, 0] = 255; h[:, 6] = 255; h[:, 7] = 255; h[:, 3] = 0; h[:, 5, :, 0] = AIM
    for q in range(N):
        for w in (1, W - 6, W - 5):
            x[q, 5, :, w] = aim(rng, P - 1); t[q, 5, :, w] = both[q, 5, :, w]
        for w in (2, W - 8):
            x[q, 5, :, w] = lanes(int(rng.choice(np.arange(VB, 53000, VM)))); t[q, 5, :, w] = NB
    s["x"] = x; s["nm"] = t & (M - 1); s["asl"] = t >= M; s["h"] = h
    s["d"] = np.where(rng.random((N, 8, 16, ST)) < 0.5, 16, 1)
    return pack(s)
def setup_inputs_corners(rng):
    s = parts(rng); z = (N, 8, 16, W); row = np.arange(16)[None, None, :, None]
    o = np.argsort(rng.random((N, 8, 16, 64)), axis=2); s["g"][..., :64] = np.where(o < 8 + np.arange(64) % 4, 0, 15)
    s["g"][..., M - 1] = 0; s["e"][..., M - 1] = 0; s["g"][..., M - 2] = 15
    kind = rng.integers(0, 8, (N, 8, 1, W)); kind[:, 5, :, :8] = 1; kind[:, 5, :, W - 8:] = 1
    x = np.where(kind == 7, s["x"], rng.integers(1, 14, z)); one = rng.integers(0, 16, (N, 8, 1, W)); end = 15 * rng.integers(0, 2, (N, 8, 1, W))
    low = rng.integers(0, 64, z); nm = s["nm"]
    asl = np.where(kind == 0, True, np.where(kind <= 4, False, np.where(kind == 5, row != end, s["asl"])))
    nm = np.where(kind == 1, M - 1, np.where(kind == 2, M - 2, np.where(kind == 3, np.where(row == one, M - 1, M - 2), nm)))
    nm = np.where((kind == 4) | ((kind == 5) & (row == end)), low, np.where(kind == 6, (M - 1) * rng.integers(0, 2, z), nm))
    s["h"][:, 5, :, 0] = AIM; s["h"][:, 2] = 255; s["h"][:, 6, 15] = 0
    s["d"] = rng.choice(np.array([1, 2, 8, 15, 16]), (N, 8, 16, ST))
    s["th"] = rng.choice(np.array([0, 1, 60, 240]), (N, 8, 1, 1)); s["th"][:, 0] = 1; s["th"][:, 4] = 0; s["th"][:, 7] = 240
    r = rng.random((N, 8, 1, P)); s["k"] = np.where(r < 0.25, M, np.where((r < 0.5) & (s["k"] == M), (M - 1) * rng.integers(0, 2, (N, 8, 16, P)), s["k"]))
    for q in range(N):
        for w in list(range(8)) + list(range(W - 8, W)):
            x[q, 5, :, w] = aim(rng, (0, P - 1)[(w + q) & 1])
        for g in range(8):
            w = np.flatnonzero(kind[q, g, 0] == 0)
            if len(w) == 0: continue
            xs = np.array(x[q, g][:, w]); c = spot(np.add.reduce(s["h"][q, g] * xs, axis=0))
            xs[15] = xs[15] + rng.integers(0, 3, len(w)); s["y"][q, g][:, c] = xs
            m = rng.random((16, len(w))); own = nm[q, g][:, w]
            s["k"][q, g][:, c] = np.where(m < 0.6, own, np.where(m < 0.8, M, (own + 1) & (M - 1)))
    s["x"] = x; s["nm"] = nm; s["asl"] = asl
    return pack(s)
def setup_inputs_crowd(rng):
    s = parts(rng); row = np.arange(16)[None, None, :, None]; w = np.arange(W)[None, None, None, :]
    s["e"][:, :3] = 0; s["g"][:, 0] = 0; a = rng.integers(0, 16, (8, 16, 1)); a[:, 0] = 2; s["x"][:, :3] = a[None, :3]
    for q in range(N): s["x"][q, 1, :, (0, W - 1)[q & 1]] = 15 - a[1, :, 0]
    b = rng.integers(0, 3, (N, 1, W)); s["x"][:, 2] = np.where(b == 0, a[None, 2], np.where(b == 1, 15 - a[None, 2], (a[None, 2] + 5) & 15))
    s["h"][:, 3] = 0
    one = rng.integers(0, 16, (N, 1, 1, W)); s["asl"][:, :1] = np.where(w % 4 == 0, False, np.where(w % 4 == 1, row == one, s["asl"][:, :1]))
    two = rng.integers(0, M, (8, 16, 2)); t = names(rng, two, 1.0, W); k = names(rng, two, 1.0, P)
    s["nm"][:, :4] = np.where(s["asl"], t, s["nm"])[:, :4]; s["k"][:, :4] = np.where(s["k"] < M, k, M)[:, :4]
    s["th"][:, 0] = 0; s["th"][:, 1] = 240 * rng.integers(0, 2, (N, 1, 1))
    s["e"][:, 4] = 0; s["h"][:, 4, :, 0] = AIM
    s["asl"][:, 5] = True; s["x"][:, 5] = rng.integers(1, 15, (N, 16, W)); s["g"][:, 5, :, 0] = 0; s["e"][:, 5, :, 0] = 15; s["d"][:, 5, :, 0] = 1
    for q in range(N):
        o = rng.permutation(53000); i = np.unique(spot(o), return_index=True)[1]
        i = rng.permutation(np.concatenate([i[:1], i[-1:], rng.permutation(i[1:-1])[:W - 2]]))
        s["x"][q, 4] = np.stack([lanes(int(j)) for j in o[i]], axis=1); s["th"][q, 4] = 16 * (q & 1)
        m = (2, 4, 8, W)[q & 3]; at = np.arange(m - 1, W, m); ro = rng.integers(0, 15, len(at))
        s["asl"][q, 5, ro, at] = False; s["nm"][q, 5, ro, at] = 0
    s["asl"][:, 6] = False; s["g"][:, 6] = 15; s["g"][:, 6, :, 0] = 0; s["e"][:, 6, :, 0] = np.minimum(s["e"][:, 6, :, 0], 14); s["x"][:, 6] = np.minimum(s["x"][:, 6], 14)
    s["nm"][:, 6] = np.where(row[0] == one[:, 0], 0, np.maximum(s["nm"][:, 6], 1))
    return pack(s)
def check_inputs(d):
    bad = []
    for k, lo, hi in (("fx", 0, 255), ("y0", 0, 15), ("k0", 0, M), ("x0", 0, 15), ("t0", 0, 2 * M - 1), ("dw", 1, 16), ("hw", 0, 255), ("th", 0, 240)):
        a = np.asarray(d[k]).astype(np.float64)
        if not (np.min(a) >= lo and np.max(a) <= hi): bad.append("range of " + k)
        elif not np.all(a == np.floor(a)): bad.append("whole numbers in " + k)
    a = np.asarray(d["th"]).reshape(-1, 16)
    if not np.all(a == a[:, :1]): bad.append("th alike in a group")
    return bad
def reference(fx, y0, k0, x0, t0, dw, hw, th):
    F = fx.astype(np.float32).astype(np.int32).reshape(N, 8, 16, M); Y = y0.astype(np.float32).astype(np.int32).reshape(N, 8, 16, P); K = np.array(k0, np.int32).reshape(N, 8, 16, P)
    X = x0.astype(np.float32).astype(np.int32).reshape(N, 8, 16, W); t1 = np.array(t0, np.int32).reshape(N, 8, 16, W)
    T = t1 & (M - 1); S = t1 >= M; A = np.zeros((N, 8, W), np.int32)
    dd = dw.reshape(N, 8, 16, ST); hh = hw.astype(np.int32).reshape(N, 8, 16, 1); top = th.reshape(N, 8, 16)[:, :, :1]
    row = np.arange(16, dtype=np.int32)[None, :, None]; turn = (np.arange(W) & 3)[None, :]
    for t in range(ST):
        if t > 0: X = np.roll(X, SH, axis=0); T = np.roll(T, SH, axis=0); S = np.roll(S, SH, axis=0); A = np.roll(A, SH, axis=0)
        for q in range(N):
            x = X[q]; nm = T[q]; asl = S[q]
            f = np.take_along_axis(F[q], nm.reshape(8, 1, 16 * W), 2).reshape(8, 16, 16, W)
            gu = f & 15; ef = f >> 4; xx = x[:, :, None, :]
            en = np.add.reduce((xx >= gu).astype(np.int32), axis=1) >= 9 + A[q][:, None, :]
            cand = en & ~asl; ci = cand.astype(np.int32); before = np.add.accumulate(ci, axis=1) - ci
            pos = np.minimum(turn, np.add.reduce(ci, axis=1) - 1)[:, None, :]
            go = cand & (before == pos)
            e = np.add.reduce(ef * go[:, None, :, :].astype(np.int32), axis=2, dtype=np.int32); ee = e[:, :, None, :]
            asl = asl | (cand & (before < pos))
            differ = np.abs(np.abs(xx - ef) - ee) != np.abs(np.abs(xx - ee) - ef)
            asl = asl & (np.add.reduce(differ.astype(np.int32), axis=1) < dd[q][:, :, t:t + 1])
            x = np.abs(x - e)
            u = np.add.reduce(hh[q] * x, axis=1); v = (u & (VM - 1))[:, None, :]
            nm = np.where(asl, nm, (((nm * (2 * v + 1)) >> 5) + nm + 37 * row) & (M - 1))
            c = ((u * 241) >> 6) & (P - 1)
            yc = np.take_along_axis(Y[q], c[:, None, :], 2); kc = np.take_along_axis(K[q], c[:, None, :], 2)
            hit = np.add.reduce(np.abs(yc - x), axis=1) <= top[q]; hb = hit[:, None, :]
            same = asl & (kc == nm)
            y1 = np.where(hb, yc, x); k1 = np.where(hb, np.where(same, kc, M), np.where(asl, nm, M))
            get = hb & (kc < M) & ~same
            nm = np.where(get, kc, nm); asl = asl & ~get
            for g in range(8):
                win = np.full(P, -1); np.maximum.at(win, c[g], np.arange(W)); at = np.flatnonzero(win >= 0)
                Y[q, g][:, at] = y1[g][:, win[at]]; K[q, g][:, at] = k1[g][:, win[at]]
            X[q] = x; T[q] = nm; S[q] = asl; A[q] = hit
    return {"yx": X.reshape(N, 128, W).astype(np.float32).astype(BF), "yt": (T + M * S.astype(np.int32)).reshape(N, 128, W).astype(np.float32),
            "yy": Y.reshape(N, 128, P).astype(np.float32).astype(BF), "yk": K.reshape(N, 128, P).astype(np.float32)}

@@ -1,0 +1,545 @@
+import numpy as np
+from concourse.bass import DstId, RemoteDMATransfer
+from concourse.mybir import AluOpType as A, ActivationFunctionType as AF
+
+NWS = [128, 128]
+C = len(NWS)
+REP = 2
+KA = 12
+DERD = 8
+SENDU = True
+BIG = 16384.0
+MAGIC = 12582912.0
+CY, PC, FV, FA, FP, LAT, LSELF, GR, SC = 1.0e-3, 0.5e-3, 0.06, 0.08, 0.01, 0.15, 0.08, 1.56, 3.8
+COMM, WIN, STG = 3.5, 0.15, 3.0
+EGA = False
+SPLIT = 3
+SEED, NOISE = 0, 0.0
+RANKS = {"dve('P', 7, 3)": 2, "pe('P', 2, 0)": 1, "dve('ta', 0, 8)": 20, "dve('ta', 1, 14)": 20, "act('ega', 1)": -4, "act('fall', 0)": -1, "dve('iu', 1)": 8, "act('P', 7, 0)": 4, "act('zc', 0)": 4, "act('ad', 1)": 8, "dve('tb', 1, 6)": 8, "dve('zg', 0, 15)": -2, "pe('P', 4, 0)": 4, "dve('pp', 1)": 1, "dve('yts', 0)": -4, "pe('P', 1, 's')": 4, "dve('off', 1)": 1, "dve('ss', 1)": -4, "dve('ta', 1, 2)": 8, "dve('nm1', 0)": -2, "act('P', 7, 1)": 4, "pe('P', 0, 's')": 2, "act('zg', 1, 0)": -8, "dve('of0', 0)": -1, "dve('ta', 1, 0)": 1, "dve('nn', 1)": -4, "dve('of0', 1)": 20, "dve('cb0', 1)": -2, "act('za', 1)": -2, "dve('yts', 1)": -8, "act('zg', 0, 4)": 8, "act('zg', 0, 0)": 8, "dve('zz', 0)": 2}
+GD = 0
+G0 = 8
+
+BF, F32, I32, U16 = "bfloat16", "float32", "int32", "uint16"
+SCRATCH = {
+    "ftab": ("sbuf", [128, 8192], BF), "fg": ("sbuf", [128, 4096], BF), "eg": ("sbuf", [128, 256, 16], BF),
+    "zg": ("sbuf", [128, 4096], BF), "ta": ("sbuf", [128, 4096], BF), "tb": ("sbuf", [128, 4096], BF),
+    "st": ("sbuf", [128, 1040], F32), "kin": ("sbuf", [128, 1024], I32), "yin": ("sbuf", [128, 1024], BF),
+    "w1": ("sbuf", [128, 1024], F32), "w2": ("sbuf", [128, 1024], F32), "yo": ("sbuf", [128, 1024], BF),
+    "tin": ("sbuf", [128, 256], I32), "tnm": ("sbuf", [128, 256], I32), "xin": ("sbuf", [128, 256], BF),
+    "din": ("sbuf", [128, 8], I32), "hin": ("sbuf", [128, 8], I32), "thin": ("sbuf", [128, 8], I32),
+    "xs": ("sbuf", [128, 4 * 512], BF), "ns": ("sbuf", [128, 4 * 256], F32), "us": ("sbuf", [128, 4 * 256], U16), "zs": ("sbuf", [128, 4 * 256], BF),
+    "lx": ("sbuf", [128, 4 * 512], BF), "ln": ("sbuf", [128, 4 * 256], F32), "lu": ("sbuf", [128, 4 * 256], U16), "lz": ("sbuf", [128, 4 * 256], BF),
+    "ci": ("sbuf", [128, 256], I32), "cj": ("sbuf", [128, 256], I32), "cf": ("sbuf", [128, 160], F32), "col": ("sbuf", [128, 32], F32),
+    "coli": ("sbuf", [128, 8], I32), "dm": ("sbuf", [128, 16 * 128], BF), "sw": ("sbuf", [128, 6 * 144], BF), "wt": ("sbuf", [128, 22 * 128], BF),
+    "ct": ("sbuf", [128, 12 * 128], BF), "bco": ("sbuf", [128, 16], U16), "iu": ("sbuf", [128, 32], U16), "cu": ("sbuf", [128, 32], U16),
+    "cd": ("sbuf", [128, 16], I32), "cd0": ("sbuf", [128, 16], I32), "of0": ("sbuf", [128, 16], F32), "off": ("sbuf", [128, 32], U16),
+    "yts": ("sbuf", [128, 256], F32),
+}
+for _n in ("cand", "pos", "go", "fall", "ee", "e0", "za", "zc", "le", "qq", "hi", "yq", "ad", "hd", "eq"):
+    SCRATCH[_n] = ("sbuf", [128, 256], BF)
+for _n in ("kc", "t1", "nm1", "zz", "kb", "kk", "y16"):
+    SCRATCH[_n] = ("sbuf", [128, 256], F32)
+for _n in ("pp", "q5", "ss", "nn", "cb0", "cb"):
+    SCRATCH[_n] = ("sbuf", [128, 256], I32)
+for _b in range(8):
+    SCRATCH["pb%d" % _b] = ("psum", [128, 512], F32)
+SEMAPHORES = ["pe", "dve", "act", "pool", "sent"] + ["d%d" % i for i in range(24)] + \
+    ["a%d_%d_%d" % (k, t, c) for k in range(2) for t in range(1, 4) for c in range(C)]
+
+
+def plan(ops):
+    n = len(ops)
+    succ = [[] for _ in range(n)]
+    for i, o in enumerate(ops):
+        for d in o["deps"] | o["soft"]:
+            succ[d].append(i)
+    pr = [0.0] * n
+    for i in range(n - 1, -1, -1):
+        o = ops[i]
+        pr[i] = o["dur"] + o["lat"] + max([pr[j] + LAT for j in succ[i]] + [0.0]) + o["bias"]
+    z = SEED * 7919 + 1
+    for i in range(n):
+        z = (z * 1103515245 + 12345) % 2147483648
+        pr[i] += NOISE * (z / 2147483648.0) + RANKS.get(ops[i]["tag"], 0)
+    left = [len(o["deps"] | o["soft"]) for o in ops]
+    ready = [i for i in range(n) if left[i] == 0]
+    fin = [0.0] * n; free = {}; bank = {}; lock = {}; order = []
+    while ready:
+        cands = []
+        for i in ready:
+            o = ops[i]
+            if o["grp"] is not None and lock.get(o["grp"][0], o["grp"][1]) != o["grp"][1]:
+                continue
+            t = free.get(o["eng"], 0.0)
+            for d in o["deps"] | o["soft"]:
+                t = max(t, fin[d] + (0.0 if d in o["chain"] else LSELF if ops[d]["eng"] == o["eng"] else LAT))
+            for b in o["banks"]:
+                for e, j in bank.get(b, {}).items():
+                    if e != o["eng"]:
+                        t = max(t, fin[j] + LAT)
+            cands.append((t, i))
+        t0, i0 = min(cands)
+        e0 = ops[i0]["eng"]
+        t, i = max([(tt, ii) for tt, ii in cands if ops[ii]["eng"] == e0 and tt <= t0 + WIN], key=lambda z: pr[z[1]] - STG * ops[z[1]]["stage"])
+        o = ops[i]
+        for b in o["banks"]:
+            for e, j in bank.get(b, {}).items():
+                if e != o["eng"]:
+                    o["deps"].add(j)
+            bank.setdefault(b, {})[o["eng"]] = i
+        if o["grp"] is not None:
+            if o["grp"][2]:
+                lock.pop(o["grp"][0], None)
+            else:
+                lock[o["grp"][0]] = o["grp"][1]
+        if o["eng"] is not None:
+            free[o["eng"]] = t + o["dur"]
+        o["t"] = t
+        fin[i] = t + o["dur"] + o["lat"]
+        order.append(i); ready.remove(i)
+        for j in succ[i]:
+            left[j] -= 1
+            if left[j] == 0:
+                ready.append(j)
+    assert len(order) == n
+    return order, max(fin)
+
+
+def emit(g, T, ops, order):
+    Q = {"pe": g.tensor, "dve": g.vector, "act": g.scalar, "pool": g, "sp": g.sync}
+    pos = {}; cnt = {}
+    for i in order:
+        o = ops[i]
+        if o["sem"] is None:
+            cnt[o["eng"]] = cnt.get(o["eng"], 0) + 1; pos[i] = (o["eng"], cnt[o["eng"]])
+        else:
+            pos[i] = (o["sem"][0], 1)
+    clock = {}; known = {e: {} for e in Q}; waits = {}; needed = set()
+    for i in order:
+        o = ops[i]
+        if o["eng"] is None:
+            clock[i] = {pos[i][0]: 1}
+            continue
+        k = known[o["eng"]]; w = []
+        for d in sorted(o["deps"] - o["chain"], key=lambda z: -ops[z]["t"]):
+            s, v = pos[d]
+            if k.get(s, 0) >= v:
+                continue
+            w.append(d); needed.add(d)
+            for s2, v2 in clock[d].items():
+                k[s2] = max(k.get(s2, 0), v2)
+        waits[i] = w
+        clock[i] = dict(k); clock[i][pos[i][0]] = pos[i][1]
+    last = {}
+    for i in order:
+        if ops[i]["sem"] is None and ops[i]["fin"]:
+            last[ops[i]["eng"]] = i
+    needed |= set(last.values())
+    val = {}; tot = {}
+    for i in order:
+        o = ops[i]
+        if o["sem"] is not None:
+            val[i] = o["sem"]; tot[o["sem"][0]] = o["sem"][1]
+        elif i in needed:
+            tot[o["eng"]] = tot.get(o["eng"], 0) + 1; val[i] = (o["eng"], tot[o["eng"]])
+    seen = set()
+    for i in order:
+        o = ops[i]
+        if o["eng"] is None:
+            continue
+        q = Q[o["eng"]]
+        for d in waits[i]:
+            q.wait_ge(T.sem[val[d][0]], val[d][1]); seen.add(val[d])
+        ins = o["fn"](q)
+        if o["sem"] is not None:
+            ins.then_inc(T.sem[o["sem"][0]], 16)
+        elif i in needed:
+            ins.then_inc(T.sem[o["eng"]], 1)
+    return [(s, v) for s, v in tot.items() if (s, v) not in seen]
+
+
+def build(T, dst, eng):
+    ops = []; lw = {}; rd = {}; nd = [0]; sent = [0]; stage = [0]
+
+    def op(e, fn, r, w, dur, banks=(), grp=None, sem=None, lat=0.0, soft=(), bias=0.0, fin=True):
+        i = len(ops); deps = set(); chain = set()
+        for k in r:
+            if k in lw:
+                deps.add(lw[k])
+        for k in w:
+            if k in lw:
+                deps.add(lw[k])
+                if e == "pe" and ops[lw[k]]["eng"] == "pe":
+                    chain.add(lw[k])
+            deps |= set(rd.get(k, []))
+        for k in r:
+            rd.setdefault(k, []).append(i)
+        for k in w:
+            lw[k] = i; rd[k] = []
+        deps.discard(i)
+        ops.append(dict(eng=e, fn=fn, deps=deps, chain=chain, soft=set(soft), dur=dur, banks=tuple(banks), grp=grp, sem=sem,
+                        lat=lat, bias=bias, fin=fin, stage=stage[0], tag=str(e) + str(w[0] if w else r[0])))
+        return i
+
+    def bk(keys):
+        return sorted(set(k[1] for k in keys if isinstance(k, tuple) and k[0] == "P"))
+
+    def dma(q, out, in_, r, w, us, slow=False):
+        s = "d%d" % nd[0]; nd[0] += 1
+        return op(q, lambda h: h.dma_start(out, in_), r, w, 0.05, sem=(s, 16), lat=2.0 + us)
+
+    def ts(out, in0, s1, s2, o0, o1, r, w, n, rate=1.0, **kw):
+        if o1 is None:
+            f = lambda h: h.tensor_scalar(out, in0, s1, None, o0)
+        else:
+            f = lambda h: h.tensor_scalar(out, in0, s1, s2, o0, o1)
+        return op("dve", f, r, w, FV + CY * max(64, n * rate), bk(r + w), **kw)
+
+    def tt(out, in0, in1, o, r, w, n, rate=1.0, **kw):
+        return op("dve", lambda h: h.tensor_tensor(out, in0, in1, o), r, w, FV + CY * max(64, n * rate), bk(r + w), **kw)
+
+    def cp(out, in_, r, w, n, rate=1.0, **kw):
+        return op("dve", lambda h: h.tensor_copy(out, in_), r, w, FV + CY * max(64, n * rate), bk(r + w), **kw)
+
+    def ms(ap, v, w, r=()):
+        return op("dve", lambda h: h.memset(ap, v), list(r), w, FV + 0.1)
+
+    def act(out, in_, f, bias, scale, r, w, n, rate=1.0, **kw):
+        if f == AF.Copy:
+            fn = lambda h: h.activation(out, in_, f)
+        else:
+            fn = lambda h: h.activation(out, in_, f, bias=bias, scale=scale)
+        return op("act", fn, r, w, FA + CY * max(64, n * rate), bk(r + w), **kw)
+
+    def mm(items, r, w, grp=None, **kw):
+        def f(h):
+            for it in items:
+                ins = h.matmul(it[0], it[1], it[2], it[3], it[4])
+            return ins
+        if grp is None:
+            grp = (w[0][1], ("one", len(ops)), True)
+        return op("pe", f, r, w, sum(FP + PC * max(64, it[5]) for it in items), bk(w), grp=grp, lat=0.05, **kw)
+
+    def acc(out, terms, n):
+        return [(out, a, b, j == 0, j == len(terms) - 1, n) for j, (a, b) in enumerate(terms)]
+
+    def iota(out, pat, base, cm, w):
+        return op("pool", lambda h: h.iota(out, pat, base, cm), [], w, 0.13 + 2 * CY * int(np.prod([p[1] for p in pat])))
+
+    NW = 128; ND = 8
+
+    def pt(b, s, n=None):
+        return T["pb%d" % b][:, s * 128:s * 128 + (n or NW)], ("P", b, s)
+
+    dma("sp", T.ftab[:], T.fx[:], [], ["ftab"], 7.0)
+    dma("act", T.tin[:], T.t0[:], [], ["tin"], 0.6)
+    dma("act", T.xin[:], T.x0[:], [], ["xin"], 0.6)
+    dma("act", T.din[:, 0:4], T.dw[:], [], ["din"], 0.6)
+    dma("act", T.hin[:, 0:1], T.hw[:], [], ["hin"], 0.6)
+    dma("act", T.thin[:, 0:1], T.th[:], [], ["thin"], 0.6)
+    dma("sp", T.kin[:], T.k0[:], [], ["kin"], 9.0)
+    dma("sp", T.yin[:], T.y0[:], [], ["yin"], 10.0)
+
+    col = lambda j: T.col[:, j:j + 1]
+    iota(T.coli[:, 0:1], [[1, 1]], 0, 1, ["p"])
+    iota(T.ci[:, 0:144], [[1, 144]], 0, 0, ["ci"])
+    iota(T.cj[:, 0:NW], [[0, NW // 4], [16, 4]], 160, 0, ["cj"])
+    iota(T.cj[:, 128:128 + ND], [[256, ND]], 0, 0, ["cj2"])
+    ts(T.coli[:, 1:2], T.coli[:, 0:1], 15, None, A.bitwise_and, None, ["p"], ["pk"], 1)
+    cp(col(0), T.coli[:, 0:1], ["p"], ["c0"], 1)
+    cp(col(1), T.coli[:, 1:2], ["pk"], ["c1"], 1)
+    tt(col(2), col(0), col(1), A.subtract, ["c0", "c1"], ["c2"], 1)
+    ts(col(3), col(2), 15.0, None, A.add, None, ["c2"], ["c3"], 1)
+    ts(col(4), col(1), 37.0, None, A.mult, None, ["c1"], ["c4"], 1)
+    ts(col(5), col(1), 51.0, 8.0, A.add, A.mult, ["c1"], ["c5"], 1)
+    ts(col(6), col(1), 1024.0, None, A.add, None, ["c1"], ["c6"], 1)
+    ts(col(7), col(1), 16.0, None, A.mult, None, ["c1"], ["c7"], 1)
+    cp(col(8), T.hin[:, 0:1], ["hin"], ["c8"], 1)
+    ts(col(9), T.hin[:, 0:1], 2.0, None, A.mult, None, ["hin"], ["c9"], 1)
+    ts(T.col[:, 10:14], T.din[:, 0:4], -16.5, BIG, A.add, A.mult, ["din"], ["c10"], 4)
+    ts(col(14), col(1), 0.0, -1.0, A.is_equal, A.mult, ["c1"], ["c14"], 1)
+    tt(col(15), col(14), T.thin[:, 0:1], A.mult, ["c14", "thin"], ["c15"], 1)
+    ts(col(16), col(1), 1.0, -0.5, A.is_equal, A.mult, ["c1"], ["c16"], 1)
+    tt(col(17), col(15), col(16), A.add, ["c15", "c16"], ["c17"], 1)
+    cp(T.cf[:, 0:144], T.ci[:, 0:144], ["ci"], ["cf"], 144)
+    sw = lambda j, k: T.sw[:, j * 144 + 15 - k:j * 144 + 143 - k]
+    swf = lambda j: T.sw[:, j * 144:j * 144 + 144]
+    ts(swf(0), T.cf[:, 0:144], col(3), None, A.is_equal, None, ["cf", "c3"], ["sw0"], 144)
+    for j, v in ((1, -16.0), (2, BIG), (3, -BIG)):
+        act(swf(j), swf(0), AF.Identity, 0.0, v, ["sw0"], ["sw%d" % j], 144)
+    act(swf(4), swf(0), AF.Identity, 0.0, col(1), ["sw0", "c1"], ["sw4"], 144)
+    act(swf(5), swf(0), AF.Identity, 0.0, col(8), ["sw0", "c8"], ["sw5"], 144)
+    wn = {}
+
+    def wt(name):
+        wn.setdefault(name, len(wn))
+        return T.wt[:, wn[name] * 128:wn[name] * 128 + 128]
+    cm = T.cf[:, 0:128]
+    ts(wt("I"), cm, col(0), None, A.is_equal, None, ["cf", "c0"], ["I"], 128)
+    for name, v in (("nI", -1.0), ("I8", 8.0), ("I512", 512.0), ("IB", 32 * BIG), ("I16", 16.0), ("In2048", -2048.0), ("IBn", -16 * BIG),
+                    ("I16th", 1.0 / 16), ("I32", 32.0), ("In256", -256.0)):
+        act(wt(name), wt("I"), AF.Identity, 0.0, v, ["I"], [name], 128)
+    ts(wt("ge"), cm, col(2), None, A.is_ge, None, ["cf", "c2"], ["ge"], 128)
+    ts(wt("le"), cm, col(3), None, A.is_le, None, ["cf", "c3"], ["lew"], 128)
+    tt(wt("BO"), wt("ge"), wt("le"), A.mult, ["ge", "lew"], ["BO"], 128)
+    act(wt("BO8"), wt("BO"), AF.Identity, 0.0, 8.0, ["BO"], ["BO8"], 128)
+    act(wt("BOn"), wt("BO"), AF.Identity, 0.0, -2 * BIG, ["BO"], ["BOn"], 128)
+    act(wt("H2"), wt("BO"), AF.Identity, 0.0, col(9), ["BO", "c9"], ["H2"], 128)
+    ts(wt("ge"), cm, col(0), 8.0, A.is_ge, A.mult, ["cf", "c0"], ["ge"], 128)
+    tt(wt("tr0"), wt("ge"), wt("le"), A.mult, ["ge", "lew"], ["tr0"], 128)
+    tt(wt("TRI"), wt("tr0"), wt("In256"), A.add, ["tr0", "In256"], ["TRI"], 128)
+    CW = T.wt[0:2, 20 * 128:21 * 128]; CX = T.wt[0:2, 21 * 128:22 * 128]
+    ms(CW, 1.0, ["CW"]); ms(T.wt[0:1, 20 * 128:21 * 128], 327680.0, ["CW"])
+    if KA < 16:
+        ms(CX, 7.5, ["CX"]); ms(T.wt[0:1, 21 * 128:22 * 128], 2304.0, ["CX"])
+    assert len(wn) <= 20
+    ct = lambda j, n=None: T.ct[:, j * 128:j * 128 + (n or NW)]
+    ms(ct(0, 128), 1.0, ["ones"]); ms(ct(1), 272.0, ["c256"]); ms(ct(2), 144.0, ["c128"]); ms(ct(3), -1.0, ["neg"])
+    ts(ct(4), ct(0), col(5), None, A.mult, None, ["ones", "c5"], ["cP"], 64)
+    ts(ct(5), ct(0), col(17), None, A.mult, None, ["ones", "c17"], ["cT"], 64)
+    for t in range(4):
+        ts(ct(6 + t), ct(0), col(10 + t), None, A.mult, None, ["ones", "c10"], ["cD%d" % t], 64)
+    cp(ct(10), T.cj[:, 0:NW], ["cj"], ["turn"], NW)
+    ts(ct(11, ND), T.cj[:, 128:128 + ND], col(7), None, A.add, None, ["cj2", "c7"], ["cI"], ND)
+    cp(T.bco[:], T.ci[:, 0:16], ["ci"], ["bco"], 16)
+    ts(T.cf[:, 144:160], T.cf[:, 0:16], col(1), 2048.0, A.is_gt, A.mult, ["cf", "c1"], ["dmc"], 16)
+    for r in range(1, 16):
+        if r % 2:
+            ts(T.dm[:, r * 128:r * 128 + 128], wt("I"), T.cf[:, 144 + r:145 + r], None, A.mult, None, ["I", "dmc"], ["dm%d" % r], 64)
+        else:
+            act(T.dm[:, r * 128:r * 128 + 128], wt("I"), AF.Identity, 0.0, T.cf[:, 144 + r:145 + r], ["I", "dmc"], ["dm%d" % r], 128)
+    ms(T.st[:, 1024:1040], 0.0, ["st"])
+    allp = lambda b: [("P", b, s) for s in range(4)]
+    for h, s, b1, b2 in ((0, "a", 2, 6), (1, "b", 3, 7)):
+        hs = slice(h * 512, h * 512 + 512)
+        ts(T["pb%d" % b1][:], T.kin[:, hs], 8192.0, -8193.0, A.is_ge, A.mult, ["kin"], allp(b1), 512)
+        tt(T.w1[:, hs], T["pb%d" % b1][:], T.kin[:, hs], A.add, allp(b1) + ["kin"], ["w1" + s], 512)
+        act(T["pb%d" % b2][:], T.yin[:, hs], AF.Identity, 1 - 7.5 / 16, 1.0 / 16, ["yin"], allp(b2), 512)
+        tt(T.st[:, hs], T["pb%d" % b2][:], T.w1[:, hs], A.add, allp(b2) + ["w1" + s], ["st"], 512)
+    ts(T.lz[:, 0:256], T.tin[:], 8192.0, None, A.is_ge, None, ["tin"], [("lz", 0, c) for c in range(C)], 256)
+    ts(T.tnm[:], T.tin[:], 8191, None, A.bitwise_and, None, ["tin"], ["tnm"], 256)
+    cp(T.lu[:, 0:256], T.tnm[:], ["tnm"], [("lu", 0, c) for c in range(C)], 256)
+    cp(T.ln[:, 0:256], T.tnm[:], ["tnm"], [("ln", 0, c) for c in range(C)], 256)
+
+    def mask(es):
+        return sum(1 << e for e in es)
+    stream = [0]
+    G = 4
+    for t in range(4):
+        for c in range(C):
+            NW = NWS[c]; ND = NW // 16
+            w0 = sum(NWS[:c]); sl = slice(w0, w0 + NW); s4 = slice(t * 256 + w0, t * 256 + w0 + NW)
+            stage[0] = t * C + c
+            K = lambda s: (s, c)
+            S = lambda s: T[s][:, sl]
+            x2 = t * 512 + 2 * w0
+            if t == 0:
+                x, fl, kx, kf = T.xin[:, sl], ct(3), "xin", "neg"
+            else:
+                x, fl, kx = T.lx[:, x2:x2 + NW], T.lx[:, x2 + NW:x2 + 2 * NW], ("lx", t, c); kf = kx
+            nf, nu, asl = T.ln[:, s4], T.lu[:, s4], T.lz[:, s4]
+            kn, ku, kz = ("ln", t, c), ("lu", t, c), ("lz", t, c)
+            if t > 0:
+                if SENDU:
+                    cp(nf, nu, [ku], [kn], NW)
+                else:
+                    cp(nu, nf, [kn], [ku], NW)
+            xn, fo, kxn, kfo = T.xs[:, x2:x2 + NW], T.xs[:, x2 + NW:x2 + 2 * NW], ("xn", t, c), ("fo", t, c)
+            big = lambda s, a, b: T[s][:, 16 * w0 + a:16 * w0 + b]
+            first = t == 0 and c == 0
+            wg = NW * (G0 if first else GD) // 16; n0 = t * 256 + w0
+            if wg > 0:
+                cp(big("fg", 0, 16 * wg), T.ftab[:].indirect(T.lu[:, n0:n0 + wg]), ["ftab", ku], [K("fgd")], 16 * wg, GR)
+            if wg < NW:
+                act(big("fg", 16 * wg, 16 * NW), T.ftab[:].indirect(T.lu[:, n0 + wg:n0 + NW]), AF.Copy, 0, 1, ["ftab", ku], [K("fga")], 16 * (NW - wg), GR)
+            kfg = [K("fgd"), K("fga")]
+            wd = NW * (16 if first else DERD) // 16
+            if wd > 0:
+                ts(T.eg[:, w0:w0 + wd, :], big("fg", 0, 16 * wd), 1.0 / 16, 143.53125, A.mult, A.add, kfg, [K("egd")], 16 * wd, 0.5)
+            if wd < NW:
+                act(T.eg[:, w0 + wd:w0 + NW, :], big("fg", 16 * wd, 16 * NW), AF.Identity, 143.53125, 1.0 / 16, kfg, [K("ega")], 16 * (NW - wd))
+            ke = [K("egd"), K("ega")]
+            act(S("za"), x, AF.Relu, 16.0, -16.0, [kx], [K("za")], NW)
+            cn, kcn = pt(4, c); gid = ("cn", t, c)
+            mm([(cn, wt("I8"), fl, True, False, NW), (cn, wt("I512"), asl, False, False, NW)], [kf, kz, ku, "I8", "I512"], [kcn], (4, gid, False))
+            zparts = []
+            fk = lambda k: T.fg[:, 16 * w0 + k:16 * (w0 + NW):16]
+            for k0 in range(0, KA, G):
+                b = stream[0] % 2; stream[0] += 1
+                it = []
+                for j in range(G):
+                    o = T["pb%d" % b][:, j * NW:(j + 1) * NW]
+                    it += acc(o, [(wt("I"), fk(k0 + j)), (wt("nI"), x)], NW)
+                mm(it, kfg + [kx, "I", "nI"], [("P", b, "s")])
+                act(big("zg", k0 * NW, (k0 + G) * NW), T["pb%d" % b][:, 0:G * NW], AF.Identity, 2311.5, 1.0, [("P", b, "s")], [("zg", c, k0)], G * NW)
+                zparts.append((k0, [(k0 + j, big("zg", (k0 + j) * NW, (k0 + j + 1) * NW)) for j in range(G)]))
+            if KA < 16:
+                b = stream[0] % 2; stream[0] += 1
+                it = []
+                it += acc(T["pb%d" % b][:, 0:NW], [(wt("nI"), x), (CX, T.ct[0:2, 0:NW])], NW)
+                mm(it, [kx, "nI", "CX", "ones"], [("P", b, "s")])
+                for k0 in range(KA, 16):
+                    tt(big("zg", k0 * NW, (k0 + 1) * NW), fk(k0), T["pb%d" % b][:, 0:NW], A.add, kfg + [("P", b, "s")], [("zg", c, k0)], NW)
+                    zparts.append((k0, [(k0, big("zg", k0 * NW, (k0 + 1) * NW))]))
+            for k0 in range(0, 16, 4):
+                mm([(cn, sw(1, k), T.eg[:, sl, k], False, False, NW) for k in range(k0, k0 + 4)], ke + ["sw1"], [kcn], (4, gid, False))
+            for j, (k0, parts) in enumerate(zparts):
+                e = j == len(zparts) - 1
+                mm([(cn, sw(0, k), ap, False, e and k == parts[-1][0], NW) for k, ap in parts], [("zg", c, k0), "sw0"], [kcn], (4, gid, e))
+            act(S("cand"), cn, AF.Sign, 108.0, -1.0, [kcn], [K("cand")], NW)
+            mp, kmp = pt(5, 0); pr, kpr = pt(5, 1); ix, kix = pt(5, 2, ND)
+            mm(acc(mp, [(wt("BO8"), S("cand")), (wt("I"), ct(1))], NW) + acc(pr, [(wt("TRI"), S("cand")), (wt("I"), ct(4))], NW),
+               [K("cand"), "BO8", "TRI", "I", "c256", "cP"], [kmp, kpr])
+            tt(S("pos"), mp, ct(10), A.min, [kmp, "turn"], [K("pos")], NW)
+            tt(S("go"), pr, S("pos"), A.is_equal, [kpr, K("pos")], [K("go")], NW)
+            dl, kdl = pt(5, 3)
+            mm(acc(dl, [(wt("TRI"), S("cand")), (wt("I"), ct(4)), (wt("nI"), S("pos"))], NW), [K("cand"), K("pos"), "TRI", "I", "nI", "cP"], [kdl])
+            act(S("fall"), dl, AF.Sign, 8.0, 1.0, [kdl], [K("fall")], NW)
+            mm(acc(ix, [(wt("I"), ct(11, ND))] + [(sw(4, r), T.go[:, w0 + r:w0 + NW:16]) for r in range(16)], ND), [K("go"), "sw4", "I", "cI"], [kix])
+            iu = T.iu[:, w0 // 16:w0 // 16 + ND]
+            cp(iu, ix, [kix], [K("iu")], ND)
+            if EGA:
+                act(S("e0"), big("fg", 0, 16 * NW).indirect(iu), AF.Identity, 143.53125, 1.0 / 16, kfg + [K("iu")], [K("e0")], NW, GR)
+            else:
+                ts(S("e0"), big("fg", 0, 16 * NW).indirect(iu), 1.0 / 16, 143.53125, A.mult, A.add, kfg + [K("iu")], [K("e0")], NW, GR)
+            tt(S("ee"), S("e0"), S("pos"), A.min, [K("e0"), K("pos")], [K("ee")], NW, 2)
+            d0, kd0 = pt(5, 0); ds, kds = pt(5, 2); au, kau = pt(5, 3)
+            mm(acc(au, [(wt("I"), x), (wt("I"), S("za"))], NW), [kx, K("za"), "I"], [kau])
+            mm(acc(ds, [(wt("I"), x), (wt("I"), S("za")), (wt("nI"), S("ee"))], NW) + acc(d0, [(wt("I"), x), (wt("nI"), S("ee"))], NW),
+               [kx, K("za"), K("ee"), "I", "nI"], [kds, kd0])
+            act(S("le"), ds, AF.Relu, 32.0 * 145, 32.0, [kds], [K("le")], NW)
+            tt(S("qq"), au, S("le"), A.min, [kau, K("le")], [K("qq")], NW)
+            act(xn, d0, AF.Abs, 144.0, 1.0, [kd0], [kxn], NW)
+            act(S("zc"), S("ee"), AF.Relu, 2320.0, -16.0, [K("ee")], [K("zc")], NW)
+            R = REP * NW
+            if 2 * R <= 512:
+                kap, th, kkap, kth = (lambda a, b, s: T.pb2[:, a:b:s]), (lambda a, b, s: T.pb2[:, R + a:R + b:s]), ("P", 2, 0), ("P", 2, 1)
+            else:
+                kap, th, kkap, kth = (lambda a, b, s: T.pb2[:, a:b:s]), (lambda a, b, s: T.pb2[:, a:b:s]), ("P", 2, 0), ("P", 2, 0)
+            wq, kwq = pt(3, c); gid = ("w", t, c)
+            mm([(wq, wt("I"), ct(6 + t), True, False, NW), (wq, wt("IB"), asl, False, False, NW), (wq, wt("IBn"), S("fall"), False, False, NW)],
+               [kz, K("fall"), K("le"), "I", "IB", "IBn", "cD%d" % t], [kwq], (3, gid, False))
+            for nm_, src, ksrc, o, wj, terms in (("tb", kap, kkap, A.is_equal, 2, [(S("ee"), K("ee")), (S("le"), K("le"))]),
+                                                 ("ta", th, kth, A.is_gt, 3, [(ct(2), "c128"), (S("zc"), K("zc")), (S("qq"), K("qq"))])):
+                it = []
+                for j in range(REP):
+                    it += acc(src(j, R, REP), [(wt("I"), a) for a, _ in terms], NW)
+                mm(it, [k for _, k in terms] + ["I"], [ksrc])
+                for k0 in range(0, 16, REP):
+                    tt(big(nm_, k0 * NW, k0 * NW + R), T.eg[:, sl, k0:k0 + REP], src(0, R, 1), o, ke + [ksrc], [(nm_, c, k0)], R)
+                for k0 in range(0, 16, 4):
+                    e = nm_ == "ta" and k0 == 12
+                    it = []
+                    for k in range(k0, k0 + 4):
+                        kb_ = k - k % REP
+                        it.append((wq, sw(wj, k), T[nm_][:, 16 * w0 + kb_ * NW + k % REP:16 * w0 + kb_ * NW + R:REP], False, e and k == 15, NW))
+                    mm(it, [(nm_, c, k) for k in range(k0 - k0 % REP, k0 + 4, REP)] + ["sw%d" % wj], [kwq], (3, gid, e))
+            u0, ku0 = pt(6, 0); v2, kv2 = pt(6, 1); dy, kdy = pt(6, 2); sn, ksn = pt(6, 3); ud = pt(6, 3, ND)[0]
+            mm(acc(ud, [(sw(5, r), T.xs[:, x2 + r:x2 + NW:16]) for r in range(16)], ND), [kxn, "sw5"], [ksn])
+            mm(acc(u0, [(wt("H2"), xn)], NW), [kxn, "H2"], [ku0])
+            dsl = slice(w0 // 16, w0 // 16 + ND)
+            ts(T.cd0[:, dsl], ud, 241.0, None, A.mult, None, [ksn], [K("cd0")], ND)
+            ts(T.cd[:, dsl], T.cd0[:, dsl], 6, 1023, A.logical_shift_right, A.bitwise_and, [K("cd0")], [K("cd")], ND)
+            cu = T.cu[:, dsl]
+            cp(cu, T.cd[:, dsl], [K("cd")], [K("cu")], ND)
+            act(S("hi"), u0, AF.Identity, 159.5 + 1.0 / 2048, 1.0 / 2048, [ku0], [K("hi")], NW)
+            ts(S("cb0"), u0, 120.5, None, A.mult, None, [ku0], [K("cb0")], NW)
+            mm(acc(v2, [(wt("H2"), xn), (CW, T.ct[0:2, 0:NW]), (wt("In2048"), S("hi"))], NW), [kxn, K("hi"), "H2", "CW", "ones", "In2048"], [kv2])
+            sa, ksa = pt(7, 0); sb, ksb = pt(7, 1); ka, kka = pt(7, 2); sd, ksd = pt(7, 3)
+            act(sa, nf, AF.Identity, col(4), 1.0, [kn, "c4"], [ksa], NW)
+            tt(S("pp"), v2, nf, A.mult, [kv2, kn], [K("pp")], NW)
+            ts(S("q5"), S("pp"), 5, None, A.logical_shift_right, None, [K("pp")], [K("q5")], NW)
+            tt(S("ss"), sa, S("q5"), A.add, [ksa, K("q5")], [K("ss")], NW)
+            ts(S("nn"), S("ss"), 8191, None, A.bitwise_and, None, [K("ss")], [K("nn")], NW)
+            ts(S("kc"), T.st[:].indirect(cu), MAGIC, MAGIC + 1, A.add, A.subtract, ["st", K("cu")], [K("kc")], NW, GR)
+            tt(S("yq"), T.st[:].indirect(cu), S("kc"), A.subtract, ["st", K("cu"), K("kc")], [K("yq")], NW, GR)
+            mm(acc(dy, [(wt("nI"), xn), (wt("I16"), S("yq"))], NW), [kxn, K("yq"), "nI", "I16"], [kdy])
+            act(S("ad"), dy, AF.Abs, -8.5, 1.0, [kdy], [K("ad")], NW)
+            mm(acc(sn, [(wt("BOn"), ct(5)), (wt("BOn"), S("ad"))], NW), [K("ad"), "BOn", "cT"], [ksn])
+            act(fo, sn, AF.Sign, 0.0, 1.0, [ksn], [kfo], NW)
+            tt(S("zz"), sn, S("kc"), A.min, [ksn, K("kc")], [K("zz")], NW)
+            act(sb, S("zz"), AF.Relu, 0.0, -BIG, [K("zz")], [ksb], NW)
+            if t < 3:
+                lx = T.lx[:, x2 + 512:x2 + 512 + 2 * NW]; sx = T.xs[:, x2:x2 + 2 * NW]; sa_ = "a0_%d_%d" % (t + 1, c)
+                i = op("pool", lambda h, lx=lx, sx=sx, s=sa_: h.remote_dma(lx, sx, T.sem[s], T.sem.sent, dst[1], dst[0], mask(eng)),
+                       [kxn, kfo], [], 0.3, fin=False)
+                sent[0] += len(eng)
+                op(None, None, [], [("lx", t + 1, c)], 0.0, sem=(sa_, len(eng)), lat=COMM, soft=[i])
+            tt(ka, wq, nf, A.min, [kwq, kn], [kka], NW)
+            act(sa, wq, AF.Identity, 0.0, -1.0, [kwq], [ksa], NW)
+            tt(S("t1"), sa, S("nn"), A.min, [ksa, K("nn")], [K("t1")], NW)
+            tt(S("nm1"), ka, S("t1"), A.max, [kka, K("t1")], [K("nm1")], NW)
+            tt(sd, sb, S("nm1"), A.min, [ksb, K("nm1")], [ksd], NW)
+            no, zo, uo = T.ns[:, s4], T.zs[:, s4], T.us[:, s4]
+            kno, kzo, kuo = ("ns", t, c), ("zs", t, c), ("us", t, c)
+            tt(no, sd, S("zz"), A.max, [ksd, K("zz")], [kno], NW)
+            tt(zo, ka, no, A.is_equal, [kka, kno], [kzo], NW)
+            if t < 3:
+                sb_ = "a1_%d_%d" % (t + 1, c); n4 = (t + 1) * 256 + w0; m4 = t * 256 + w0; h2 = NW // 2
+                if SENDU:
+                    cp(uo, no, [kno], [kuo], NW)
+                    tr = [(T.lu[:, n4:n4 + NW], uo, eng[:4]), (T.lz[:, n4:n4 + NW], zo, eng[4:])]
+                    rr, ww = [kuo, kzo], [("lu", t + 1, c), ("lz", t + 1, c)]
+                else:
+                    tr = [(T.ln[:, n4:n4 + h2], T.ns[:, m4:m4 + h2], eng[:2]), (T.ln[:, n4 + h2:n4 + NW], T.ns[:, m4 + h2:m4 + NW], eng[2:4]),
+                          (T.lz[:, n4:n4 + NW], zo, eng[4:])]
+                    rr, ww = [kno, kzo], [("ln", t + 1, c), ("lz", t + 1, c)]
+                i = op("pool", lambda h, tr=tr, s=sb_: h.remote_dma_fused(
+                    [RemoteDMATransfer(dst_ids=[DstId(rid=dst[0], pnc=dst[1])], dma_engine_mask=mask(e), remote_sem=T.sem[s], src=a, dst=b)
+                     for b, a, e in tr], local_sem=T.sem.sent), rr, [], 0.3, fin=False)
+                sent[0] += len(eng)
+                op(None, None, [], ww, 0.0, sem=(sb_, len(eng)), lat=COMM, soft=[i])
+            else:
+                act(sa, zo, AF.Identity, 0.0, 8192.0, [kzo], [ksa], NW)
+                tt(S("yts"), sa, no, A.add, [ksa, kno], [K("yts")], NW)
+                dma("sp", T.yt[:, sl], S("yts"), [K("yts")], [], 0.3)
+                dma("sp", T.yx[:, sl], xn, [kxn], [], 0.3)
+            stage[0] = (t + 1) * C
+            act(S("kb"), ka, AF.Relu, 1.0, 1.0, [kka], [K("kb")], NW)
+            act(sd, S("zz"), AF.Abs, 1.0, 1.0, [K("zz")], [ksd], NW)
+            tt(sb, sd, S("kb"), A.min, [ksd, K("kb")], [ksb], NW)
+            tt(S("kk"), sb, zo, A.mult, [ksb, kzo], [K("kk")], NW)
+            mm(acc(dy, [(wt("nI"), xn), (wt("I16"), S("yq")), (wt("I32"), fo)], NW), [kxn, K("yq"), kfo, "nI", "I16", "I32"], [kdy])
+            act(S("hd"), dy, AF.Relu, -8.5, 1.0, [kdy], [K("hd")], NW)
+            mm(acc(u0, [(wt("I16th"), xn), (wt("nI"), fo), (wt("I16th"), S("hd"))], NW), [kxn, kfo, K("hd"), "I16th", "nI"], [ku0])
+            act(S("y16"), u0, AF.Identity, -23.5 / 16, 1.0, [ku0], [K("y16")], NW)
+        for cs in ([[c] for c in range(C)] if t >= SPLIT else [list(range(C))]):
+            al = lambda s: [(s, c) for c in cs]
+            a, n = sum(NWS[:cs[0]]) // 16, sum(NWS[c] for c in cs) // 16; ws = slice(16 * a, 16 * (a + n))
+            if t >= SPLIT:
+                stage[0] = t * C + cs[0] + 1
+            ts(T.cb[:, ws], T.cb0[:, ws], 6, 1023, A.logical_shift_right, A.bitwise_and, al("cb0"), al("cb"), 16 * n)
+            tt(T.eq[:, ws], T.cd[:, 0:a + n].indirect(T.bco[:, a:a + n]), T.cb[:, ws], A.is_equal,
+               [("cd", c) for c in range(cs[-1] + 1)] + ["bco"] + al("cb"), al("eq"), 16 * n, GR)
+            lo, klo = T.pb3[:, 384 + a:384 + a + n], ("P", 3, "lo", cs[0])
+            mm(acc(lo, [(T.dm[:, r * 128:r * 128 + 128], T.eq[:, 16 * a + r:16 * (a + n):16]) for r in range(1, 16)], n),
+               al("eq") + ["dm%d" % r for r in range(1, 16)] + [("P", 3, 3)], [klo])
+            tt(T.of0[:, a:a + n], lo, T.cd[:, a:a + n], A.max, [klo] + al("cd"), al("of0"), n)
+            ts(T.off[:, 2 * a:2 * (a + n):2], T.of0[:, a:a + n], col(6), None, A.min, None, al("of0") + ["c6"], al("off"), n)
+        for b in range(16):
+            c = max(j for j in range(C) if sum(NWS[:j]) <= 16 * b)
+            tt(T.st[:].indirect(T.off[:, 2 * b:2 * b + 1]), T.kk[:, 16 * b:16 * b + 16], T.y16[:, 16 * b:16 * b + 16], A.add,
+               [("off", c), ("kk", c), ("y16", c)], ["st"], 16, SC)
+    for h, s in ((0, "a"), (1, "b")):
+        hs = slice(h * 512, h * 512 + 512); pb = T["pb%d" % h][:]; kp = ("P", h, "s")
+        ts(pb, T.st[:, hs], MAGIC, MAGIC + 1, A.add, A.subtract, ["st"], [kp], 512)
+        tt(T.w2[:, hs], pb, T.st[:, hs], A.subtract, [kp, "st"], ["w2" + s], 512)
+        act(T.w1[:, hs], pb, AF.Identity, 0.0, -8192.0, [kp], ["w1" + s], 512)
+        act(T.yo[:, hs], T.w2[:, hs], AF.Identity, -8.5, -16.0, ["w2" + s], ["yo" + s], 512)
+        tt(T.w1[:, hs], pb, T.w1[:, hs], A.max, [kp, "w1" + s], ["w1" + s], 512)
+        dma("sp", T.yk[:, hs], T.w1[:, hs], ["w1" + s], [], 0.8)
+        dma("act", T.yy[:, hs], T.yo[:, hs], ["yo" + s], [], 0.4)
+    return ops, sent[0]
+
+
+def rank_program(g, core, T, topo):
+    rank = T.rank_of(core)
+    if rank is None:
+        return
+    nxt = T.cores[(rank + 1) % len(T.cores)]
+    assert topo.may_write(core, nxt)
+    ops, sent = build(T, topo.addr(nxt), topo.engines(core, nxt)[:8])
+    order, _ = plan(ops)
+    for s, v in emit(g, T, ops, order):
+        g.wait_ge(T.sem[s], v)
+    g.wait_ge(T.sem.sent, sent)

@@ -7,44 +7,59 @@ C = len(NWS)
 REP = 2
 KA = 12
 DERD = 8
-SENDU = True
-BIG = 16384.0
-MAGIC = 12582912.0
-CY, PC, FV, FA, FP, LAT, LSELF, GR, SC = 1.0e-3, 0.5e-3, 0.06, 0.08, 0.01, 0.15, 0.08, 1.56, 3.8
-COMM, WIN, STG = 3.5, 0.15, 3.0
-EGA = False
-SPLIT = 3
-SEED, NOISE = 0, 0.0
-RANKS = {"dve('P', 7, 3)": 2, "pe('P', 2, 0)": 1, "dve('ta', 0, 8)": 20, "dve('ta', 1, 14)": 20, "act('ega', 1)": -4, "act('fall', 0)": -1, "dve('iu', 1)": 8, "act('P', 7, 0)": 4, "act('zc', 0)": 4, "act('ad', 1)": 8, "dve('tb', 1, 6)": 8, "dve('zg', 0, 15)": -2, "pe('P', 4, 0)": 4, "dve('pp', 1)": 1, "dve('yts', 0)": -4, "pe('P', 1, 's')": 4, "dve('off', 1)": 1, "dve('ss', 1)": -4, "dve('ta', 1, 2)": 8, "dve('nm1', 0)": -2, "act('P', 7, 1)": 4, "pe('P', 0, 's')": 2, "act('zg', 1, 0)": -8, "dve('of0', 0)": -1, "dve('ta', 1, 0)": 1, "dve('nn', 1)": -4, "dve('of0', 1)": 20, "dve('cb0', 1)": -2, "act('za', 1)": -2, "dve('yts', 1)": -8, "act('zg', 0, 4)": 8, "act('zg', 0, 0)": 8, "dve('zz', 0)": 2}
 GD = 0
 G0 = 8
+GS = 4
+ES = 2
+GSD, ESD = 1, 1
+TA = 16
+MIX = True
+TG, TW, WQB = True, True, None
+ROUNDS = 6
+GB, TB = (0, 1), (0, 1)
+OFF, STP, ENT = 3.0, 6.0, 6.0
+EGA = False
+FALLA = False
+SSP = True
+VP = True
+SEA = False
+SPLIT = 3
+INORDER = False
+CY, PC, FV, FA, FP, LAT, LSELF, GR, SC = 0.83e-3, 0.42e-3, 0.05, 0.065, 0.005, 0.12, 0.06, 1.56, 3.8
+COMM, WIN, STG, TAB = 3.0, 0.15, 3.0, 6.0
+TA, KA, DERD, GD, SSP, SEA = 8, 0, 8, 0, False, True
+U = 80.0 * 2 ** 18
+Y0 = 192.0
+HB = 2033
 
-BF, F32, I32, U16 = "bfloat16", "float32", "int32", "uint16"
+BF, F32, I32, U16, F16 = "bfloat16", "float32", "int32", "uint16", "float16"
 SCRATCH = {
-    "ftab": ("sbuf", [128, 8192], BF), "fg": ("sbuf", [128, 4096], BF), "eg": ("sbuf", [128, 256, 16], BF),
+    "ftab": ("sbuf", [128, 8192], BF), "fg": ("sbuf", [128, 4096 + 16 * C], BF), "eg": ("sbuf", [128, 256, 16], BF),
     "zg": ("sbuf", [128, 4096], BF), "ta": ("sbuf", [128, 4096], BF), "tb": ("sbuf", [128, 4096], BF),
     "st": ("sbuf", [128, 1040], F32), "kin": ("sbuf", [128, 1024], I32), "yin": ("sbuf", [128, 1024], BF),
-    "w1": ("sbuf", [128, 1024], F32), "w2": ("sbuf", [128, 1024], F32), "yo": ("sbuf", [128, 1024], BF),
+    "w1": ("sbuf", [128, 1024], F32), "wi": ("sbuf", [128, 1024], I32), "wj": ("sbuf", [128, 1024], I32),
+    "yo": ("sbuf", [128, 1024], BF), "ys": ("sbuf", [128, 1024], BF),
     "tin": ("sbuf", [128, 256], I32), "tnm": ("sbuf", [128, 256], I32), "xin": ("sbuf", [128, 256], BF),
     "din": ("sbuf", [128, 8], I32), "hin": ("sbuf", [128, 8], I32), "thin": ("sbuf", [128, 8], I32),
-    "xs": ("sbuf", [128, 4 * 512], BF), "ns": ("sbuf", [128, 4 * 256], F32), "us": ("sbuf", [128, 4 * 256], U16), "zs": ("sbuf", [128, 4 * 256], BF),
-    "lx": ("sbuf", [128, 4 * 512], BF), "ln": ("sbuf", [128, 4 * 256], F32), "lu": ("sbuf", [128, 4 * 256], U16), "lz": ("sbuf", [128, 4 * 256], BF),
-    "ci": ("sbuf", [128, 256], I32), "cj": ("sbuf", [128, 256], I32), "cf": ("sbuf", [128, 160], F32), "col": ("sbuf", [128, 32], F32),
-    "coli": ("sbuf", [128, 8], I32), "dm": ("sbuf", [128, 16 * 128], BF), "sw": ("sbuf", [128, 6 * 144], BF), "wt": ("sbuf", [128, 22 * 128], BF),
-    "ct": ("sbuf", [128, 12 * 128], BF), "bco": ("sbuf", [128, 16], U16), "iu": ("sbuf", [128, 32], U16), "cu": ("sbuf", [128, 32], U16),
-    "cd": ("sbuf", [128, 16], I32), "cd0": ("sbuf", [128, 16], I32), "of0": ("sbuf", [128, 16], F32), "off": ("sbuf", [128, 32], U16),
-    "yts": ("sbuf", [128, 256], F32),
+    "xs": ("sbuf", [128, 4 * 512], BF), "us": ("sbuf", [128, 4 * 256], U16), "zs": ("sbuf", [128, 4 * 256], BF),
+    "lx": ("sbuf", [128, 4 * 512], BF), "lu": ("sbuf", [128, 4 * 256], U16), "lz": ("sbuf", [128, 4 * 256], BF),
+    "ci": ("sbuf", [128, 256], I32), "cj": ("sbuf", [128, 512], I32), "cf": ("sbuf", [128, 160], F32), "col": ("sbuf", [128, 48], F32),
+    "coli": ("sbuf", [128, 8], I32), "dm": ("sbuf", [128, 17 * 128], F16), "sw": ("sbuf", [128, 6 * 144], BF), "swi": ("sbuf", [128, 144], F16),
+    "wt": ("sbuf", [128, 30 * 128], BF), "tr": ("sbuf", [128, 128 * C], BF), "wf": ("sbuf", [128, 4 * 128], F32),
+    "ct": ("sbuf", [128, 12 * 128], BF), "iu": ("sbuf", [128, 32], U16), "cu": ("sbuf", [128, 32], U16),
+    "cd": ("sbuf", [128, 16], I32), "cd0": ("sbuf", [128, 16], I32), "cdh": ("sbuf", [128, 16], F16), "off": ("sbuf", [128, 32], U16),
+    "go": ("sbuf", [128, 256], F16),
 }
-for _n in ("cand", "pos", "go", "fall", "ee", "e0", "za", "zc", "le", "qq", "hi", "yq", "ad", "hd", "eq"):
+for _n in ("cand", "r2", "fall", "ee", "za", "zc", "le", "qq", "hi", "yq", "ad", "hd", "eq", "se"):
     SCRATCH[_n] = ("sbuf", [128, 256], BF)
-for _n in ("kc", "t1", "nm1", "zz", "kb", "kk", "y16"):
+for _n in ("nf", "pp", "wg", "aa", "m0", "sg", "vv", "yn", "yts"):
     SCRATCH[_n] = ("sbuf", [128, 256], F32)
-for _n in ("pp", "q5", "ss", "nn", "cb0", "cb"):
+for _n in ("mi", "fi"):
     SCRATCH[_n] = ("sbuf", [128, 256], I32)
 for _b in range(8):
     SCRATCH["pb%d" % _b] = ("psum", [128, 512], F32)
 SEMAPHORES = ["pe", "dve", "act", "pool", "sent"] + ["d%d" % i for i in range(24)] + \
-    ["a%d_%d_%d" % (k, t, c) for k in range(2) for t in range(1, 4) for c in range(C)]
+    ["a%d_%d_%d" % (k, t, c) for k in range(3) for t in range(1, 4) for c in range(C)]
 
 
 def plan(ops):
@@ -57,10 +72,6 @@ def plan(ops):
     for i in range(n - 1, -1, -1):
         o = ops[i]
         pr[i] = o["dur"] + o["lat"] + max([pr[j] + LAT for j in succ[i]] + [0.0]) + o["bias"]
-    z = SEED * 7919 + 1
-    for i in range(n):
-        z = (z * 1103515245 + 12345) % 2147483648
-        pr[i] += NOISE * (z / 2147483648.0) + RANKS.get(ops[i]["tag"], 0)
     left = [len(o["deps"] | o["soft"]) for o in ops]
     ready = [i for i in range(n) if left[i] == 0]
     fin = [0.0] * n; free = {}; bank = {}; lock = {}; order = []
@@ -72,7 +83,7 @@ def plan(ops):
                 continue
             t = free.get(o["eng"], 0.0)
             for d in o["deps"] | o["soft"]:
-                t = max(t, fin[d] + (0.0 if d in o["chain"] else LSELF if ops[d]["eng"] == o["eng"] else LAT))
+                t = max(t, fin[d] + (-ops[d]["lat"] if d in o["chain"] else LSELF if ops[d]["eng"] == o["eng"] else LAT))
             for b in o["banks"]:
                 for e, j in bank.get(b, {}).items():
                     if e != o["eng"]:
@@ -80,7 +91,7 @@ def plan(ops):
             cands.append((t, i))
         t0, i0 = min(cands)
         e0 = ops[i0]["eng"]
-        t, i = max([(tt, ii) for tt, ii in cands if ops[ii]["eng"] == e0 and tt <= t0 + WIN], key=lambda z: pr[z[1]] - STG * ops[z[1]]["stage"])
+        t, i = max([(tt, ii) for tt, ii in cands if ops[ii]["eng"] == e0 and tt <= t0 + WIN], key=lambda z: pr[z[1]] - ops[z[1]]["stage"])
         o = ops[i]
         for b in o["banks"]:
             for e, j in bank.get(b, {}).items():
@@ -103,6 +114,71 @@ def plan(ops):
                 ready.append(j)
     assert len(order) == n
     return order, max(fin)
+
+
+def place(ops, before, key):
+    n = len(ops); start = [0.0] * n; busy = {}; left = [len(b) for b in before]; after = [[] for _ in range(n)]
+    for i, b in enumerate(before):
+        for d, _ in b:
+            after[d].append(i)
+    ready = [i for i in range(n) if left[i] == 0]
+    while ready:
+        i = min(ready, key=lambda j: key[j]); ready.remove(i)
+        o = ops[i]; e = o["eng"]; dur = o["dur"]
+        t = max([start[d] + ops[d]["dur"] + w for d, w in before[i]] + [0.0])
+        if e is not None:
+            lines = [(busy.setdefault(e, []), 0.0)] + [(v, LAT + 0.05) for b in o["banks"] for f, v in busy.setdefault(b, {}).items() if f != e]
+            moved = True
+            while moved:
+                moved = False
+                for v, gap in lines:
+                    lo, hi = 0, len(v)
+                    while lo < hi:
+                        m = (lo + hi) // 2
+                        if v[m][1] + gap <= t + 1e-9:
+                            lo = m + 1
+                        else:
+                            hi = m
+                    while lo < len(v) and v[lo][0] - gap < t + dur - 1e-9:
+                        t = v[lo][1] + gap; lo += 1; moved = True
+            for v in [busy[e]] + [busy[b].setdefault(e, []) for b in o["banks"]]:
+                v.append((t, t + dur)); v.sort()
+        start[i] = t
+        for j in after[i]:
+            left[j] -= 1
+            if left[j] == 0:
+                ready.append(j)
+    return start
+
+
+def plan(ops):
+    n = len(ops); fw = [[] for _ in range(n)]; bw = [[] for _ in range(n)]
+    for i, o in enumerate(ops):
+        for d in o["deps"] | o["soft"]:
+            w = 0.0 if d in o["chain"] else ops[d]["lat"] + (LSELF if ops[d]["eng"] == o["eng"] else LAT)
+            fw[i].append((d, w)); bw[d].append((i, w))
+    pr = [0.0] * n
+    for i in range(n - 1, -1, -1):
+        pr[i] = ops[i]["dur"] + max([pr[j] + w for j, w in bw[i]] + [ops[i]["lat"]])
+    key = [ops[i]["stage"] - pr[i] for i in range(n)]
+    end = lambda s: max(s[i] + ops[i]["dur"] + ops[i]["lat"] for i in range(n))
+    tail = dict(eng=None, dur=0.0, banks=())
+    best = None
+    for _ in range(ROUNDS):
+        s = place(ops, fw, key)
+        if best is None or end(s) < end(best):
+            best = s
+        r = place(ops + [tail], [b or [(n, ops[i]["lat"])] for i, b in enumerate(bw)] + [[]], [-s[i] - ops[i]["dur"] for i in range(n)] + [0.0])
+        key = [-r[i] - ops[i]["dur"] for i in range(n)]
+    order = sorted(range(n), key=lambda i: (best[i], i)); bank = {}
+    for i in order:
+        o = ops[i]; o["t"] = best[i]
+        for b in o["banks"]:
+            for e, j in bank.get(b, {}).items():
+                if e != o["eng"]:
+                    o["deps"].add(j)
+            bank.setdefault(b, {})[o["eng"]] = i
+    return order, end(best)
 
 
 def emit(g, T, ops, order):
@@ -159,23 +235,26 @@ def emit(g, T, ops, order):
 
 
 def build(T, dst, eng):
-    ops = []; lw = {}; rd = {}; nd = [0]; sent = [0]; stage = [0]
+    ops = []; lw = {}; rd = {}; nd = [0]; sent = [0]; stage = [0]; sums_in = {}
 
     def op(e, fn, r, w, dur, banks=(), grp=None, sem=None, lat=0.0, soft=(), bias=0.0, fin=True):
-        i = len(ops); deps = set(); chain = set()
+        i = len(ops); raw = set(); other = set(); chain = set()
         for k in r:
             if k in lw:
-                deps.add(lw[k])
+                raw.add(lw[k])
         for k in w:
             if k in lw:
-                deps.add(lw[k])
+                other.add(lw[k])
                 if e == "pe" and ops[lw[k]]["eng"] == "pe":
                     chain.add(lw[k])
-            deps |= set(rd.get(k, []))
+            other |= set(rd.get(k, []))
+        if INORDER and e in ("dve", "act") and sem is None:
+            chain |= set(d for d in other - raw - set(lw.get(k) for k in w) if ops[d]["eng"] == e and ops[d]["sem"] is None)
         for k in r:
             rd.setdefault(k, []).append(i)
         for k in w:
             lw[k] = i; rd[k] = []
+        deps = raw | other
         deps.discard(i)
         ops.append(dict(eng=e, fn=fn, deps=deps, chain=chain, soft=set(soft), dur=dur, banks=tuple(banks), grp=grp, sem=sem,
                         lat=lat, bias=bias, fin=fin, stage=stage[0], tag=str(e) + str(w[0] if w else r[0])))
@@ -184,7 +263,7 @@ def build(T, dst, eng):
     def bk(keys):
         return sorted(set(k[1] for k in keys if isinstance(k, tuple) and k[0] == "P"))
 
-    def dma(q, out, in_, r, w, us, slow=False):
+    def dma(q, out, in_, r, w, us):
         s = "d%d" % nd[0]; nd[0] += 1
         return op(q, lambda h: h.dma_start(out, in_), r, w, 0.05, sem=(s, 16), lat=2.0 + us)
 
@@ -202,7 +281,7 @@ def build(T, dst, eng):
         return op("dve", lambda h: h.tensor_copy(out, in_), r, w, FV + CY * max(64, n * rate), bk(r + w), **kw)
 
     def ms(ap, v, w, r=()):
-        return op("dve", lambda h: h.memset(ap, v), list(r), w, FV + 0.1)
+        return op("dve", lambda h: h.memset(ap, v), list(r), w, FV + 0.06)
 
     def act(out, in_, f, bias, scale, r, w, n, rate=1.0, **kw):
         if f == AF.Copy:
@@ -216,12 +295,20 @@ def build(T, dst, eng):
             for it in items:
                 ins = h.matmul(it[0], it[1], it[2], it[3], it[4])
             return ins
+        i = op("pe", f, r, w, sum(FP + PC * max(64, it[5]) for it in items), bk(w), lat=0.05, **kw)
+        b = w[0][1]; z = sums_in.setdefault(b, dict(open=None, shut=[], ones=[])); first = []
         if grp is None:
-            grp = (w[0][1], ("one", len(ops)), True)
-        return op("pe", f, r, w, sum(FP + PC * max(64, it[5]) for it in items), bk(w), grp=grp, lat=0.05, **kw)
+            assert z["open"] is None
+            first = z["shut"]; z["ones"].append(i)
+        elif z["open"] is None:
+            first = z["shut"] + z["ones"]; z["open"] = grp[1]; z["ones"] = []
+        if grp is not None and grp[2]:
+            z["open"] = None; z["shut"] = [i]
+        ops[i]["chain"] |= set(first) - ops[i]["deps"]; ops[i]["deps"] |= set(first)
+        return i
 
     def acc(out, terms, n):
-        return [(out, a, b, j == 0, j == len(terms) - 1, n) for j, (a, b) in enumerate(terms)]
+        return [(out, z[0], z[1], j == 0, j == len(terms) - 1, max(64, n) * (4 if len(z) > 2 else 1)) for j, z in enumerate(terms)]
 
     def iota(out, pat, base, cm, w):
         return op("pool", lambda h: h.iota(out, pat, base, cm), [], w, 0.13 + 2 * CY * int(np.prod([p[1] for p in pat])))
@@ -230,106 +317,135 @@ def build(T, dst, eng):
 
     def pt(b, s, n=None):
         return T["pb%d" % b][:, s * 128:s * 128 + (n or NW)], ("P", b, s)
+    allp = lambda b: [("P", b, s) for s in range(4)]
 
-    dma("sp", T.ftab[:], T.fx[:], [], ["ftab"], 7.0)
+    dma("sp", T.ftab[:], T.fx[:], [], ["ftab"], TAB)
     dma("act", T.tin[:], T.t0[:], [], ["tin"], 0.6)
     dma("act", T.xin[:], T.x0[:], [], ["xin"], 0.6)
     dma("act", T.din[:, 0:4], T.dw[:], [], ["din"], 0.6)
     dma("act", T.hin[:, 0:1], T.hw[:], [], ["hin"], 0.6)
     dma("act", T.thin[:, 0:1], T.th[:], [], ["thin"], 0.6)
-    dma("sp", T.kin[:], T.k0[:], [], ["kin"], 9.0)
-    dma("sp", T.yin[:], T.y0[:], [], ["yin"], 10.0)
+    dma("sp", T.kin[:], T.k0[:], [], ["kin"], TAB + 1.5)
+    dma("sp", T.yin[:], T.y0[:], [], ["yin"], TAB + 2.3)
 
     col = lambda j: T.col[:, j:j + 1]
     iota(T.coli[:, 0:1], [[1, 1]], 0, 1, ["p"])
     iota(T.ci[:, 0:144], [[1, 144]], 0, 0, ["ci"])
-    iota(T.cj[:, 0:NW], [[0, NW // 4], [16, 4]], 160, 0, ["cj"])
+    iota(T.cj[:, 0:NW], [[0, NW // 4], [2, 4]], -64, 0, ["cj"])
     iota(T.cj[:, 128:128 + ND], [[256, ND]], 0, 0, ["cj2"])
     ts(T.coli[:, 1:2], T.coli[:, 0:1], 15, None, A.bitwise_and, None, ["p"], ["pk"], 1)
     cp(col(0), T.coli[:, 0:1], ["p"], ["c0"], 1)
     cp(col(1), T.coli[:, 1:2], ["pk"], ["c1"], 1)
     tt(col(2), col(0), col(1), A.subtract, ["c0", "c1"], ["c2"], 1)
     ts(col(3), col(2), 15.0, None, A.add, None, ["c2"], ["c3"], 1)
-    ts(col(4), col(1), 37.0, None, A.mult, None, ["c1"], ["c4"], 1)
-    ts(col(5), col(1), 51.0, 8.0, A.add, A.mult, ["c1"], ["c5"], 1)
+    ts(col(4), col(1), 1184.0, -2.0 ** 24, A.mult, A.add, ["c1"], ["c4"], 1)
+    ts(col(5), col(1), 50.0, None, A.add, None, ["c1"], ["c5"], 1)
     ts(col(6), col(1), 1024.0, None, A.add, None, ["c1"], ["c6"], 1)
     ts(col(7), col(1), 16.0, None, A.mult, None, ["c1"], ["c7"], 1)
     cp(col(8), T.hin[:, 0:1], ["hin"], ["c8"], 1)
-    ts(col(9), T.hin[:, 0:1], 2.0, None, A.mult, None, ["hin"], ["c9"], 1)
-    ts(T.col[:, 10:14], T.din[:, 0:4], -16.5, BIG, A.add, A.mult, ["din"], ["c10"], 4)
+    ts(col(9), T.hin[:, 0:1], 1.0 / 16, None, A.mult, None, ["hin"], ["c9"], 1)
+    ts(T.col[:, 10:14], T.din[:, 0:4], -8.875 if FALLA else -16.875, None, A.add, None, ["din"], ["c10"], 4)
     ts(col(14), col(1), 0.0, -1.0, A.is_equal, A.mult, ["c1"], ["c14"], 1)
     tt(col(15), col(14), T.thin[:, 0:1], A.mult, ["c14", "thin"], ["c15"], 1)
     ts(col(16), col(1), 1.0, -0.5, A.is_equal, A.mult, ["c1"], ["c16"], 1)
     tt(col(17), col(15), col(16), A.add, ["c15", "c16"], ["c17"], 1)
+    ts(col(18), col(1), float(HB), None, A.add, None, ["c1"], ["c18"], 1)
     cp(T.cf[:, 0:144], T.ci[:, 0:144], ["ci"], ["cf"], 144)
     sw = lambda j, k: T.sw[:, j * 144 + 15 - k:j * 144 + 143 - k]
     swf = lambda j: T.sw[:, j * 144:j * 144 + 144]
     ts(swf(0), T.cf[:, 0:144], col(3), None, A.is_equal, None, ["cf", "c3"], ["sw0"], 144)
-    for j, v in ((1, -16.0), (2, BIG), (3, -BIG)):
+    for j, v in ((1, -16.0), (2, U), (3, -U), (4, -U / 2)):
         act(swf(j), swf(0), AF.Identity, 0.0, v, ["sw0"], ["sw%d" % j], 144)
-    act(swf(4), swf(0), AF.Identity, 0.0, col(1), ["sw0", "c1"], ["sw4"], 144)
+    ts(T.swi[:], swf(0), col(18), None, A.mult, None, ["sw0", "c18"], ["swi"], 144, 0.5)
     act(swf(5), swf(0), AF.Identity, 0.0, col(8), ["sw0", "c8"], ["sw5"], 144)
     wn = {}
 
     def wt(name):
         wn.setdefault(name, len(wn))
         return T.wt[:, wn[name] * 128:wn[name] * 128 + 128]
+    wf = lambda j: T.wf[:, j * 128:j * 128 + 128]
     cm = T.cf[:, 0:128]
     ts(wt("I"), cm, col(0), None, A.is_equal, None, ["cf", "c0"], ["I"], 128)
-    for name, v in (("nI", -1.0), ("I8", 8.0), ("I512", 512.0), ("IB", 32 * BIG), ("I16", 16.0), ("In2048", -2048.0), ("IBn", -16 * BIG),
-                    ("I16th", 1.0 / 16), ("I32", 32.0), ("In256", -256.0)):
+    for name, v in (("nI", -1.0), ("I8", 8.0), ("I512", 512.0), ("IU", U), ("IU16", (8 if FALLA else 16) * U), ("IV16", 16 * U), ("In64", -64.0), ("I32", 32.0),
+                    ("I21", 2.0 ** 21), ("In25", -2.0 ** 25), ("I4", 4.0), ("I2048", 2048.0), ("I8192", 8192.0), ("I64", 64.0)):
         act(wt(name), wt("I"), AF.Identity, 0.0, v, ["I"], [name], 128)
+    for j, v in ((0, 1.0), (1, 33.0), (2, 0.75 * 2.0 ** -28)):
+        act(wf(j), wt("I"), AF.Identity, 0.0, v, ["I"], ["wf%d" % j], 128)
     ts(wt("ge"), cm, col(2), None, A.is_ge, None, ["cf", "c2"], ["ge"], 128)
     ts(wt("le"), cm, col(3), None, A.is_le, None, ["cf", "c3"], ["lew"], 128)
-    tt(wt("BO"), wt("ge"), wt("le"), A.mult, ["ge", "lew"], ["BO"], 128)
-    act(wt("BO8"), wt("BO"), AF.Identity, 0.0, 8.0, ["BO"], ["BO8"], 128)
-    act(wt("BOn"), wt("BO"), AF.Identity, 0.0, -2 * BIG, ["BO"], ["BOn"], 128)
-    act(wt("H2"), wt("BO"), AF.Identity, 0.0, col(9), ["BO", "c9"], ["H2"], 128)
-    ts(wt("ge"), cm, col(0), 8.0, A.is_ge, A.mult, ["cf", "c0"], ["ge"], 128)
-    tt(wt("tr0"), wt("ge"), wt("le"), A.mult, ["ge", "lew"], ["tr0"], 128)
-    tt(wt("TRI"), wt("tr0"), wt("In256"), A.add, ["tr0", "In256"], ["TRI"], 128)
-    CW = T.wt[0:2, 20 * 128:21 * 128]; CX = T.wt[0:2, 21 * 128:22 * 128]
-    ms(CW, 1.0, ["CW"]); ms(T.wt[0:1, 20 * 128:21 * 128], 327680.0, ["CW"])
+    tt(wt("BO"), wt("ge"), wt("le"), A.mult, ["ge", "lew"], ["BO"], 128, 2)
+    act(wt("nBO"), wt("BO"), AF.Identity, 0.0, -1.0, ["BO"], ["nBO"], 128)
+    act(wt("BOn"), wt("BO"), AF.Identity, 0.0, -2.0 ** 30, ["BO"], ["BOn"], 128)
+    act(wt("BO16"), wt("BO"), AF.Identity, 0.0, -16.0, ["BO"], ["BO16"], 128)
+    act(wt("BOh"), wt("BO"), AF.Identity, 0.0, -0.5, ["BO"], ["BOh"], 128)
+    act(wt("I16"), wt("I"), AF.Identity, 0.0, 16.0, ["I"], ["I16"], 128)
+    bg = lambda name: T.wt[:, wn[name] * 128:wn[name] * 128 + 128:16]
+    act(wt("H16"), wt("BO"), AF.Identity, 0.0, col(9), ["BO", "c9"], ["H16"], 128)
+    ts(wt("gt"), cm, col(0), -1.0, A.is_gt, A.mult, ["cf", "c0"], ["gt"], 128)
+    tt(wt("gt"), wt("gt"), wt("le"), A.mult, ["gt", "lew"], ["gt"], 128, 2)
+    tt(wt("TRI"), wt("gt"), wt("I64"), A.add, ["gt", "I64"], ["TRI"], 128, 2)
+    ts(wt("le"), cm, col(0), -1.0, A.is_lt, A.mult, ["cf", "c0", "TRI"], ["lew"], 128)
+    tt(wt("le"), wt("le"), wt("ge"), A.mult, ["ge", "lew"], ["lew"], 128, 2)
+    tt(wt("le"), wt("le"), wt("I"), A.add, ["I", "lew"], ["lew"], 128, 2)
+    assert len(wn) <= 27
+    rows = lambda j, n: T.wt[0:n, (j + 4) * 128:(j + 4) * 128 + 128]
+    for n, v in ((3, 1.0 / 32), (2, -32.0), (1, 10240.0)):
+        ms(rows(23, n), v, ["CW"])
     if KA < 16:
-        ms(CX, 7.5, ["CX"]); ms(T.wt[0:1, 21 * 128:22 * 128], 2304.0, ["CX"])
-    assert len(wn) <= 20
+        ms(rows(24, 2), 7.5, ["CX"]); ms(rows(24, 1), 2304.0, ["CX"])
+    if SSP:
+        iota(T.cj[:, 256:384], [[0, 8], [1, 16]], 0, 0, ["cj3"])
+        ts(col(19), col(0), 1.0, 1024.0, A.is_equal, A.mult, ["c0"], ["c19"], 1)
+        ts(col(20), col(0), 2.0, 160.0, A.is_equal, A.mult, ["c0"], ["c20"], 1)
+        tt(col(21), col(19), col(20), A.add, ["c19", "c20"], ["c21"], 1)
+        ts(col(22), col(0), 0.0, -2.0 ** 24, A.is_equal, A.mult, ["c0"], ["c22"], 1)
+        ts(rows(25, 128), T.cj[:, 256:384], col(21), col(22), A.mult, A.add, ["cj3", "c21", "c22"], ["CS"], 128)
     ct = lambda j, n=None: T.ct[:, j * 128:j * 128 + (n or NW)]
-    ms(ct(0, 128), 1.0, ["ones"]); ms(ct(1), 272.0, ["c256"]); ms(ct(2), 144.0, ["c128"]); ms(ct(3), -1.0, ["neg"])
-    ts(ct(4), ct(0), col(5), None, A.mult, None, ["ones", "c5"], ["cP"], 64)
+    ms(ct(0, 128), 1.0, ["ones"]); ms(ct(1), Y0 - 16, ["c176"]); ms(ct(2), 144.0, ["c128"]); ms(ct(3), -1.0, ["neg"])
+    for c in range(C):
+        b0 = 16 * sum(NWS[:c]) + 16 * c
+        ms(T.fg[:, b0:b0 + 16], 0.0, [("pad", c)])
+    ts(ct(4), T.cj[:, 0:NW], col(1), None, A.subtract, None, ["cj", "c1"], ["cP"], NW)
     ts(ct(5), ct(0), col(17), None, A.mult, None, ["ones", "c17"], ["cT"], 64)
+    ts(col(23), col(1), float(TA), -8.0, A.is_lt, A.mult, ["c1"], ["c23"], 1)
     for t in range(4):
-        ts(ct(6 + t), ct(0), col(10 + t), None, A.mult, None, ["ones", "c10"], ["cD%d" % t], 64)
-    cp(ct(10), T.cj[:, 0:NW], ["cj"], ["turn"], NW)
+        ts(ct(6 + t), ct(0), col(10 + t), col(23), A.mult, A.add, ["ones", "c10", "c23"], ["cD%d" % t], 64)
     ts(ct(11, ND), T.cj[:, 128:128 + ND], col(7), None, A.add, None, ["cj2", "c7"], ["cI"], ND)
-    cp(T.bco[:], T.ci[:, 0:16], ["ci"], ["bco"], 16)
-    ts(T.cf[:, 144:160], T.cf[:, 0:16], col(1), 2048.0, A.is_gt, A.mult, ["cf", "c1"], ["dmc"], 16)
+    ts(T.cf[:, 144:160], T.cf[:, 0:16], col(1), -1.0, A.is_equal, A.mult, ["cf", "c1"], ["dmc"], 16)
+    dm = lambda r: T.dm[:, r * 128:r * 128 + 128]
+    cp(dm(0), wt("I"), ["I"], ["dm0"], 64)
     for r in range(1, 16):
-        if r % 2:
-            ts(T.dm[:, r * 128:r * 128 + 128], wt("I"), T.cf[:, 144 + r:145 + r], None, A.mult, None, ["I", "dmc"], ["dm%d" % r], 64)
-        else:
-            act(T.dm[:, r * 128:r * 128 + 128], wt("I"), AF.Identity, 0.0, T.cf[:, 144 + r:145 + r], ["I", "dmc"], ["dm%d" % r], 128)
+        ts(dm(r), wt("le"), T.cf[:, 144 + r:145 + r], None, A.max, None, ["lew", "dmc"], ["dm%d" % r], 64)
+    stage[0] = 1
     ms(T.st[:, 1024:1040], 0.0, ["st"])
-    allp = lambda b: [("P", b, s) for s in range(4)]
-    for h, s, b1, b2 in ((0, "a", 2, 6), (1, "b", 3, 7)):
+    for h, s, b in ((0, "a", 2), (1, "b", 3)):
         hs = slice(h * 512, h * 512 + 512)
-        ts(T["pb%d" % b1][:], T.kin[:, hs], 8192.0, -8193.0, A.is_ge, A.mult, ["kin"], allp(b1), 512)
-        tt(T.w1[:, hs], T["pb%d" % b1][:], T.kin[:, hs], A.add, allp(b1) + ["kin"], ["w1" + s], 512)
-        act(T["pb%d" % b2][:], T.yin[:, hs], AF.Identity, 1 - 7.5 / 16, 1.0 / 16, ["yin"], allp(b2), 512)
-        tt(T.st[:, hs], T["pb%d" % b2][:], T.w1[:, hs], A.add, allp(b2) + ["w1" + s], ["st"], 512)
-    ts(T.lz[:, 0:256], T.tin[:], 8192.0, None, A.is_ge, None, ["tin"], [("lz", 0, c) for c in range(C)], 256)
+        ts(T.w1[:, hs], T.kin[:, hs], 32.0, Y0 * 2 ** 21, A.mult, A.add, ["kin"], ["w1" + s], 512)
+        act(T.ys[:, hs], T.w1[:, hs], AF.Sign, Y0 * 2 ** 21 + 2 ** 18 - 32, -1.0, ["w1" + s], ["ys" + s], 512)
+        act(T.ys[:, hs], T.ys[:, hs], AF.Sign, 0.5, 1.0, ["ys" + s], ["ys" + s], 512)
+        mm(acc(T["pb%d" % b][:], [(wf(0), T.w1[:, hs], 1), (wt("I21"), T.yin[:, hs])], 512), ["w1" + s, "yin", "wf0", "I21"], allp(b))
+        tt(T.st[:, hs], T["pb%d" % b][:], T.ys[:, hs], A.mult, allp(b) + ["ys" + s], ["st"], 512)
+    stage[0] = 0
     ts(T.tnm[:], T.tin[:], 8191, None, A.bitwise_and, None, ["tin"], ["tnm"], 256)
     cp(T.lu[:, 0:256], T.tnm[:], ["tnm"], [("lu", 0, c) for c in range(C)], 256)
-    cp(T.ln[:, 0:256], T.tnm[:], ["tnm"], [("ln", 0, c) for c in range(C)], 256)
+    ts(T.lz[:, 0:256], T.tin[:], 8192.0, None, A.is_ge, None, ["tin"], [("lz", 0, c) for c in range(C)], 256)
 
     def mask(es):
         return sum(1 << e for e in es)
+
+    def send(kind, t, c, to, frm, r, w):
+        s = "a%d_%d_%d" % (kind, t + 1, c)
+        i = op("pool", lambda h: h.remote_dma(to, frm, T.sem[s], T.sem.sent, dst[1], dst[0], mask(eng)), r, [], 0.3, fin=False)
+        sent[0] += len(eng)
+        op(None, None, [], w, 0.0, sem=(s, len(eng)), lat=COMM, soft=[i])
     stream = [0]
     G = 4
     for t in range(4):
         for c in range(C):
             NW = NWS[c]; ND = NW // 16
+            BA, BS = 4 + c % 2, 6 + c % 2
             w0 = sum(NWS[:c]); sl = slice(w0, w0 + NW); s4 = slice(t * 256 + w0, t * 256 + w0 + NW)
-            stage[0] = t * C + c
+            stage[0] = OFF * c + STP * t
             K = lambda s: (s, c)
             S = lambda s: T[s][:, sl]
             x2 = t * 512 + 2 * w0
@@ -337,198 +453,231 @@ def build(T, dst, eng):
                 x, fl, kx, kf = T.xin[:, sl], ct(3), "xin", "neg"
             else:
                 x, fl, kx = T.lx[:, x2:x2 + NW], T.lx[:, x2 + NW:x2 + 2 * NW], ("lx", t, c); kf = kx
-            nf, nu, asl = T.ln[:, s4], T.lu[:, s4], T.lz[:, s4]
-            kn, ku, kz = ("ln", t, c), ("lu", t, c), ("lz", t, c)
-            if t > 0:
-                if SENDU:
-                    cp(nf, nu, [ku], [kn], NW)
-                else:
-                    cp(nu, nf, [kn], [ku], NW)
+            nu, asl = T.lu[:, s4], T.lz[:, s4]
+            ku, kz = ("lu", t, c), ("lz", t, c)
+            nf, kn = S("nf"), K("nf")
+            ts(nf, nu, 32.0, None, A.mult, None, [ku], [kn], NW)
             xn, fo, kxn, kfo = T.xs[:, x2:x2 + NW], T.xs[:, x2 + NW:x2 + 2 * NW], ("xn", t, c), ("fo", t, c)
             big = lambda s, a, b: T[s][:, 16 * w0 + a:16 * w0 + b]
+            f0 = 16 * w0 + 16 * c + 16
+            fgs = lambda a, b: T.fg[:, f0 + 16 * a:f0 + 16 * b]
             first = t == 0 and c == 0
-            wg = NW * (G0 if first else GD) // 16; n0 = t * 256 + w0
-            if wg > 0:
-                cp(big("fg", 0, 16 * wg), T.ftab[:].indirect(T.lu[:, n0:n0 + wg]), ["ftab", ku], [K("fgd")], 16 * wg, GR)
-            if wg < NW:
-                act(big("fg", 16 * wg, 16 * NW), T.ftab[:].indirect(T.lu[:, n0 + wg:n0 + NW]), AF.Copy, 0, 1, ["ftab", ku], [K("fga")], 16 * (NW - wg), GR)
-            kfg = [K("fgd"), K("fga")]
-            wd = NW * (16 if first else DERD) // 16
-            if wd > 0:
-                ts(T.eg[:, w0:w0 + wd, :], big("fg", 0, 16 * wd), 1.0 / 16, 143.53125, A.mult, A.add, kfg, [K("egd")], 16 * wd, 0.5)
-            if wd < NW:
-                act(T.eg[:, w0 + wd:w0 + NW, :], big("fg", 16 * wd, 16 * NW), AF.Identity, 143.53125, 1.0 / 16, kfg, [K("ega")], 16 * (NW - wd))
-            ke = [K("egd"), K("ega")]
+            wg = NW * (G0 if first else GD) // 16 // 4 * 4; n0 = t * 256 + w0
+            cuts = lambda a, b, n: [z for z in [(a + (b - a) * j // n // 4 * 4, a + (b - a) * (j + 1) // n // 4 * 4 if j < n - 1 else b) for j in range(n)] if z[1] > z[0]]
+            under = lambda s, a, b: [(s, c, j) for j in range(a, b, 4)]
+            for a, b in cuts(0, wg, GSD):
+                cp(fgs(a, b), T.ftab[:].indirect(T.lu[:, n0 + a:n0 + b]), ["ftab", ku], under("fg", a, b), 16 * (b - a), GR)
+            for a, b in cuts(wg, NW, GS):
+                act(fgs(a, b), T.ftab[:].indirect(T.lu[:, n0 + a:n0 + b]), AF.Copy, 0, 1, ["ftab", ku], under("fg", a, b), 16 * (b - a), GR)
+            wd = NW * (16 if first else DERD) // 16 // 4 * 4
+            for a, b in cuts(0, wd, ESD):
+                ts(T.eg[:, w0 + a:w0 + b, :], fgs(a, b), 1.0 / 16, 143.53125, A.mult, A.add, under("fg", a, b), under("eg", a, b), 16 * (b - a), 0.5)
+            for a, b in cuts(wd, NW, ES):
+                act(T.eg[:, w0 + a:w0 + b, :], fgs(a, b), AF.Identity, 143.53125, 1.0 / 16, under("fg", a, b), under("eg", a, b), 16 * (b - a))
+            kfg = under("fg", 0, NW); ke = under("eg", 0, NW)
             act(S("za"), x, AF.Relu, 16.0, -16.0, [kx], [K("za")], NW)
-            cn, kcn = pt(4, c); gid = ("cn", t, c)
-            mm([(cn, wt("I8"), fl, True, False, NW), (cn, wt("I512"), asl, False, False, NW)], [kf, kz, ku, "I8", "I512"], [kcn], (4, gid, False))
+            cn, kcn = pt(BA, 0); gid = ("cn", t, c)
             zparts = []
-            fk = lambda k: T.fg[:, 16 * w0 + k:16 * (w0 + NW):16]
+            fk = lambda k: T.fg[:, f0 + k:f0 + 16 * NW:16]
             for k0 in range(0, KA, G):
-                b = stream[0] % 2; stream[0] += 1
+                b = GB[k0 // G % len(GB)]
                 it = []
                 for j in range(G):
-                    o = T["pb%d" % b][:, j * NW:(j + 1) * NW]
-                    it += acc(o, [(wt("I"), fk(k0 + j)), (wt("nI"), x)], NW)
-                mm(it, kfg + [kx, "I", "nI"], [("P", b, "s")])
-                act(big("zg", k0 * NW, (k0 + G) * NW), T["pb%d" % b][:, 0:G * NW], AF.Identity, 2311.5, 1.0, [("P", b, "s")], [("zg", c, k0)], G * NW)
+                    it += acc(T["pb%d" % b][:, j * NW:(j + 1) * NW], [(wt("I"), fk(k0 + j)), (wt("nI"), x)], NW)
+                mm(it, kfg + [kx, "I", "nI"], allp(b))
+                act(big("zg", k0 * NW, (k0 + G) * NW), T["pb%d" % b][:, 0:G * NW], AF.Identity, 2311.5, 1.0, allp(b), [("zg", c, k0 + j) for j in range(G)], G * NW)
                 zparts.append((k0, [(k0 + j, big("zg", (k0 + j) * NW, (k0 + j + 1) * NW)) for j in range(G)]))
             if KA < 16:
-                b = stream[0] % 2; stream[0] += 1
-                it = []
-                it += acc(T["pb%d" % b][:, 0:NW], [(wt("nI"), x), (CX, T.ct[0:2, 0:NW])], NW)
-                mm(it, [kx, "nI", "CX", "ones"], [("P", b, "s")])
+                xp, kxp = pt(BS, 3)
+                mm(acc(xp, [(wt("nI"), x), (rows(24, 2), T.ct[0:2, 0:NW])], NW), [kx, "nI", "CX", "ones"], [kxp])
                 for k0 in range(KA, 16):
-                    tt(big("zg", k0 * NW, (k0 + 1) * NW), fk(k0), T["pb%d" % b][:, 0:NW], A.add, kfg + [("P", b, "s")], [("zg", c, k0)], NW)
-                    zparts.append((k0, [(k0, big("zg", k0 * NW, (k0 + 1) * NW))]))
-            for k0 in range(0, 16, 4):
-                mm([(cn, sw(1, k), T.eg[:, sl, k], False, False, NW) for k in range(k0, k0 + 4)], ke + ["sw1"], [kcn], (4, gid, False))
-            for j, (k0, parts) in enumerate(zparts):
-                e = j == len(zparts) - 1
-                mm([(cn, sw(0, k), ap, False, e and k == parts[-1][0], NW) for k, ap in parts], [("zg", c, k0), "sw0"], [kcn], (4, gid, e))
-            act(S("cand"), cn, AF.Sign, 108.0, -1.0, [kcn], [K("cand")], NW)
-            mp, kmp = pt(5, 0); pr, kpr = pt(5, 1); ix, kix = pt(5, 2, ND)
-            mm(acc(mp, [(wt("BO8"), S("cand")), (wt("I"), ct(1))], NW) + acc(pr, [(wt("TRI"), S("cand")), (wt("I"), ct(4))], NW),
-               [K("cand"), "BO8", "TRI", "I", "c256", "cP"], [kmp, kpr])
-            tt(S("pos"), mp, ct(10), A.min, [kmp, "turn"], [K("pos")], NW)
-            tt(S("go"), pr, S("pos"), A.is_equal, [kpr, K("pos")], [K("go")], NW)
-            dl, kdl = pt(5, 3)
-            mm(acc(dl, [(wt("TRI"), S("cand")), (wt("I"), ct(4)), (wt("nI"), S("pos"))], NW), [K("cand"), K("pos"), "TRI", "I", "nI", "cP"], [kdl])
-            act(S("fall"), dl, AF.Sign, 8.0, 1.0, [kdl], [K("fall")], NW)
-            mm(acc(ix, [(wt("I"), ct(11, ND))] + [(sw(4, r), T.go[:, w0 + r:w0 + NW:16]) for r in range(16)], ND), [K("go"), "sw4", "I", "cI"], [kix])
-            iu = T.iu[:, w0 // 16:w0 // 16 + ND]
-            cp(iu, ix, [kix], [K("iu")], ND)
-            if EGA:
-                act(S("e0"), big("fg", 0, 16 * NW).indirect(iu), AF.Identity, 143.53125, 1.0 / 16, kfg + [K("iu")], [K("e0")], NW, GR)
+                    tt(big("zg", k0 * NW, (k0 + 1) * NW), fk(k0), xp, A.add, kfg + [kxp], [("zg", c, k0)], NW)
+                for k0 in range(KA, 16, G):
+                    zparts.append((k0, [(k0 + j, big("zg", (k0 + j) * NW, (k0 + j + 1) * NW)) for j in range(G)]))
+            turned = T["pb%d" % BA][0:NW, 0:128]; tk = lambda k: T["pb%d" % BA][0:NW, k:128:16]
+            sq = lambda name: T.wt[0:NW, wn[name] * 128:wn[name] * 128 + NW]
+            back = T.tr[0:NW, 128 * c:128 * c + 128]
+            if TG:
+                sums = [([(tk(k), ap, bg("BO"), 8) for k, ap in parts], [("zg", c, k) for k, ap in parts] + ["BO"]) for k0, parts in zparts]
+                sums[0:0] = [([(turned, fl, wt("I8"), 128)] * (k0 == 0) + [(tk(k), T.eg[:, sl, k], bg("BO16"), 8) for k in range(k0, k0 + 8)], ke + [kf, "BO16", "I8"]) for k0 in (0, 8)]
+                sums[-1:-1] = [([(turned, asl, wt("I512"), 128)], [kz, "I512"])]
             else:
-                ts(S("e0"), big("fg", 0, 16 * NW).indirect(iu), 1.0 / 16, 143.53125, A.mult, A.add, kfg + [K("iu")], [K("e0")], NW, GR)
-            tt(S("ee"), S("e0"), S("pos"), A.min, [K("e0"), K("pos")], [K("ee")], NW, 2)
-            d0, kd0 = pt(5, 0); ds, kds = pt(5, 2); au, kau = pt(5, 3)
-            mm(acc(au, [(wt("I"), x), (wt("I"), S("za"))], NW), [kx, K("za"), "I"], [kau])
-            mm(acc(ds, [(wt("I"), x), (wt("I"), S("za")), (wt("nI"), S("ee"))], NW) + acc(d0, [(wt("I"), x), (wt("nI"), S("ee"))], NW),
-               [kx, K("za"), K("ee"), "I", "nI"], [kds, kd0])
-            act(S("le"), ds, AF.Relu, 32.0 * 145, 32.0, [kds], [K("le")], NW)
+                sums = [([(cn, sw(0, k), ap, NW) for k, ap in parts], [("zg", c, k) for k, ap in parts] + ["sw0"]) for k0, parts in zparts]
+                sums[1:1] = [([(cn, sw(1, k), T.eg[:, sl, k], NW) for k in range(k0, k0 + 4)], ke + ["sw1"]) for k0 in range(0, 16, 4)]
+                sums[-1:-1] = [([(cn, wt("I8"), fl, NW), (cn, wt("I512"), asl, NW)], [kf, kz, "I8", "I512"])]
+            for j, (it, r) in enumerate(sums):
+                e = j == len(sums) - 1
+                mm([(o, a, b, j == 0 and i == 0, e and i == len(it) - 1, n) for i, (o, a, b, n) in enumerate(it)], r, [kcn], (BA, gid, e))
+            if TG:
+                act(back, turned, AF.Copy, 0.0, 1.0, [kcn], [K("tr")], 128)
+                mm(acc(cn, [(back, sq("I"))], NW), [K("tr"), "I"], [kcn])
+            act(S("cand"), cn, AF.Sign, 108.0, -1.0, [kcn], [K("cand")], NW)
+            mp, kmp = pt(BA, 1); pr, kpr = pt(BA, 2); ix = pt(BA, 1, ND)[0]; au, kau = pt(BA, 3)
+            mm(acc(mp, [(wt("I"), ct(4)), (wt("nBO"), S("cand"))], NW) + acc(pr, [(wt("I"), ct(4)), (wt("TRI"), S("cand"))], NW),
+               [K("cand"), "nBO", "TRI", "I", "cP"], [kmp, kpr])
+            act(S("r2"), mp, AF.Relu, col(5), 1.0, [kmp, "c5"], [K("r2")], NW)
+            tt(S("go"), pr, S("r2"), A.is_equal, [kpr, K("r2")], [K("go")], NW)
+            if FALLA:
+                dl, kdl = pt(BS, 2)
+                mm(acc(dl, [(wt("I"), ct(4)), (wt("TRI"), S("cand")), (wt("nI"), S("r2"))], NW), [K("cand"), K("r2"), "TRI", "I", "nI", "cP"], [kdl])
+                act(S("fall"), dl, AF.Sign, -1.0, 1.0, [kdl], [K("fall")], NW)
+            else:
+                tt(S("fall"), pr, S("r2"), A.is_gt, [kpr, K("r2")], [K("fall")], NW)
+            mm(acc(ix, [(wt("I"), ct(11, ND))] + [(T.swi[:, 15 - r:143 - r], T.go[:, w0 + r:w0 + NW:16]) for r in range(16)], ND),
+               [K("go"), "swi", "I", "cI"], [kmp])
+            iu = T.iu[:, w0 // 16:w0 // 16 + ND]
+            ts(iu, ix, 16.0 - HB, None, A.add, None, [kmp], [K("iu")], ND)
+            win = T.fg[:, f0 - 16:f0 + 16 * NW].indirect(iu)
+            if EGA:
+                act(S("ee"), win, AF.Identity, 143.53125, 1.0 / 16, kfg + [K("iu"), ("pad", c)], [K("ee")], NW, GR)
+            else:
+                ts(S("ee"), win, 1.0 / 16, 143.53125, A.mult, A.add, kfg + [K("iu"), ("pad", c)], [K("ee")], NW, GR)
+            ds, kds = pt(BA, 1); d0, kd0 = pt(BA, 2)
+            act(S("zc"), S("ee"), AF.Relu, 2320.0, -16.0, [K("ee")], [K("zc")], NW)
+            mm(acc(ds, [(wt("I"), x), (wt("I"), S("za")), (wt("nI"), S("ee"))], NW), [kx, K("za"), K("ee"), "I", "nI"], [kds])
+            mm(acc(d0, [(wt("I"), x), (wt("nI"), S("ee"))], NW), [kx, K("ee"), "I", "nI"], [kd0])
+            mm(acc(au, [(wt("I"), x), (wt("I"), S("za")), (wt("I"), S("zc"))], NW), [kx, K("za"), K("zc"), "I"], [kau])
+            act(S("le"), ds, AF.Relu, 64.0 * 145, 64.0, [kds], [K("le")], NW)
             tt(S("qq"), au, S("le"), A.min, [kau, K("le")], [K("qq")], NW)
             act(xn, d0, AF.Abs, 144.0, 1.0, [kd0], [kxn], NW)
-            act(S("zc"), S("ee"), AF.Relu, 2320.0, -16.0, [K("ee")], [K("zc")], NW)
             R = REP * NW
-            if 2 * R <= 512:
-                kap, th, kkap, kth = (lambda a, b, s: T.pb2[:, a:b:s]), (lambda a, b, s: T.pb2[:, R + a:R + b:s]), ("P", 2, 0), ("P", 2, 1)
-            else:
-                kap, th, kkap, kth = (lambda a, b, s: T.pb2[:, a:b:s]), (lambda a, b, s: T.pb2[:, a:b:s]), ("P", 2, 0), ("P", 2, 0)
-            wq, kwq = pt(3, c); gid = ("w", t, c)
-            mm([(wq, wt("I"), ct(6 + t), True, False, NW), (wq, wt("IB"), asl, False, False, NW), (wq, wt("IBn"), S("fall"), False, False, NW)],
-               [kz, K("fall"), K("le"), "I", "IB", "IBn", "cD%d" % t], [kwq], (3, gid, False))
-            for nm_, src, ksrc, o, wj, terms in (("tb", kap, kkap, A.is_equal, 2, [(S("ee"), K("ee")), (S("le"), K("le"))]),
-                                                 ("ta", th, kth, A.is_gt, 3, [(ct(2), "c128"), (S("zc"), K("zc")), (S("qq"), K("qq"))])):
+            wq, kwq = pt(BA, 0); gid = ("w", t, c); sums = {}
+            term = lambda j, k, ap: (tk(k), ap, bg({2: "BO", 3: "nBO", 4: "BOh"}[j]), 8) if TW else (wq, sw(j, k), ap, NW)
+            for k0 in range(0, TA, G):
+                b = TB[k0 // G % len(TB)]
                 it = []
+                for j in range(G):
+                    it += acc(T["pb%d" % b][:, j * NW:(j + 1) * NW], [(wt("I"), T.eg[:, sl, k0 + j]), (wt("nI"), S("qq"))], NW)
+                mm(it, ke + [K("qq"), "I", "nI"], allp(b))
+                act(big("ta", k0 * NW, (k0 + G) * NW), T["pb%d" % b][:, 0:G * NW], AF.Sign, -144.5, 1.0, allp(b), [("ta", c, k0 + j) for j in range(G)], G * NW)
+                sums["ta", k0] = ([term(4, k, big("ta", k * NW, (k + 1) * NW)) for k in range(k0, k0 + G)], [("ta", c, k0), "sw4", "BOh"])
+            for nm_, b, o, wj, k1, terms in (("tb", 2, A.is_equal, 2, 0, [(S("ee"), K("ee")), (S("le"), K("le"))]),
+                                             ("ta", 3, A.is_gt, 3, TA, [(ct(2), "c128"), (S("qq"), K("qq"))])):
+                if k1 == 16:
+                    continue
+                it = []; pb = T["pb%d" % b]
                 for j in range(REP):
-                    it += acc(src(j, R, REP), [(wt("I"), a) for a, _ in terms], NW)
-                mm(it, [k for _, k in terms] + ["I"], [ksrc])
-                for k0 in range(0, 16, REP):
-                    tt(big(nm_, k0 * NW, k0 * NW + R), T.eg[:, sl, k0:k0 + REP], src(0, R, 1), o, ke + [ksrc], [(nm_, c, k0)], R)
-                for k0 in range(0, 16, 4):
-                    e = nm_ == "ta" and k0 == 12
-                    it = []
-                    for k in range(k0, k0 + 4):
-                        kb_ = k - k % REP
-                        it.append((wq, sw(wj, k), T[nm_][:, 16 * w0 + kb_ * NW + k % REP:16 * w0 + kb_ * NW + R:REP], False, e and k == 15, NW))
-                    mm(it, [(nm_, c, k) for k in range(k0 - k0 % REP, k0 + 4, REP)] + ["sw%d" % wj], [kwq], (3, gid, e))
-            u0, ku0 = pt(6, 0); v2, kv2 = pt(6, 1); dy, kdy = pt(6, 2); sn, ksn = pt(6, 3); ud = pt(6, 3, ND)[0]
+                    it += acc(pb[:, j:R:REP], [(wt("I"), a) for a, _ in terms], NW)
+                mm(it, [k for _, k in terms] + ["I"], allp(b))
+                for k0 in range(k1, 16, REP):
+                    tt(big(nm_, k0 * NW, k0 * NW + R), T.eg[:, sl, k0:k0 + REP], pb[:, 0:R], o, ke + allp(b), [(nm_, c, k0 + j) for j in range(REP)], R)
+                for k0 in range(k1, 16, G):
+                    sums[nm_, k0] = ([term(wj, k, T[nm_][:, 16 * w0 + (k - k % REP) * NW + k % REP:16 * w0 + (k - k % REP) * NW + R:REP]) for k in range(k0, k0 + G)],
+                                     [(nm_, c, k) for k in range(k0, k0 + G)] + ["sw%d" % wj, "nBO", "BO"])
+            if TA < 16 or not MIX:
+                seq = [("tb", k0) for k0 in range(0, 16, G)] + [("ta", k0) for k0 in range(0, 16, G)]
+            else:
+                seq = [(nm_, k0) for k0 in range(0, 16, G) for nm_ in ("tb", "ta")]
+            if TW:
+                mm([(turned, asl, wt("I16"), True, False, 128), (turned, S("fall"), wt("I8" if FALLA else "I16"), False, False, 128)],
+                   [kz, K("fall"), kxn, K("qq"), "I16", "I8"], [kwq], (BA, gid, False))
+                for j, z in enumerate(seq):
+                    it, r = sums[z]; e = j == len(seq) - 1
+                    mm([(o, a, b, False, e and i == len(it) - 1, n) for i, (o, a, b, n) in enumerate(it)], r, [kwq], (BA, gid, e))
+                act(back, turned, AF.Copy, 0.0, 1.0, [kwq], [K("tr")], 128)
+                if WQB is None:
+                    mm(acc(wq, [(wt("IU"), ct(6 + t)), (wf(0), nf, 1), (back, sq("IU"))], NW), [kn, K("tr"), "wf0", "IU", "cD%d" % t], [kwq])
+                else:
+                    wq, kwq = pt(WQB, 0)
+                    mm([(wq, wt("IU"), ct(6 + t), True, False, NW), (wq, wf(0), nf, False, False, 4 * NW)], [kn, "wf0", "IU", "cD%d" % t], [kwq], (WQB, gid, False))
+                    mm([(wq, back, sq("IU"), False, True, NW)], [K("tr"), "IU"], [kwq], (WQB, gid, True))
+            else:
+                for j, z in enumerate(seq):
+                    it, r = sums[z]
+                    mm([(o, a, b, j == 0 and i == 0, False, n) for i, (o, a, b, n) in enumerate(it)], r + ([kxn, K("qq")] if j == 0 else []), [kwq], (BA, gid, False))
+                    if j == 0:
+                        mm([(wq, wt("IU"), ct(6 + t), False, False, NW), (wq, wf(0), nf, False, False, 4 * NW)],
+                           [kn, "wf0", "IU", "cD%d" % t], [kwq], (BA, gid, False))
+                mm([(wq, wt("IV16"), asl, False, False, NW), (wq, wt("IU16"), S("fall"), False, True, NW)],
+                   [kz, K("fall"), "IU16", "IV16"], [kwq], (BA, gid, True))
+            u0, ku0 = pt(BS, 0); v2, kv2 = pt(BS, 1); dy, kdy = pt(BS, 2); sn, ksn = pt(BS, 3); ud = pt(BS, 3, ND)[0]
             mm(acc(ud, [(sw(5, r), T.xs[:, x2 + r:x2 + NW:16]) for r in range(16)], ND), [kxn, "sw5"], [ksn])
-            mm(acc(u0, [(wt("H2"), xn)], NW), [kxn, "H2"], [ku0])
+            mm(acc(u0, [(wt("H16"), xn)], NW), [kxn, "H16"], [ku0])
             dsl = slice(w0 // 16, w0 // 16 + ND)
             ts(T.cd0[:, dsl], ud, 241.0, None, A.mult, None, [ksn], [K("cd0")], ND)
             ts(T.cd[:, dsl], T.cd0[:, dsl], 6, 1023, A.logical_shift_right, A.bitwise_and, [K("cd0")], [K("cd")], ND)
             cu = T.cu[:, dsl]
             cp(cu, T.cd[:, dsl], [K("cd")], [K("cu")], ND)
-            act(S("hi"), u0, AF.Identity, 159.5 + 1.0 / 2048, 1.0 / 2048, [ku0], [K("hi")], NW)
-            ts(S("cb0"), u0, 120.5, None, A.mult, None, [ku0], [K("cb0")], NW)
-            mm(acc(v2, [(wt("H2"), xn), (CW, T.ct[0:2, 0:NW]), (wt("In2048"), S("hi"))], NW), [kxn, K("hi"), "H2", "CW", "ones", "In2048"], [kv2])
-            sa, ksa = pt(7, 0); sb, ksb = pt(7, 1); ka, kka = pt(7, 2); sd, ksd = pt(7, 3)
-            act(sa, nf, AF.Identity, col(4), 1.0, [kn, "c4"], [ksa], NW)
+            act(S("hi"), u0, AF.Identity, 159.5 + 1.0 / 2048, 1.0 / 64, [ku0], [K("hi")], NW)
+            mm(acc(v2, [(wt("H16"), xn), (rows(23, 3), T.ct[0:3, 0:NW]), (wt("In64"), S("hi"))], NW), [kxn, K("hi"), "H16", "CW", "ones", "In64"], [kv2])
             tt(S("pp"), v2, nf, A.mult, [kv2, kn], [K("pp")], NW)
-            ts(S("q5"), S("pp"), 5, None, A.logical_shift_right, None, [K("pp")], [K("q5")], NW)
-            tt(S("ss"), sa, S("q5"), A.add, [ksa, K("q5")], [K("ss")], NW)
-            ts(S("nn"), S("ss"), 8191, None, A.bitwise_and, None, [K("ss")], [K("nn")], NW)
-            ts(S("kc"), T.st[:].indirect(cu), MAGIC, MAGIC + 1, A.add, A.subtract, ["st", K("cu")], [K("kc")], NW, GR)
-            tt(S("yq"), T.st[:].indirect(cu), S("kc"), A.subtract, ["st", K("cu"), K("kc")], [K("yq")], NW, GR)
-            mm(acc(dy, [(wt("nI"), xn), (wt("I16"), S("yq"))], NW), [kxn, K("yq"), "nI", "I16"], [kdy])
-            act(S("ad"), dy, AF.Abs, -8.5, 1.0, [kdy], [K("ad")], NW)
-            mm(acc(sn, [(wt("BOn"), ct(5)), (wt("BOn"), S("ad"))], NW), [K("ad"), "BOn", "cT"], [ksn])
-            act(fo, sn, AF.Sign, 0.0, 1.0, [ksn], [kfo], NW)
-            tt(S("zz"), sn, S("kc"), A.min, [ksn, K("kc")], [K("zz")], NW)
-            act(sb, S("zz"), AF.Relu, 0.0, -BIG, [K("zz")], [ksb], NW)
-            if t < 3:
-                lx = T.lx[:, x2 + 512:x2 + 512 + 2 * NW]; sx = T.xs[:, x2:x2 + 2 * NW]; sa_ = "a0_%d_%d" % (t + 1, c)
-                i = op("pool", lambda h, lx=lx, sx=sx, s=sa_: h.remote_dma(lx, sx, T.sem[s], T.sem.sent, dst[1], dst[0], mask(eng)),
-                       [kxn, kfo], [], 0.3, fin=False)
-                sent[0] += len(eng)
-                op(None, None, [], [("lx", t + 1, c)], 0.0, sem=(sa_, len(eng)), lat=COMM, soft=[i])
-            tt(ka, wq, nf, A.min, [kwq, kn], [kka], NW)
-            act(sa, wq, AF.Identity, 0.0, -1.0, [kwq], [ksa], NW)
-            tt(S("t1"), sa, S("nn"), A.min, [ksa, K("nn")], [K("t1")], NW)
-            tt(S("nm1"), ka, S("t1"), A.max, [kka, K("t1")], [K("nm1")], NW)
-            tt(sd, sb, S("nm1"), A.min, [ksb, K("nm1")], [ksd], NW)
-            no, zo, uo = T.ns[:, s4], T.zs[:, s4], T.us[:, s4]
-            kno, kzo, kuo = ("ns", t, c), ("zs", t, c), ("us", t, c)
-            tt(no, sd, S("zz"), A.max, [ksd, K("zz")], [kno], NW)
-            tt(zo, ka, no, A.is_equal, [kka, kno], [kzo], NW)
-            if t < 3:
-                sb_ = "a1_%d_%d" % (t + 1, c); n4 = (t + 1) * 256 + w0; m4 = t * 256 + w0; h2 = NW // 2
-                if SENDU:
-                    cp(uo, no, [kno], [kuo], NW)
-                    tr = [(T.lu[:, n4:n4 + NW], uo, eng[:4]), (T.lz[:, n4:n4 + NW], zo, eng[4:])]
-                    rr, ww = [kuo, kzo], [("lu", t + 1, c), ("lz", t + 1, c)]
-                else:
-                    tr = [(T.ln[:, n4:n4 + h2], T.ns[:, m4:m4 + h2], eng[:2]), (T.ln[:, n4 + h2:n4 + NW], T.ns[:, m4 + h2:m4 + NW], eng[2:4]),
-                          (T.lz[:, n4:n4 + NW], zo, eng[4:])]
-                    rr, ww = [kno, kzo], [("ln", t + 1, c), ("lz", t + 1, c)]
-                i = op("pool", lambda h, tr=tr, s=sb_: h.remote_dma_fused(
-                    [RemoteDMATransfer(dst_ids=[DstId(rid=dst[0], pnc=dst[1])], dma_engine_mask=mask(e), remote_sem=T.sem[s], src=a, dst=b)
-                     for b, a, e in tr], local_sem=T.sem.sent), rr, [], 0.3, fin=False)
-                sent[0] += len(eng)
-                op(None, None, [], ww, 0.0, sem=(sb_, len(eng)), lat=COMM, soft=[i])
+            if SSP:
+                mm(acc(u0, [(rows(25, 3), T.ct[0:3, 0:NW]), (wf(1), nf, 1), (wf(0), S("pp"), 1)], NW), [kn, K("pp"), "CS", "ones", "wf0", "wf1"], [ku0])
             else:
-                act(sa, zo, AF.Identity, 0.0, 8192.0, [kzo], [ksa], NW)
-                tt(S("yts"), sa, no, A.add, [ksa, kno], [K("yts")], NW)
+                act(u0, nf, AF.Identity, col(4), 33.0, [kn, "c4"], [ku0], NW)
+                tt(u0, u0, S("pp"), A.add, [ku0, K("pp")], [ku0], NW)
+            act(S("yq"), T.st[:].indirect(cu), AF.Abs, 0.0, 2.0 ** -21, ["st", K("cu")], [K("yq")], NW, GR)
+            act(S("wg"), T.st[:].indirect(cu), AF.Copy, 0.0, 1.0, ["st", K("cu")], [K("wg")], NW, GR)
+            mm(acc(dy, [(wt("nI"), xn), (wt("I"), S("yq"))], NW), [kxn, K("yq"), "nI", "I"], [kdy])
+            act(S("ad"), dy, AF.Abs, -Y0, 1.0, [kdy], [K("ad")], NW)
+            mm(acc(sn, [(wt("BOn"), ct(5)), (wt("BOn"), S("ad"))], NW), [K("ad"), "BOn", "cT"], [ksn])
+            tt(S("aa"), sn, S("wg"), A.min, [ksn, K("wg")], [K("aa")], NW)
+            act(fo, sn, AF.Sign, 0.0, 1.0, [ksn], [kfo], NW)
+            if t < 3:
+                send(0, t, c, T.lx[:, x2 + 512:x2 + 512 + 2 * NW], T.xs[:, x2:x2 + 2 * NW], [kxn, kfo], [("lx", t + 1, c)])
+            tt(S("m0"), u0, S("aa"), A.max, [ku0, K("aa")], [K("m0")], NW)
+            tt(S("mi"), wq, S("m0"), A.max, [kwq, K("m0")], [K("mi")], NW)
+            ts(S("fi"), S("mi"), 8191 * 32, None, A.bitwise_and, None, [K("mi")], [K("fi")], NW)
+            zo, uo = T.zs[:, s4], T.us[:, s4]; kzo, kuo = ("zs", t, c), ("us", t, c)
+            n4 = (t + 1) * 256 + w0
+            if t < 3:
+                ts(uo, S("fi"), 1.0 / 32, None, A.mult, None, [K("fi")], [kuo], NW)
+                send(1, t, c, T.lu[:, n4:n4 + NW], uo, [kuo], [("lu", t + 1, c)])
+            ka, kka = pt(BA, 1); sg, ksg = pt(BA, 2); zp, kzp = pt(BA, 3)
+            tt(ka, wq, nf, A.min, [kwq, kn], [kka], NW)
+            tt(zo, ka, S("fi"), A.is_equal, [kka, K("fi")], [kzo], NW)
+            if t < 3:
+                send(2, t, c, T.lz[:, n4:n4 + NW], zo, [kzo], [("lz", t + 1, c)])
+            else:
+                ts(S("yn"), S("fi"), 1.0 / 32, None, A.mult, None, [K("fi")], [K("yn")], NW)
+                mm(acc(zp, [(wt("I8192"), zo)], NW), [kzo, "I8192"], [kzp])
+                tt(S("yts"), zp, S("yn"), A.add, [kzp, K("yn")], [K("yts")], NW)
                 dma("sp", T.yt[:, sl], S("yts"), [K("yts")], [], 0.3)
                 dma("sp", T.yx[:, sl], xn, [kxn], [], 0.3)
-            stage[0] = (t + 1) * C
-            act(S("kb"), ka, AF.Relu, 1.0, 1.0, [kka], [K("kb")], NW)
-            act(sd, S("zz"), AF.Abs, 1.0, 1.0, [K("zz")], [ksd], NW)
-            tt(sb, sd, S("kb"), A.min, [ksd, K("kb")], [ksb], NW)
-            tt(S("kk"), sb, zo, A.mult, [ksb, kzo], [K("kk")], NW)
-            mm(acc(dy, [(wt("nI"), xn), (wt("I16"), S("yq")), (wt("I32"), fo)], NW), [kxn, K("yq"), kfo, "nI", "I16", "I32"], [kdy])
-            act(S("hd"), dy, AF.Relu, -8.5, 1.0, [kdy], [K("hd")], NW)
-            mm(acc(u0, [(wt("I16th"), xn), (wt("nI"), fo), (wt("I16th"), S("hd"))], NW), [kxn, kfo, K("hd"), "I16th", "nI"], [ku0])
-            act(S("y16"), u0, AF.Identity, -23.5 / 16, 1.0, [ku0], [K("y16")], NW)
+            stage[0] = ENT + STP * t
+            ts(T.cdh[:, dsl], T.cd[:, dsl], 1.0, None, A.add, None, [K("cd")], [K("cdh")], ND)
+            if SEA:
+                act(S("se"), S("wg"), AF.Sign, 0.0, 1.0, [K("wg")], [K("se")], NW)
+                mm(acc(sg, [(wt("I"), S("se")), (wt("nI"), fo), (wt("I4"), zo)], NW), [K("se"), kfo, kzo, "I", "nI", "I4"], [ksg])
+            else:
+                mm(acc(sg, [(wf(2), S("wg"), 1), (wt("nI"), fo), (wt("I4"), zo)], NW), [K("wg"), kfo, kzo, "wf2", "nI", "I4"], [ksg])
+            act(S("sg"), sg, AF.Sign, -3.0, 1.0, [ksg], [K("sg")], NW)
+            mm(acc(dy, [(wt("nI"), xn), (wt("I"), S("yq")), (wt("I32"), fo)], NW), [kxn, K("yq"), kfo, "nI", "I", "I32"], [kdy])
+            act(S("hd"), dy, AF.Relu, -Y0, 1.0, [kdy], [K("hd")], NW)
+            terms = [(wt("I21"), xn), (wt("In25"), fo), (wt("I21"), S("hd"))]
+            if VP:
+                mm(acc(v2, terms + [(wf(0), nf, 1)], NW), [kxn, kfo, K("hd"), kn, "I21", "In25", "wf0"], [kv2])
+                act(S("vv"), v2, AF.Identity, (Y0 - 16) * 2 ** 21, 1.0, [kv2], [K("vv")], NW)
+            else:
+                mm(acc(v2, terms + [(wt("I21"), ct(1))], NW), [kxn, kfo, K("hd"), "I21", "In25", "c176"], [kv2])
+                tt(S("vv"), v2, nf, A.add, [kv2, kn], [K("vv")], NW)
         for cs in ([[c] for c in range(C)] if t >= SPLIT else [list(range(C))]):
             al = lambda s: [(s, c) for c in cs]
             a, n = sum(NWS[:cs[0]]) // 16, sum(NWS[c] for c in cs) // 16; ws = slice(16 * a, 16 * (a + n))
             if t >= SPLIT:
-                stage[0] = t * C + cs[0] + 1
-            ts(T.cb[:, ws], T.cb0[:, ws], 6, 1023, A.logical_shift_right, A.bitwise_and, al("cb0"), al("cb"), 16 * n)
-            tt(T.eq[:, ws], T.cd[:, 0:a + n].indirect(T.bco[:, a:a + n]), T.cb[:, ws], A.is_equal,
-               [("cd", c) for c in range(cs[-1] + 1)] + ["bco"] + al("cb"), al("eq"), 16 * n, GR)
-            lo, klo = T.pb3[:, 384 + a:384 + a + n], ("P", 3, "lo", cs[0])
-            mm(acc(lo, [(T.dm[:, r * 128:r * 128 + 128], T.eq[:, 16 * a + r:16 * (a + n):16]) for r in range(1, 16)], n),
-               al("eq") + ["dm%d" % r for r in range(1, 16)] + [("P", 3, 3)], [klo])
-            tt(T.of0[:, a:a + n], lo, T.cd[:, a:a + n], A.max, [klo] + al("cd"), al("of0"), n)
-            ts(T.off[:, 2 * a:2 * (a + n):2], T.of0[:, a:a + n], col(6), None, A.min, None, al("of0") + ["c6"], al("off"), n)
+                stage[0] = OFF * cs[0] + STP * t
+            b = 3 if TA == 16 else 2; pb = T["pb%d" % b]
+            mm([(pb[:, r:16 * n:16], dm(r), T.cdh[:, a:a + n], True, True, n) for r in range(16)], al("cdh") + ["dm%d" % r for r in range(16)], allp(b))
+            ts(T.eq[:, ws], pb[:, 0:16 * n], 0.0, None, A.is_equal, None, allp(b), al("eq"), 16 * n)
+            lo = pb[:, 0:n]
+            mm(acc(lo, [(dm(0), T.cdh[:, a:a + n])] + [(wt("I2048"), T.eq[:, 16 * a + r:16 * (a + n):16]) for r in range(1, 16)], n),
+               al("eq") + al("cdh") + ["dm0", "I2048"], allp(b))
+            ts(T.off[:, 2 * a:2 * (a + n):2], lo, -1.0, col(6), A.add, A.min, allp(b) + ["c6"], al("off"), n)
         for b in range(16):
             c = max(j for j in range(C) if sum(NWS[:j]) <= 16 * b)
-            tt(T.st[:].indirect(T.off[:, 2 * b:2 * b + 1]), T.kk[:, 16 * b:16 * b + 16], T.y16[:, 16 * b:16 * b + 16], A.add,
-               [("off", c), ("kk", c), ("y16", c)], ["st"], 16, SC)
-    for h, s in ((0, "a"), (1, "b")):
-        hs = slice(h * 512, h * 512 + 512); pb = T["pb%d" % h][:]; kp = ("P", h, "s")
-        ts(pb, T.st[:, hs], MAGIC, MAGIC + 1, A.add, A.subtract, ["st"], [kp], 512)
-        tt(T.w2[:, hs], pb, T.st[:, hs], A.subtract, [kp, "st"], ["w2" + s], 512)
-        act(T.w1[:, hs], pb, AF.Identity, 0.0, -8192.0, [kp], ["w1" + s], 512)
-        act(T.yo[:, hs], T.w2[:, hs], AF.Identity, -8.5, -16.0, ["w2" + s], ["yo" + s], 512)
-        tt(T.w1[:, hs], pb, T.w1[:, hs], A.max, [kp, "w1" + s], ["w1" + s], 512)
-        dma("sp", T.yk[:, hs], T.w1[:, hs], ["w1" + s], [], 0.8)
-        dma("act", T.yy[:, hs], T.yo[:, hs], ["yo" + s], [], 0.4)
+            tt(T.st[:].indirect(T.off[:, 2 * b:2 * b + 1]), T.vv[:, 16 * b:16 * b + 16], T.sg[:, 16 * b:16 * b + 16], A.mult,
+               [("off", c), ("vv", c), ("sg", c)], ["st"], 16, SC)
+    for h in range(4):
+        hs = slice(h * 256, h * 256 + 256); k = lambda s: (s, "o", h)
+        ts(T.wi[:, hs], T.st[:, hs], 2.0 ** 18, None, A.max, None, ["st"], [k("wi")], 256)
+        ts(T.wj[:, hs], T.wi[:, hs], 5, 16383, A.logical_shift_right, A.bitwise_and, [k("wi")], [k("wj")], 256)
+        cp(T.w1[:, hs], T.wj[:, hs], [k("wj")], [k("w1"), "w1" + "ab"[h // 2]], 256)
+        act(T.ys[:, hs], T.st[:, hs], AF.Abs, 0.0, 2.0 ** -21, ["st"], [k("ys"), "ys" + "ab"[h // 2]], 256)
+        act(T.yo[:, hs], T.ys[:, hs], AF.Identity, -Y0, 1.0, [k("ys")], [k("yo")], 256)
+        dma("sp", T.yk[:, hs], T.w1[:, hs], [k("w1")], [], 0.4)
+        if h % 2:
+            h2 = slice(h * 256 - 256, h * 256 + 256)
+            dma("act", T.yy[:, h2], T.yo[:, h2], [k("yo"), ("yo", "o", h - 1)], [], 0.4)
     return ops, sent[0]
 
 

@@ -1,119 +1,74 @@
+import math
 import numpy as np
 from concourse.bass import DstId, RemoteDMATransfer
 from concourse.mybir import AluOpType as A, ActivationFunctionType as AF
 
 NWS = [128, 128]
-C = len(NWS)
+CMAX = 4
 REP = 2
-KA = 12
+REPG = 1
+KA = 0
+TA = 8
 DERD = 8
 GD = 0
 G0 = 8
-GS = 4
-ES = 2
+GS, ES = 4, 2
 GSD, ESD = 1, 1
-TA = 16
-MIX = True
-TG, TW, WQB = True, True, None
-ROUNDS = 6
-GB, TB = (0, 1), (0, 1)
-OFF, STP, ENT = 3.0, 6.0, 6.0
 EGA = False
 FALLA = False
-SSP = True
+SSP = False
 VP = True
-SEA = False
+SEA = True
+AAP = False
+KAP = False
+TG, TW = True, True
+F3, HG, LED, WQB = False, 1, False, None
 SPLIT = 3
-INORDER = False
+BANKS = "chunk"
+GB, TB, KB, THB, DB = (0, 1), (0, 1), 2, 3, 2
 CY, PC, FV, FA, FP, LAT, LSELF, GR, SC = 0.83e-3, 0.42e-3, 0.05, 0.065, 0.005, 0.12, 0.06, 1.56, 3.8
-COMM, WIN, STG, TAB = 3.0, 0.15, 3.0, 6.0
-TA, KA, DERD, GD, SSP, SEA = 8, 0, 8, 0, False, True
+COMM, TAB, ROUNDS = 3.0, 6.0, 6
+OFF, STP, ENT = 3.0, 6.0, 6.0
+MOVES, HEAT, SEED, KEPT = 40000, 0.2, 1, {}
+REPG, HG, LED, ESD, ES, REP, HW = 4, 2, True, 1, 2, 4, 1
 U = 80.0 * 2 ** 18
 Y0 = 192.0
 HB = 2033
+PLACES = {
+    "chunk": dict(cn=("A", 0), xp=("S", 2), mp=("A", 1), pr=("A", 2), ix=("A", 1), dl=("S", 2), ds=("A", 1), d0=("A", 2), au=("A", 3), wq=("A", 0), xa=("S", 0),
+                  ka=("A", 1), zp=("A", 3), u0=("S", 0), ud=("S", 3), v2=("S", 1), dy=("S", 2), sn=("S", 3), ap=("S", 2), sg=("A", 2), d2=("S", 2), vv=("S", 1)),
+    "phase": dict(cn=(4, 0), xp=(3, 2), mp=(5, 0), pr=(5, 1), ix=(5, 2), dl=(5, 3), ds=(5, 0), d0=(5, 1), au=(5, 2), wq=(6, 0),
+                  ka=(6, 1), zp=(6, 2), u0=(7, 0), ud=(7, 3), v2=(7, 1), dy=(7, 2), sn=(7, 3), ap=(7, 2), sg=(3, 0), d2=(3, 1), vv=(3, 0)),
+}
 
 BF, F32, I32, U16, F16 = "bfloat16", "float32", "int32", "uint16", "float16"
 SCRATCH = {
-    "ftab": ("sbuf", [128, 8192], BF), "fg": ("sbuf", [128, 4096 + 16 * C], BF), "eg": ("sbuf", [128, 256, 16], BF),
+    "ftab": ("sbuf", [128, 8192], BF), "eg": ("sbuf", [128, 4096 + 16 * CMAX], BF), "fg": ("sbuf", [128, 4096 + 16 * CMAX], BF),
     "zg": ("sbuf", [128, 4096], BF), "ta": ("sbuf", [128, 4096], BF), "tb": ("sbuf", [128, 4096], BF),
     "st": ("sbuf", [128, 1040], F32), "kin": ("sbuf", [128, 1024], I32), "yin": ("sbuf", [128, 1024], BF),
     "w1": ("sbuf", [128, 1024], F32), "wi": ("sbuf", [128, 1024], I32), "wj": ("sbuf", [128, 1024], I32),
-    "yo": ("sbuf", [128, 1024], BF), "ys": ("sbuf", [128, 1024], BF),
+    "yo": ("sbuf", [128, 1024], BF), "ys": ("sbuf", [128, 1024], BF), "one": ("sbuf", [128, 512], BF),
     "tin": ("sbuf", [128, 256], I32), "tnm": ("sbuf", [128, 256], I32), "xin": ("sbuf", [128, 256], BF),
     "din": ("sbuf", [128, 8], I32), "hin": ("sbuf", [128, 8], I32), "thin": ("sbuf", [128, 8], I32),
     "xs": ("sbuf", [128, 4 * 512], BF), "us": ("sbuf", [128, 4 * 256], U16), "zs": ("sbuf", [128, 4 * 256], BF),
     "lx": ("sbuf", [128, 4 * 512], BF), "lu": ("sbuf", [128, 4 * 256], U16), "lz": ("sbuf", [128, 4 * 256], BF),
-    "ci": ("sbuf", [128, 256], I32), "cj": ("sbuf", [128, 512], I32), "cf": ("sbuf", [128, 160], F32), "col": ("sbuf", [128, 48], F32),
-    "coli": ("sbuf", [128, 8], I32), "dm": ("sbuf", [128, 17 * 128], F16), "sw": ("sbuf", [128, 6 * 144], BF), "swi": ("sbuf", [128, 144], F16),
-    "wt": ("sbuf", [128, 30 * 128], BF), "tr": ("sbuf", [128, 128 * C], BF), "wf": ("sbuf", [128, 4 * 128], F32),
+    "cj": ("sbuf", [128, 512], F32), "cf": ("sbuf", [128, 160], F32), "col": ("sbuf", [128, 48], F32),
+    "coli": ("sbuf", [128, 8], I32), "dm": ("sbuf", [128, 16 * 128], F16), "sw": ("sbuf", [128, 6 * 144], BF), "swi": ("sbuf", [128, 144], F16),
+    "wt": ("sbuf", [128, 36 * 128], BF), "tr": ("sbuf", [128, 128 * CMAX], BF), "wf": ("sbuf", [128, 4 * 128], F32),
     "ct": ("sbuf", [128, 12 * 128], BF), "iu": ("sbuf", [128, 32], U16), "cu": ("sbuf", [128, 32], U16),
     "cd": ("sbuf", [128, 16], I32), "cd0": ("sbuf", [128, 16], I32), "cdh": ("sbuf", [128, 16], F16), "off": ("sbuf", [128, 32], U16),
     "go": ("sbuf", [128, 256], F16),
 }
-for _n in ("cand", "r2", "fall", "ee", "za", "zc", "le", "qq", "hi", "yq", "ad", "hd", "eq", "se"):
+for _n in ("cand", "r2", "fall", "ee", "za", "zc", "le", "qq", "hi", "yq", "ad", "hd", "eq", "se", "sa"):
     SCRATCH[_n] = ("sbuf", [128, 256], BF)
-for _n in ("nf", "pp", "wg", "aa", "m0", "sg", "vv", "yn", "yts"):
+for _n in ("nf", "pp", "ss", "wg", "aa", "m0", "sg", "vv", "yn", "yts"):
     SCRATCH[_n] = ("sbuf", [128, 256], F32)
 for _n in ("mi", "fi"):
     SCRATCH[_n] = ("sbuf", [128, 256], I32)
 for _b in range(8):
     SCRATCH["pb%d" % _b] = ("psum", [128, 512], F32)
-SEMAPHORES = ["pe", "dve", "act", "pool", "sent"] + ["d%d" % i for i in range(24)] + \
-    ["a%d_%d_%d" % (k, t, c) for k in range(3) for t in range(1, 4) for c in range(C)]
-
-
-def plan(ops):
-    n = len(ops)
-    succ = [[] for _ in range(n)]
-    for i, o in enumerate(ops):
-        for d in o["deps"] | o["soft"]:
-            succ[d].append(i)
-    pr = [0.0] * n
-    for i in range(n - 1, -1, -1):
-        o = ops[i]
-        pr[i] = o["dur"] + o["lat"] + max([pr[j] + LAT for j in succ[i]] + [0.0]) + o["bias"]
-    left = [len(o["deps"] | o["soft"]) for o in ops]
-    ready = [i for i in range(n) if left[i] == 0]
-    fin = [0.0] * n; free = {}; bank = {}; lock = {}; order = []
-    while ready:
-        cands = []
-        for i in ready:
-            o = ops[i]
-            if o["grp"] is not None and lock.get(o["grp"][0], o["grp"][1]) != o["grp"][1]:
-                continue
-            t = free.get(o["eng"], 0.0)
-            for d in o["deps"] | o["soft"]:
-                t = max(t, fin[d] + (-ops[d]["lat"] if d in o["chain"] else LSELF if ops[d]["eng"] == o["eng"] else LAT))
-            for b in o["banks"]:
-                for e, j in bank.get(b, {}).items():
-                    if e != o["eng"]:
-                        t = max(t, fin[j] + LAT)
-            cands.append((t, i))
-        t0, i0 = min(cands)
-        e0 = ops[i0]["eng"]
-        t, i = max([(tt, ii) for tt, ii in cands if ops[ii]["eng"] == e0 and tt <= t0 + WIN], key=lambda z: pr[z[1]] - ops[z[1]]["stage"])
-        o = ops[i]
-        for b in o["banks"]:
-            for e, j in bank.get(b, {}).items():
-                if e != o["eng"]:
-                    o["deps"].add(j)
-            bank.setdefault(b, {})[o["eng"]] = i
-        if o["grp"] is not None:
-            if o["grp"][2]:
-                lock.pop(o["grp"][0], None)
-            else:
-                lock[o["grp"][0]] = o["grp"][1]
-        if o["eng"] is not None:
-            free[o["eng"]] = t + o["dur"]
-        o["t"] = t
-        fin[i] = t + o["dur"] + o["lat"]
-        order.append(i); ready.remove(i)
-        for j in succ[i]:
-            left[j] -= 1
-            if left[j] == 0:
-                ready.append(j)
-    assert len(order) == n
-    return order, max(fin)
+SEMAPHORES = ["pe", "dve", "act", "pool", "sent"] + ["d%d" % i for i in range(28)] + \
+    ["a%d_%d_%d" % (k, t, c) for k in range(3) for t in range(1, 4) for c in range(CMAX)]
 
 
 def place(ops, before, key):
@@ -151,6 +106,83 @@ def place(ops, before, key):
     return start
 
 
+def tighten(ops, before, order):
+    n = len(ops); E = {"pe": 0, "dve": 1, "act": 2, "pool": 3, "sp": 4, None: 5}
+    eng = [E[o["eng"]] for o in ops]; dur = [o["dur"] for o in ops]; lat = [o["lat"] for o in ops]; bk = [o["banks"] for o in ops]
+    fw = [[(d, w + dur[d]) for d, w in b] for b in before]; gap = LAT + 0.05
+    pre = [set(d for d, _ in f) for f in fw]; suc = [set() for _ in range(n)]
+    for i in range(n):
+        for d in pre[i]:
+            suc[d].add(i)
+
+    def times(pi):
+        s = [0.0] * n; why = [-1] * n; res = [False] * n
+        fe = [0.0] * 6; le = [-1] * 6; bt = [[-9.0] * 3 for _ in range(8)]; bo = [[-1] * 3 for _ in range(8)]
+        end = 0.0; last = -1
+        for i in pi:
+            t = 0.0; y = -1; r = False
+            for d, w in fw[i]:
+                v = s[d] + w
+                if v > t:
+                    t = v; y = d
+            e = eng[i]
+            if e != 5:
+                if fe[e] > t + 1e-9:
+                    t = fe[e]; y = le[e]; r = True
+                for b in bk[i]:
+                    for f in range(3):
+                        if f != e and bt[b][f] > t + 1e-9:
+                            t = bt[b][f]; y = bo[b][f]; r = True
+                x = t + dur[i]; fe[e] = x; le[e] = i
+                for b in bk[i]:
+                    bt[b][e] = x + gap; bo[b][e] = i
+            s[i] = t; why[i] = y; res[i] = r
+            v = t + dur[i] + lat[i]
+            if v > end:
+                end = v; last = i
+        return end, s, why, res, last
+    z = [SEED]
+
+    def rnd():
+        z[0] = (z[0] * 1103515245 + 12345) % 2147483648
+        return z[0] / 2147483648.0
+    pi = list(order); cur = times(pi); best = cur
+    for it in range(MOVES):
+        _, s, why, res, i = cur; pairs = []
+        while i >= 0:
+            if res[i] and why[i] not in pre[i]:
+                pairs.append((why[i], i))
+            i = why[i]
+        v, u = pairs[int(rnd() * len(pairs))]; a, b = pi.index(v), pi.index(u)
+        far = int(rnd() * 12) if rnd() < 0.3 else 0; mv = []; rest = []
+        if rnd() < 0.5:
+            a = max(0, a - far); need = {u}
+            for x in reversed(pi[a:b + 1]):
+                if x in need:
+                    mv.append(x); need |= pre[x]
+                else:
+                    rest.append(x)
+            new = pi[:a] + mv[::-1] + rest[::-1] + pi[b + 1:]
+        else:
+            b = min(n - 1, b + far); need = {v}
+            for x in pi[a:b + 1]:
+                if x in need:
+                    mv.append(x); need |= suc[x]
+                else:
+                    rest.append(x)
+            new = pi[:a] + rest + mv + pi[b + 1:]
+        if u in mv and v in mv:
+            continue
+        c = times(new)
+        if c[0] - cur[0] <= -HEAT * (0.1 ** (it / MOVES)) * math.log(1.0 - rnd()):
+            pi, cur = new, c
+            if it % 32 == 0:
+                pi.sort(key=lambda x: c[1][x]); cur = times(pi)
+            if cur[0] < best[0]:
+                best = cur
+    return sorted(range(n), key=lambda i: (best[1][i], i)), best[1]
+
+
 def plan(ops):
     n = len(ops); fw = [[] for _ in range(n)]; bw = [[] for _ in range(n)]
     for i, o in enumerate(ops):
@@ -170,7 +202,9 @@ def plan(ops):
             best = s
         r = place(ops + [tail], [b or [(n, ops[i]["lat"])] for i, b in enumerate(bw)] + [[]], [-s[i] - ops[i]["dur"] for i in range(n)] + [0.0])
         key = [-r[i] - ops[i]["dur"] for i in range(n)]
-    order = sorted(range(n), key=lambda i: (best[i], i)); bank = {}
+    if KEPT.get("n") != n:
+        KEPT["n"] = n; KEPT["plan"] = tighten(ops, fw, sorted(range(n), key=lambda i: (best[i], i)))
+    order, best = KEPT["plan"]; bank = {}
     for i in order:
         o = ops[i]; o["t"] = best[i]
         for b in o["banks"]:
@@ -235,29 +269,33 @@ def emit(g, T, ops, order):
 
 
 def build(T, dst, eng):
-    ops = []; lw = {}; rd = {}; nd = [0]; sent = [0]; stage = [0]; sums_in = {}
+    ops = []; lw = {}; rd = {}; nd = [0]; sent = [0]; stage = [0]; sums_in = {}; part = ["c", 0, 0]
+    C = len(NWS)
 
-    def op(e, fn, r, w, dur, banks=(), grp=None, sem=None, lat=0.0, soft=(), bias=0.0, fin=True):
-        i = len(ops); raw = set(); other = set(); chain = set()
+    def op(e, fn, r, w, dur, banks=(), sem=None, lat=0.0, soft=(), fin=True):
+        i = len(ops); deps = set(); chain = set()
         for k in r:
             if k in lw:
-                raw.add(lw[k])
+                deps.add(lw[k])
         for k in w:
             if k in lw:
-                other.add(lw[k])
+                deps.add(lw[k])
                 if e == "pe" and ops[lw[k]]["eng"] == "pe":
                     chain.add(lw[k])
-            other |= set(rd.get(k, []))
-        if INORDER and e in ("dve", "act") and sem is None:
-            chain |= set(d for d in other - raw - set(lw.get(k) for k in w) if ops[d]["eng"] == e and ops[d]["sem"] is None)
+            deps |= set(rd.get(k, []))
         for k in r:
             rd.setdefault(k, []).append(i)
         for k in w:
             lw[k] = i; rd[k] = []
-        deps = raw | other
         deps.discard(i)
-        ops.append(dict(eng=e, fn=fn, deps=deps, chain=chain, soft=set(soft), dur=dur, banks=tuple(banks), grp=grp, sem=sem,
-                        lat=lat, bias=bias, fin=fin, stage=stage[0], tag=str(e) + str(w[0] if w else r[0])))
+        k = w[0] if w else r[0]
+        if part[0] == "c" or (isinstance(k, str) and k != "st"):
+            kind = ("c", i); half = 0
+        else:
+            nm = "%s:%s" % (e, k if k == "st" else k[0] if k[0] != "P" else "P%s%d" % ("AASS"[k[1] - 4] if k[1] >= 4 else k[1], k[2]))
+            part[1][nm] = part[1].get(nm, -1) + 1; kind = (part[0], nm, part[1][nm]); half = part[2]
+        ops.append(dict(eng=e, fn=fn, deps=deps, chain=chain, soft=set(soft), dur=dur, banks=tuple(banks), sem=sem,
+                        lat=lat, fin=fin, stage=stage[0], kind=kind, half=half, tag=str(e) + str(w[0] if w else r[0])))
         return i
 
     def bk(keys):
@@ -267,42 +305,42 @@ def build(T, dst, eng):
         s = "d%d" % nd[0]; nd[0] += 1
         return op(q, lambda h: h.dma_start(out, in_), r, w, 0.05, sem=(s, 16), lat=2.0 + us)
 
-    def ts(out, in0, s1, s2, o0, o1, r, w, n, rate=1.0, **kw):
+    def ts(out, in0, s1, s2, o0, o1, r, w, n, rate=1.0):
         if o1 is None:
             f = lambda h: h.tensor_scalar(out, in0, s1, None, o0)
         else:
             f = lambda h: h.tensor_scalar(out, in0, s1, s2, o0, o1)
-        return op("dve", f, r, w, FV + CY * max(64, n * rate), bk(r + w), **kw)
+        return op("dve", f, r, w, FV + CY * max(64, n * rate), bk(r + w))
 
-    def tt(out, in0, in1, o, r, w, n, rate=1.0, **kw):
-        return op("dve", lambda h: h.tensor_tensor(out, in0, in1, o), r, w, FV + CY * max(64, n * rate), bk(r + w), **kw)
+    def tt(out, in0, in1, o, r, w, n, rate=1.0):
+        return op("dve", lambda h: h.tensor_tensor(out, in0, in1, o), r, w, FV + CY * max(64, n * rate), bk(r + w))
 
-    def cp(out, in_, r, w, n, rate=1.0, **kw):
-        return op("dve", lambda h: h.tensor_copy(out, in_), r, w, FV + CY * max(64, n * rate), bk(r + w), **kw)
+    def cp(out, in_, r, w, n, rate=1.0):
+        return op("dve", lambda h: h.tensor_copy(out, in_), r, w, FV + CY * max(64, n * rate), bk(r + w))
 
-    def ms(ap, v, w, r=()):
-        return op("dve", lambda h: h.memset(ap, v), list(r), w, FV + 0.06)
+    def ms(ap, v, w, n=64):
+        return op("dve", lambda h: h.memset(ap, v), [], w, FV + CY * max(64, n))
 
-    def act(out, in_, f, bias, scale, r, w, n, rate=1.0, **kw):
+    def act(out, in_, f, bias, scale, r, w, n, rate=1.0):
         if f == AF.Copy:
             fn = lambda h: h.activation(out, in_, f)
         else:
             fn = lambda h: h.activation(out, in_, f, bias=bias, scale=scale)
-        return op("act", fn, r, w, FA + CY * max(64, n * rate), bk(r + w), **kw)
+        return op("act", fn, r, w, FA + CY * max(64, n * rate), bk(r + w))
 
-    def mm(items, r, w, grp=None, **kw):
+    def mm(items, r, w, grp=None):
         def f(h):
             for it in items:
                 ins = h.matmul(it[0], it[1], it[2], it[3], it[4])
             return ins
-        i = op("pe", f, r, w, sum(FP + PC * max(64, it[5]) for it in items), bk(w), lat=0.05, **kw)
-        b = w[0][1]; z = sums_in.setdefault(b, dict(open=None, shut=[], ones=[])); first = []
+        i = op("pe", f, r, w, sum(FP + PC * max(64, it[5]) for it in items), bk(w), lat=0.05)
+        z = sums_in.setdefault(w[0][1], dict(open=None, shut=[], ones=[])); first = []
         if grp is None:
             assert z["open"] is None
             first = z["shut"]; z["ones"].append(i)
         elif z["open"] is None:
-            first = z["shut"] + z["ones"]; z["open"] = grp[1]; z["ones"] = []
-        if grp is not None and grp[2]:
+            first = z["shut"] + z["ones"]; z["open"] = grp[0]; z["ones"] = []
+        if grp is not None and grp[1]:
             z["open"] = None; z["shut"] = [i]
         ops[i]["chain"] |= set(first) - ops[i]["deps"]; ops[i]["deps"] |= set(first)
         return i
@@ -310,13 +348,15 @@ def build(T, dst, eng):
     def acc(out, terms, n):
         return [(out, z[0], z[1], j == 0, j == len(terms) - 1, max(64, n) * (4 if len(z) > 2 else 1)) for j, z in enumerate(terms)]
 
-    def iota(out, pat, base, cm, w):
-        return op("pool", lambda h: h.iota(out, pat, base, cm), [], w, 0.13 + 2 * CY * int(np.prod([p[1] for p in pat])))
+    def run(groups, w, name):
+        for j, (it, r) in enumerate(groups):
+            e = j == len(groups) - 1
+            mm([(o, a, b, j == 0 and i == 0, e and i == len(it) - 1, n) for i, (o, a, b, n) in enumerate(it)], r, w, (name, e))
 
-    NW = 128; ND = 8
+    def iota(out, pat, base, cm, w, flag=True):
+        f = (lambda h: h.iota(out, pat, base, cm, allow_small_or_imprecise_dtypes=True)) if flag else (lambda h: h.iota(out, pat, base, cm))
+        return op("pool", f, [], w, 0.13 + 2 * CY * int(np.prod([p[1] for p in pat])))
 
-    def pt(b, s, n=None):
-        return T["pb%d" % b][:, s * 128:s * 128 + (n or NW)], ("P", b, s)
     allp = lambda b: [("P", b, s) for s in range(4)]
 
     dma("sp", T.ftab[:], T.fx[:], [], ["ftab"], TAB)
@@ -329,88 +369,92 @@ def build(T, dst, eng):
     dma("sp", T.yin[:], T.y0[:], [], ["yin"], TAB + 2.3)
 
     col = lambda j: T.col[:, j:j + 1]
-    iota(T.coli[:, 0:1], [[1, 1]], 0, 1, ["p"])
-    iota(T.ci[:, 0:144], [[1, 144]], 0, 0, ["ci"])
-    iota(T.cj[:, 0:NW], [[0, NW // 4], [2, 4]], -64, 0, ["cj"])
-    iota(T.cj[:, 128:128 + ND], [[256, ND]], 0, 0, ["cj2"])
+    lin = lambda j, a, b: act(col(j), col(1), AF.Identity, b, a, ["c1"], ["c%d" % j], 1)
+    iota(T.coli[:, 0:1], [[1, 1]], 0, 1, ["p"], False)
+    iota(col(0), [[1, 1]], 0, 1, ["c0"])
+    iota(T.cf[:, 0:144], [[1, 144]], 0, 0, ["cf"])
+    iota(T.cj[:, 0:128], [[0, 32], [2, 4]], -64, 0, ["cj"])
+    iota(T.cj[:, 128:136], [[256, 8]], 0, 0, ["cj2"])
     ts(T.coli[:, 1:2], T.coli[:, 0:1], 15, None, A.bitwise_and, None, ["p"], ["pk"], 1)
-    cp(col(0), T.coli[:, 0:1], ["p"], ["c0"], 1)
     cp(col(1), T.coli[:, 1:2], ["pk"], ["c1"], 1)
     tt(col(2), col(0), col(1), A.subtract, ["c0", "c1"], ["c2"], 1)
-    ts(col(3), col(2), 15.0, None, A.add, None, ["c2"], ["c3"], 1)
-    ts(col(4), col(1), 1184.0, -2.0 ** 24, A.mult, A.add, ["c1"], ["c4"], 1)
-    ts(col(5), col(1), 50.0, None, A.add, None, ["c1"], ["c5"], 1)
-    ts(col(6), col(1), 1024.0, None, A.add, None, ["c1"], ["c6"], 1)
-    ts(col(7), col(1), 16.0, None, A.mult, None, ["c1"], ["c7"], 1)
+    act(col(3), col(2), AF.Identity, 15.0, 1.0, ["c2"], ["c3"], 1)
+    for j, a, b in ((4, 1184.0, -2.0 ** 24), (5, 1.0, 50.0), (6, 1.0, 1024.0), (7, 16.0, 0.0), (18, 1.0, float(HB)), (24, -1.0, 0.0)):
+        lin(j, a, b)
+    ts(T.coli[:, 2:3], T.coli[:, 0:1], 3, None, A.bitwise_and, None, ["p"], ["pq"], 1)
     cp(col(8), T.hin[:, 0:1], ["hin"], ["c8"], 1)
-    ts(col(9), T.hin[:, 0:1], 1.0 / 16, None, A.mult, None, ["hin"], ["c9"], 1)
-    ts(T.col[:, 10:14], T.din[:, 0:4], -8.875 if FALLA else -16.875, None, A.add, None, ["din"], ["c10"], 4)
-    ts(col(14), col(1), 0.0, -1.0, A.is_equal, A.mult, ["c1"], ["c14"], 1)
-    tt(col(15), col(14), T.thin[:, 0:1], A.mult, ["c14", "thin"], ["c15"], 1)
+    act(col(9), col(8), AF.Identity, 0.0, 1.0 / 16, ["c8"], ["c9"], 1)
+    ts(col(23), T.coli[:, 2:3], TA / 4, -8.0, A.is_lt, A.mult, ["pq"], ["c23"], 1)
+    ts(T.col[:, 10:14], T.din[:, 0:4], -8.875 if FALLA else -16.875, col(23), A.add, A.add, ["din", "c23"], ["c10"], 4)
+    ts(col(14), T.thin[:, 0:1], -1.0, None, A.mult, None, ["thin"], ["c14"], 1)
+    ts(col(15), col(1), 0.0, col(14), A.is_equal, A.mult, ["c1", "c14"], ["c15"], 1)
     ts(col(16), col(1), 1.0, -0.5, A.is_equal, A.mult, ["c1"], ["c16"], 1)
-    tt(col(17), col(15), col(16), A.add, ["c15", "c16"], ["c17"], 1)
-    ts(col(18), col(1), float(HB), None, A.add, None, ["c1"], ["c18"], 1)
-    cp(T.cf[:, 0:144], T.ci[:, 0:144], ["ci"], ["cf"], 144)
-    sw = lambda j, k: T.sw[:, j * 144 + 15 - k:j * 144 + 143 - k]
-    swf = lambda j: T.sw[:, j * 144:j * 144 + 144]
-    ts(swf(0), T.cf[:, 0:144], col(3), None, A.is_equal, None, ["cf", "c3"], ["sw0"], 144)
-    for j, v in ((1, -16.0), (2, U), (3, -U), (4, -U / 2)):
-        act(swf(j), swf(0), AF.Identity, 0.0, v, ["sw0"], ["sw%d" % j], 144)
-    ts(T.swi[:], swf(0), col(18), None, A.mult, None, ["sw0", "c18"], ["swi"], 144, 0.5)
-    act(swf(5), swf(0), AF.Identity, 0.0, col(8), ["sw0", "c8"], ["sw5"], 144)
     wn = {}
 
     def wt(name):
         wn.setdefault(name, len(wn))
+        assert len(wn) <= 36
         return T.wt[:, wn[name] * 128:wn[name] * 128 + 128]
     wf = lambda j: T.wf[:, j * 128:j * 128 + 128]
     cm = T.cf[:, 0:128]
+    made = set()
+
+    def times(base, v):
+        name = "%s*%r" % (base, v)
+        if v == 1.0:
+            return wt(base), base
+        if name not in made:
+            made.add(name); keep = stage[0]; stage[0] = 0
+            act(wt(name), wt(base), AF.Identity, 0.0, v, [base], [name], 128); stage[0] = keep
+        return wt(name), name
     ts(wt("I"), cm, col(0), None, A.is_equal, None, ["cf", "c0"], ["I"], 128)
-    for name, v in (("nI", -1.0), ("I8", 8.0), ("I512", 512.0), ("IU", U), ("IU16", (8 if FALLA else 16) * U), ("IV16", 16 * U), ("In64", -64.0), ("I32", 32.0),
-                    ("I21", 2.0 ** 21), ("In25", -2.0 ** 25), ("I4", 4.0), ("I2048", 2048.0), ("I8192", 8192.0), ("I64", 64.0)):
-        act(wt(name), wt("I"), AF.Identity, 0.0, v, ["I"], [name], 128)
-    for j, v in ((0, 1.0), (1, 33.0), (2, 0.75 * 2.0 ** -28)):
-        act(wf(j), wt("I"), AF.Identity, 0.0, v, ["I"], ["wf%d" % j], 128)
+    for j, v, use in ((0, 1.0, True), (1, 33.0, SSP), (2, 0.75 * 2.0 ** -28, not SEA)):
+        if use:
+            act(wf(j), wt("I"), AF.Identity, 0.0, v, ["I"], ["wf%d" % j], 128)
     ts(wt("ge"), cm, col(2), None, A.is_ge, None, ["cf", "c2"], ["ge"], 128)
     ts(wt("le"), cm, col(3), None, A.is_le, None, ["cf", "c3"], ["lew"], 128)
     tt(wt("BO"), wt("ge"), wt("le"), A.mult, ["ge", "lew"], ["BO"], 128, 2)
-    act(wt("nBO"), wt("BO"), AF.Identity, 0.0, -1.0, ["BO"], ["nBO"], 128)
-    act(wt("BOn"), wt("BO"), AF.Identity, 0.0, -2.0 ** 30, ["BO"], ["BOn"], 128)
-    act(wt("BO16"), wt("BO"), AF.Identity, 0.0, -16.0, ["BO"], ["BO16"], 128)
-    act(wt("BOh"), wt("BO"), AF.Identity, 0.0, -0.5, ["BO"], ["BOh"], 128)
-    act(wt("I16"), wt("I"), AF.Identity, 0.0, 16.0, ["I"], ["I16"], 128)
-    bg = lambda name: T.wt[:, wn[name] * 128:wn[name] * 128 + 128:16]
     act(wt("H16"), wt("BO"), AF.Identity, 0.0, col(9), ["BO", "c9"], ["H16"], 128)
-    ts(wt("gt"), cm, col(0), -1.0, A.is_gt, A.mult, ["cf", "c0"], ["gt"], 128)
-    tt(wt("gt"), wt("gt"), wt("le"), A.mult, ["gt", "lew"], ["gt"], 128, 2)
-    tt(wt("TRI"), wt("gt"), wt("I64"), A.add, ["gt", "I64"], ["TRI"], 128, 2)
-    ts(wt("le"), cm, col(0), -1.0, A.is_lt, A.mult, ["cf", "c0", "TRI"], ["lew"], 128)
-    tt(wt("le"), wt("le"), wt("ge"), A.mult, ["ge", "lew"], ["lew"], 128, 2)
-    tt(wt("le"), wt("le"), wt("I"), A.add, ["I", "lew"], ["lew"], 128, 2)
-    assert len(wn) <= 27
-    rows = lambda j, n: T.wt[0:n, (j + 4) * 128:(j + 4) * 128 + 128]
-    for n, v in ((3, 1.0 / 32), (2, -32.0), (1, 10240.0)):
-        ms(rows(23, n), v, ["CW"])
-    if KA < 16:
-        ms(rows(24, 2), 7.5, ["CX"]); ms(rows(24, 1), 2304.0, ["CX"])
+    act(wt("sd"), cm, AF.Sign, col(0), -1.0, ["cf", "c0"], ["sd"], 128)
+    tt(wt("sb"), wt("sd"), wt("BO"), A.mult, ["sd", "BO"], ["sb"], 128, 2)
+    ts(wt("gt"), wt("sb"), 0.0, None, A.min, None, ["sb"], ["gt"], 64)
+    tt(wt("TRI"), wt("gt"), times("I", 64.0)[0], A.add, ["gt", "I*64.0"], ["TRI"], 128, 2)
+    ts(wt("ge"), wt("sb"), 0.0, -1.0, A.max, A.mult, ["sb", "BO"], ["ge"], 64)
+    tt(wt("le"), wt("ge"), wt("I"), A.add, ["I", "ge", "BO"], ["lew"], 128, 2)
+    sw = lambda j, k: T.sw[:, j * 144 + 15 - k:j * 144 + 143 - k]
+    swf = lambda j: T.sw[:, j * 144:j * 144 + 144]
+    ts(swf(0), T.cf[:, 0:144], col(3), None, A.is_equal, None, ["cf", "c3"], ["sw0"], 144)
+    for j, v, use in ((1, -16.0, not TG), (2, U, not TW), (3, -U, not TW), (4, -U / 2, not TW)):
+        if use:
+            act(swf(j), swf(0), AF.Identity, 0.0, v, ["sw0"], ["sw%d" % j], 144)
+    ts(T.swi[:], swf(0), col(18), None, A.mult, None, ["sw0", "c18"], ["swi"], 144, 0.5)
+    act(swf(5), swf(0), AF.Identity, 0.0, col(8), ["sw0", "c8"], ["sw5"], 144)
+
+    def rows(name, n):
+        wt(name)
+        return T.wt[0:n, wn[name] * 128:wn[name] * 128 + 128]
+    for name, vals in (("CW", (10240.0, -32.0, 1.0 / 32)), ("CX", (2304.0, 7.5)), ("CY", (Y0 * 2 ** 21,))):
+        for n in range(len(vals), 0, -1):
+            ms(rows(name, n), vals[n - 1], [name])
     if SSP:
         iota(T.cj[:, 256:384], [[0, 8], [1, 16]], 0, 0, ["cj3"])
         ts(col(19), col(0), 1.0, 1024.0, A.is_equal, A.mult, ["c0"], ["c19"], 1)
         ts(col(20), col(0), 2.0, 160.0, A.is_equal, A.mult, ["c0"], ["c20"], 1)
         tt(col(21), col(19), col(20), A.add, ["c19", "c20"], ["c21"], 1)
         ts(col(22), col(0), 0.0, -2.0 ** 24, A.is_equal, A.mult, ["c0"], ["c22"], 1)
-        ts(rows(25, 128), T.cj[:, 256:384], col(21), col(22), A.mult, A.add, ["cj3", "c21", "c22"], ["CS"], 128)
-    ct = lambda j, n=None: T.ct[:, j * 128:j * 128 + (n or NW)]
-    ms(ct(0, 128), 1.0, ["ones"]); ms(ct(1), Y0 - 16, ["c176"]); ms(ct(2), 144.0, ["c128"]); ms(ct(3), -1.0, ["neg"])
+        ts(rows("CS", 128), T.cj[:, 256:384], col(21), col(22), A.mult, A.add, ["cj3", "c21", "c22"], ["CS"], 128)
+    ct = lambda j, n: T.ct[:, j * 128:j * 128 + n]
+    ms(T.one[:], 1.0, ["ones"], 256); ms(ct(2, 128), 144.0, ["c128"]); ms(ct(3, 128), -1.0, ["neg"])
+    if not VP:
+        ms(ct(1, 128), Y0 - 16, ["c176"])
     for c in range(C):
-        b0 = 16 * sum(NWS[:c]) + 16 * c
-        ms(T.fg[:, b0:b0 + 16], 0.0, [("pad", c)])
-    ts(ct(4), T.cj[:, 0:NW], col(1), None, A.subtract, None, ["cj", "c1"], ["cP"], NW)
-    ts(ct(5), ct(0), col(17), None, A.mult, None, ["ones", "c17"], ["cT"], 64)
-    ts(col(23), col(1), float(TA), -8.0, A.is_lt, A.mult, ["c1"], ["c23"], 1)
+        b0 = sum(NWS[:c]) + c
+        ms(T.eg[:, 16 * b0:16 * b0 + 16], 144.0, [("pad", c)])
+    act(ct(4, 128), T.cj[:, 0:128], AF.Identity, col(24), 1.0, ["cj", "c24"], ["cP"], 128)
+    act(ct(5, 128), T.one[:, 0:128], AF.Identity, col(16), col(15), ["ones", "c15", "c16"], ["cT1"], 128)
     for t in range(4):
-        ts(ct(6 + t), ct(0), col(10 + t), col(23), A.mult, A.add, ["ones", "c10", "c23"], ["cD%d" % t], 64)
-    ts(ct(11, ND), T.cj[:, 128:128 + ND], col(7), None, A.add, None, ["cj2", "c7"], ["cI"], ND)
+        act(ct(6 + t, 128), T.one[:, 0:128], AF.Identity, 0.0, col(10 + t), ["ones", "c10"], ["cD%d" % t], 128)
+    act(ct(11, 8), T.cj[:, 128:136], AF.Identity, col(7), 1.0, ["cj2", "c7"], ["cI"], 8)
     ts(T.cf[:, 144:160], T.cf[:, 0:16], col(1), -1.0, A.is_equal, A.mult, ["cf", "c1"], ["dmc"], 16)
     dm = lambda r: T.dm[:, r * 128:r * 128 + 128]
     cp(dm(0), wt("I"), ["I"], ["dm0"], 64)
@@ -420,10 +464,10 @@ def build(T, dst, eng):
     ms(T.st[:, 1024:1040], 0.0, ["st"])
     for h, s, b in ((0, "a", 2), (1, "b", 3)):
         hs = slice(h * 512, h * 512 + 512)
-        ts(T.w1[:, hs], T.kin[:, hs], 32.0, Y0 * 2 ** 21, A.mult, A.add, ["kin"], ["w1" + s], 512)
-        act(T.ys[:, hs], T.w1[:, hs], AF.Sign, Y0 * 2 ** 21 + 2 ** 18 - 32, -1.0, ["w1" + s], ["ys" + s], 512)
-        act(T.ys[:, hs], T.ys[:, hs], AF.Sign, 0.5, 1.0, ["ys" + s], ["ys" + s], 512)
-        mm(acc(T["pb%d" % b][:], [(wf(0), T.w1[:, hs], 1), (wt("I21"), T.yin[:, hs])], 512), ["w1" + s, "yin", "wf0", "I21"], allp(b))
+        ts(T.w1[:, hs], T.kin[:, hs], 32.0, None, A.mult, None, ["kin"], ["w1" + s], 512)
+        act(T.ys[:, hs], T.w1[:, hs], AF.Sign, 2.0 ** 18 - 16, -1.0, ["w1" + s], ["ys" + s], 512)
+        w21, k21 = times("I", 2.0 ** 21)
+        mm(acc(T["pb%d" % b][:], [(wf(0), T.w1[:, hs], 1), (w21, T.yin[:, hs]), (rows("CY", 1), T.one[0:1, :])], 512), ["w1" + s, "yin", "wf0", k21, "CY", "ones"], allp(b))
         tt(T.st[:, hs], T["pb%d" % b][:], T.ys[:, hs], A.mult, allp(b) + ["ys" + s], ["st"], 512)
     stage[0] = 0
     ts(T.tnm[:], T.tin[:], 8191, None, A.bitwise_and, None, ["tin"], ["tnm"], 256)
@@ -438,19 +482,39 @@ def build(T, dst, eng):
         i = op("pool", lambda h: h.remote_dma(to, frm, T.sem[s], T.sem.sent, dst[1], dst[0], mask(eng)), r, [], 0.3, fin=False)
         sent[0] += len(eng)
         op(None, None, [], w, 0.0, sem=(s, len(eng)), lat=COMM, soft=[i])
-    stream = [0]
     G = 4
     for t in range(4):
         for c in range(C):
             NW = NWS[c]; ND = NW // 16
-            BA, BS = 4 + c % 2, 6 + c % 2
             w0 = sum(NWS[:c]); sl = slice(w0, w0 + NW); s4 = slice(t * 256 + w0, t * 256 + w0 + NW)
-            stage[0] = OFF * c + STP * t
+            stage[0] = OFF * c + STP * t; part[:] = ["w", {}, 2 * t + c]
             K = lambda s: (s, c)
             S = lambda s: T[s][:, sl]
+
+            def where(name):
+                b, s = PLACES[BANKS][name]
+                return {"A": 4 + c % 2, "S": 6 + c % 2}.get(b, b), s
+
+            def ps(name, n=NW):
+                b, s = where(name)
+                return T["pb%d" % b][:, s * 128:s * 128 + n], ("P", b, s)
+
+            def lsum(name, terms, n=NW):
+                o, ko = ps(name, n); it = []; r = []
+                for base, v, data, kd in terms:
+                    if data is None:
+                        r.append(kd); continue
+                    if isinstance(base, str):
+                        w, kw = times(base, v); it.append((w, data))
+                    else:
+                        w, kw = base, v; it.append((w, data, 1) if kw.startswith("wf") else (w, data))
+                    r += [kw, kd]
+                mm(acc(o, it, n), r, [ko])
+                return o, ko
+            ones = lambda n: T.one[0:n, 0:NW]
             x2 = t * 512 + 2 * w0
             if t == 0:
-                x, fl, kx, kf = T.xin[:, sl], ct(3), "xin", "neg"
+                x, fl, kx, kf = T.xin[:, sl], ct(3, NW), "xin", "neg"
             else:
                 x, fl, kx = T.lx[:, x2:x2 + NW], T.lx[:, x2 + NW:x2 + 2 * NW], ("lx", t, c); kf = kx
             nu, asl = T.lu[:, s4], T.lz[:, s4]
@@ -459,8 +523,12 @@ def build(T, dst, eng):
             ts(nf, nu, 32.0, None, A.mult, None, [ku], [kn], NW)
             xn, fo, kxn, kfo = T.xs[:, x2:x2 + NW], T.xs[:, x2 + NW:x2 + 2 * NW], ("xn", t, c), ("fo", t, c)
             big = lambda s, a, b: T[s][:, 16 * w0 + a:16 * w0 + b]
-            f0 = 16 * w0 + 16 * c + 16
-            fgs = lambda a, b: T.fg[:, f0 + 16 * a:f0 + 16 * b]
+            r0 = w0 + c + 1; f0 = 16 * r0
+            row = lambda q: q // 4 + 4 * (q % 4)
+            fgs = lambda a, b, s="fg": T[s][:, f0 + 16 * a:f0 + 16 * b]
+            fk = lambda q, s="fg": T[s][:, f0 + row(q):f0 + 16 * NW:16]
+            four = lambda s, q0, a, b: T[s][:, f0 + 16 * a + q0 // 4:f0 + 16 * b:4]
+            spread = lambda s, k, n: T[s][:, 16 * w0 + (k - k % n) * NW + k % n:16 * w0 + (k - k % n + n) * NW:n]
             first = t == 0 and c == 0
             wg = NW * (G0 if first else GD) // 16 // 4 * 4; n0 = t * 256 + w0
             cuts = lambda a, b, n: [z for z in [(a + (b - a) * j // n // 4 * 4, a + (b - a) * (j + 1) // n // 4 * 4 if j < n - 1 else b) for j in range(n)] if z[1] > z[0]]
@@ -471,151 +539,169 @@ def build(T, dst, eng):
                 act(fgs(a, b), T.ftab[:].indirect(T.lu[:, n0 + a:n0 + b]), AF.Copy, 0, 1, ["ftab", ku], under("fg", a, b), 16 * (b - a), GR)
             wd = NW * (16 if first else DERD) // 16 // 4 * 4
             for a, b in cuts(0, wd, ESD):
-                ts(T.eg[:, w0 + a:w0 + b, :], fgs(a, b), 1.0 / 16, 143.53125, A.mult, A.add, under("fg", a, b), under("eg", a, b), 16 * (b - a), 0.5)
+                ts(fgs(a, b, "eg"), fgs(a, b), 1.0 / 16, 143.53125, A.mult, A.add, under("fg", a, b), under("eg", a, b), 16 * (b - a), 0.5)
             for a, b in cuts(wd, NW, ES):
-                act(T.eg[:, w0 + a:w0 + b, :], fgs(a, b), AF.Identity, 143.53125, 1.0 / 16, under("fg", a, b), under("eg", a, b), 16 * (b - a))
+                act(fgs(a, b, "eg"), fgs(a, b), AF.Identity, 143.53125, 1.0 / 16, under("fg", a, b), under("eg", a, b), 16 * (b - a))
+            egs = lambda q0, a, b: four("eg", q0, a, b)
+            egk = lambda q: fk(q, "eg")
+            keg = lambda q0, a=0, b=NW: under("eg", a, b)
             kfg = under("fg", 0, NW); ke = under("eg", 0, NW)
             act(S("za"), x, AF.Relu, 16.0, -16.0, [kx], [K("za")], NW)
-            cn, kcn = pt(BA, 0); gid = ("cn", t, c)
-            zparts = []
-            fk = lambda k: T.fg[:, f0 + k:f0 + 16 * NW:16]
+            wI, wN = wt("I"), times("I", -1.0)[0]; kI = ["I", "I*-1.0"]
+            zk = {}; kzg = lambda k0: [("zg", c, k, a) for k in range(k0, k0 + G) for a, _ in cuts(0, NW, HG)]
             for k0 in range(0, KA, G):
-                b = GB[k0 // G % len(GB)]
-                it = []
+                b = GB[k0 // G % len(GB)]; it = []
                 for j in range(G):
-                    it += acc(T["pb%d" % b][:, j * NW:(j + 1) * NW], [(wt("I"), fk(k0 + j)), (wt("nI"), x)], NW)
-                mm(it, kfg + [kx, "I", "nI"], allp(b))
-                act(big("zg", k0 * NW, (k0 + G) * NW), T["pb%d" % b][:, 0:G * NW], AF.Identity, 2311.5, 1.0, allp(b), [("zg", c, k0 + j) for j in range(G)], G * NW)
-                zparts.append((k0, [(k0 + j, big("zg", (k0 + j) * NW, (k0 + j + 1) * NW)) for j in range(G)]))
+                    it += acc(T["pb%d" % b][:, j * NW:(j + 1) * NW], [(wI, fk(k0 + j)), (wN, x)], NW)
+                    zk[k0 + j] = spread("zg", k0 + j, 1)
+                mm(it, kfg + [kx] + kI, allp(b))
+                act(big("zg", k0 * NW, (k0 + G) * NW), T["pb%d" % b][:, 0:G * NW], AF.Identity, 2311.5, 1.0, allp(b), kzg(k0), G * NW)
             if KA < 16:
-                xp, kxp = pt(BS, 3)
-                mm(acc(xp, [(wt("nI"), x), (rows(24, 2), T.ct[0:2, 0:NW])], NW), [kx, "nI", "CX", "ones"], [kxp])
-                for k0 in range(KA, 16):
-                    tt(big("zg", k0 * NW, (k0 + 1) * NW), fk(k0), xp, A.add, kfg + [kxp], [("zg", c, k0)], NW)
-                for k0 in range(KA, 16, G):
-                    zparts.append((k0, [(k0 + j, big("zg", (k0 + j) * NW, (k0 + j + 1) * NW)) for j in range(G)]))
-            turned = T["pb%d" % BA][0:NW, 0:128]; tk = lambda k: T["pb%d" % BA][0:NW, k:128:16]
-            sq = lambda name: T.wt[0:NW, wn[name] * 128:wn[name] * 128 + NW]
+                b, s = where("xp"); R = REPG * NW; s = min(s, 4 - (R + 127) // 128); kxp = [("P", b, s + j) for j in range((R + 127) // 128)]; it = []
+                for j in range(REPG):
+                    it += acc(T["pb%d" % b][:, s * 128 + j:s * 128 + R:REPG], [(wN, x), (rows("CX", 2), ones(2))], NW)
+                mm(it, [kx, "CX", "ones"] + kI, kxp)
+                for a, z in cuts(0, NW, HG):
+                    for k0 in range(KA, 16, REPG):
+                        tt(big("zg", k0 * NW + a * REPG, k0 * NW + z * REPG), four("fg", k0, a, z),
+                           T["pb%d" % b][:, s * 128 + a * REPG:s * 128 + z * REPG], A.add, under("fg", a, z) + kxp, [("zg", c, k0 + j, a) for j in range(REPG)], (z - a) * REPG)
+                for k in range(KA, 16):
+                    zk[k] = spread("zg", k, REPG)
+
+            def turned(name):
+                b, s = where(name)
+                return T["pb%d" % b][0:NW, s * 128:s * 128 + 128], lambda q: T["pb%d" % b][0:NW, s * 128 + row(q):s * 128 + 128:16]
+
+            def bg(v):
+                kw = times("BO", v)[1]
+                return T.wt[:, wn[kw] * 128:wn[kw] * 128 + 128:16], kw
+
+            def sq(v):
+                kw = times("I", v)[1]
+                return T.wt[0:NW, wn[kw] * 128:wn[kw] * 128 + NW], kw
             back = T.tr[0:NW, 128 * c:128 * c + 128]
+            cn, kcn = ps("cn"); w8, k8 = times("I", 8.0); w512, k512 = times("I", 512.0)
             if TG:
-                sums = [([(tk(k), ap, bg("BO"), 8) for k, ap in parts], [("zg", c, k) for k, ap in parts] + ["BO"]) for k0, parts in zparts]
-                sums[0:0] = [([(turned, fl, wt("I8"), 128)] * (k0 == 0) + [(tk(k), T.eg[:, sl, k], bg("BO16"), 8) for k in range(k0, k0 + 8)], ke + [kf, "BO16", "I8"]) for k0 in (0, 8)]
-                sums[-1:-1] = [([(turned, asl, wt("I512"), 128)], [kz, "I512"])]
+                tu, tk = turned("cn")
+                sums = [([(tk(k), zk[k], bg(1.0)[0], 8) for k in range(k0, k0 + G)], kzg(k0) + ["BO"]) for k0 in range(0, 16, G)]
+                sums[0:0] = [([(tu, fl, w8, 128)] * (k0 == 0) + [(tk(k), egk(k), bg(-16.0)[0], 8) for k in range(k0, k0 + 4)], keg(k0) + [kf, bg(-16.0)[1], k8]) for k0 in range(0, 16, 4)]
+                sums[-1:-1] = [([(tu, asl, w512, 128)], [kz, k512])]
             else:
-                sums = [([(cn, sw(0, k), ap, NW) for k, ap in parts], [("zg", c, k) for k, ap in parts] + ["sw0"]) for k0, parts in zparts]
-                sums[1:1] = [([(cn, sw(1, k), T.eg[:, sl, k], NW) for k in range(k0, k0 + 4)], ke + ["sw1"]) for k0 in range(0, 16, 4)]
-                sums[-1:-1] = [([(cn, wt("I8"), fl, NW), (cn, wt("I512"), asl, NW)], [kf, kz, "I8", "I512"])]
-            for j, (it, r) in enumerate(sums):
-                e = j == len(sums) - 1
-                mm([(o, a, b, j == 0 and i == 0, e and i == len(it) - 1, n) for i, (o, a, b, n) in enumerate(it)], r, [kcn], (BA, gid, e))
+                sums = [([(cn, sw(0, row(k)), zk[k], NW) for k in range(k0, k0 + G)], kzg(k0) + ["sw0"]) for k0 in range(0, 16, G)]
+                sums[1:1] = [([(cn, sw(1, row(k)), egk(k), NW) for k in range(k0, k0 + 4)], keg(k0) + ["sw1"]) for k0 in range(0, 16, 4)]
+                sums[-1:-1] = [([(cn, w8, fl, NW), (cn, w512, asl, NW)], [kf, kz, k8, k512])]
+            run(sums, [kcn], "cn")
             if TG:
-                act(back, turned, AF.Copy, 0.0, 1.0, [kcn], [K("tr")], 128)
-                mm(acc(cn, [(back, sq("I"))], NW), [K("tr"), "I"], [kcn])
+                act(back, tu, AF.Copy, 0.0, 1.0, [kcn], [K("tr")], 128)
+                mm(acc(cn, [(back, sq(1.0)[0])], NW), [K("tr"), "I"], [kcn])
             act(S("cand"), cn, AF.Sign, 108.0, -1.0, [kcn], [K("cand")], NW)
-            mp, kmp = pt(BA, 1); pr, kpr = pt(BA, 2); ix = pt(BA, 1, ND)[0]; au, kau = pt(BA, 3)
-            mm(acc(mp, [(wt("I"), ct(4)), (wt("nBO"), S("cand"))], NW) + acc(pr, [(wt("I"), ct(4)), (wt("TRI"), S("cand"))], NW),
-               [K("cand"), "nBO", "TRI", "I", "cP"], [kmp, kpr])
+            cP = ("I", 1.0, ct(4, NW), "cP"); tri = ("TRI", 1.0, S("cand"), K("cand"))
+            (mp, kmp), (pr, kpr) = ps("mp"), ps("pr"); wb, kb = times("BO", -1.0)
+            mm(acc(mp, [(wI, ct(4, NW)), (wb, S("cand"))], NW) + acc(pr, [(wI, ct(4, NW)), (wt("TRI"), S("cand"))], NW), ["I", "cP", "TRI", kb, K("cand")], [kmp, kpr])
             act(S("r2"), mp, AF.Relu, col(5), 1.0, [kmp, "c5"], [K("r2")], NW)
             tt(S("go"), pr, S("r2"), A.is_equal, [kpr, K("r2")], [K("go")], NW)
             if FALLA:
-                dl, kdl = pt(BS, 2)
-                mm(acc(dl, [(wt("I"), ct(4)), (wt("TRI"), S("cand")), (wt("nI"), S("r2"))], NW), [K("cand"), K("r2"), "TRI", "I", "nI", "cP"], [kdl])
+                dl, kdl = lsum("dl", [cP, tri, ("I", -1.0, S("r2"), K("r2"))])
                 act(S("fall"), dl, AF.Sign, -1.0, 1.0, [kdl], [K("fall")], NW)
             else:
                 tt(S("fall"), pr, S("r2"), A.is_gt, [kpr, K("r2")], [K("fall")], NW)
-            mm(acc(ix, [(wt("I"), ct(11, ND))] + [(T.swi[:, 15 - r:143 - r], T.go[:, w0 + r:w0 + NW:16]) for r in range(16)], ND),
-               [K("go"), "swi", "I", "cI"], [kmp])
-            iu = T.iu[:, w0 // 16:w0 // 16 + ND]
-            ts(iu, ix, 16.0 - HB, None, A.add, None, [kmp], [K("iu")], ND)
-            win = T.fg[:, f0 - 16:f0 + 16 * NW].indirect(iu)
+            ix, kix = lsum("ix", [("I", 1.0, ct(11, ND), "cI")] + [(T.swi[:, 15 - r:143 - r], "swi", T.go[:, w0 + r:w0 + NW:16], K("go")) for r in range(16)], ND)
+            dsl = slice(w0 // 16, w0 // 16 + ND); d2 = 8 * c
+            iu = T.iu[:, d2:d2 + ND]
+            ts(iu, ix, 16.0 - HB, None, A.add, None, [kix], [K("iu")], ND)
+            win = T.eg[:, f0 - 16:f0 + 16 * NW].indirect(iu)
             if EGA:
-                act(S("ee"), win, AF.Identity, 143.53125, 1.0 / 16, kfg + [K("iu"), ("pad", c)], [K("ee")], NW, GR)
+                act(S("ee"), win, AF.Copy, 0, 1, ke + [K("iu"), ("pad", c)], [K("ee")], NW, GR)
             else:
-                ts(S("ee"), win, 1.0 / 16, 143.53125, A.mult, A.add, kfg + [K("iu"), ("pad", c)], [K("ee")], NW, GR)
-            ds, kds = pt(BA, 1); d0, kd0 = pt(BA, 2)
+                cp(S("ee"), win, ke + [K("iu"), ("pad", c)], [K("ee")], NW, GR)
+            tx = ("I", 1.0, x, kx); tza = ("I", 1.0, S("za"), K("za")); tee = ("I", -1.0, S("ee"), K("ee"))
             act(S("zc"), S("ee"), AF.Relu, 2320.0, -16.0, [K("ee")], [K("zc")], NW)
-            mm(acc(ds, [(wt("I"), x), (wt("I"), S("za")), (wt("nI"), S("ee"))], NW), [kx, K("za"), K("ee"), "I", "nI"], [kds])
-            mm(acc(d0, [(wt("I"), x), (wt("nI"), S("ee"))], NW), [kx, K("ee"), "I", "nI"], [kd0])
-            mm(acc(au, [(wt("I"), x), (wt("I"), S("za")), (wt("I"), S("zc"))], NW), [kx, K("za"), K("zc"), "I"], [kau])
-            act(S("le"), ds, AF.Relu, 64.0 * 145, 64.0, [kds], [K("le")], NW)
+            if LED:
+                ds, kds = lsum("xa", [tx, tza, ("I", 1.0, ct(2, NW), "c128"), ("I", 0.0, None, kcn)])
+                tt(S("le"), ds, S("ee"), A.is_ge, [kds, K("ee")], [K("le")], NW)
+            else:
+                ds, kds = lsum("ds", [tx, tza, tee])
+                act(S("le"), ds, AF.Relu, 145.0, 1.0, [kds], [K("le")], NW)
+            d0, kd0 = lsum("d0", [tx, tee])
+            au, kau = lsum("au", [("I", 1.0 / 64, x, kx), ("I", 1.0 / 64, S("za"), K("za")), ("I", 1.0 / 64, S("zc"), K("zc"))])
             tt(S("qq"), au, S("le"), A.min, [kau, K("le")], [K("qq")], NW)
             act(xn, d0, AF.Abs, 144.0, 1.0, [kd0], [kxn], NW)
             R = REP * NW
-            wq, kwq = pt(BA, 0); gid = ("w", t, c); sums = {}
-            term = lambda j, k, ap: (tk(k), ap, bg({2: "BO", 3: "nBO", 4: "BOh"}[j]), 8) if TW else (wq, sw(j, k), ap, NW)
+            wq, kwq = ps("wq"); tu, tk = turned("wq"); sums = {}
+            term = lambda j, k, ap: (tk(k), ap, bg({2: 1.0, 3: -1.0, 4: -0.5}[j])[0], 8) if TW else (wq, sw(j, row(k)), ap, NW)
+            kterm = lambda j: bg({2: 1.0, 3: -1.0, 4: -0.5}[j])[1] if TW else "sw%d" % j
             for k0 in range(0, TA, G):
-                b = TB[k0 // G % len(TB)]
-                it = []
+                b = TB[k0 // G % len(TB)]; it = []
                 for j in range(G):
-                    it += acc(T["pb%d" % b][:, j * NW:(j + 1) * NW], [(wt("I"), T.eg[:, sl, k0 + j]), (wt("nI"), S("qq"))], NW)
-                mm(it, ke + [K("qq"), "I", "nI"], allp(b))
-                act(big("ta", k0 * NW, (k0 + G) * NW), T["pb%d" % b][:, 0:G * NW], AF.Sign, -144.5, 1.0, allp(b), [("ta", c, k0 + j) for j in range(G)], G * NW)
-                sums["ta", k0] = ([term(4, k, big("ta", k * NW, (k + 1) * NW)) for k in range(k0, k0 + G)], [("ta", c, k0), "sw4", "BOh"])
-            for nm_, b, o, wj, k1, terms in (("tb", 2, A.is_equal, 2, 0, [(S("ee"), K("ee")), (S("le"), K("le"))]),
-                                             ("ta", 3, A.is_gt, 3, TA, [(ct(2), "c128"), (S("qq"), K("qq"))])):
+                    it += acc(T["pb%d" % b][:, j * NW:(j + 1) * NW], [(wI, egk(k0 + j)), (times("I", -64.0)[0], S("qq"))], NW)
+                mm(it, keg(k0) + [K("qq"), "I", "I*-64.0"], allp(b))
+                act(big("ta", k0 * NW, (k0 + G) * NW), T["pb%d" % b][:, 0:G * NW], AF.Sign, -144.5, 1.0, allp(b), [("ta", c, k0, 0)], G * NW)
+                sums["ta", k0] = ([term(4, k, spread("ta", k, 1)) for k in range(k0, k0 + G)], [("ta", c, k0, 0), kterm(4)])
+            for nm_, b, o, wj, k1, terms in (("tb", KB, A.is_equal, 2, 0, [(S("ee"), K("ee")), (S("le"), K("le"))]),
+                                             ("ta", THB, A.is_gt, 3, TA, [(ct(2, NW), "c128"), (S("qq"), K("qq"))])):
                 if k1 == 16:
                     continue
                 it = []; pb = T["pb%d" % b]
                 for j in range(REP):
-                    it += acc(pb[:, j:R:REP], [(wt("I"), a) for a, _ in terms], NW)
-                mm(it, [k for _, k in terms] + ["I"], allp(b))
-                for k0 in range(k1, 16, REP):
-                    tt(big(nm_, k0 * NW, k0 * NW + R), T.eg[:, sl, k0:k0 + REP], pb[:, 0:R], o, ke + allp(b), [(nm_, c, k0 + j) for j in range(REP)], R)
+                    it += acc(pb[:, j:R:REP], [(wI, terms[0][0]), (wt("I*64.0"), terms[1][0])], NW)
+                mm(it, [k for _, k in terms] + ["I", "I*64.0"], allp(b))
                 for k0 in range(k1, 16, G):
-                    sums[nm_, k0] = ([term(wj, k, T[nm_][:, 16 * w0 + (k - k % REP) * NW + k % REP:16 * w0 + (k - k % REP) * NW + R:REP]) for k in range(k0, k0 + G)],
-                                     [(nm_, c, k) for k in range(k0, k0 + G)] + ["sw%d" % wj, "nBO", "BO"])
-            if TA < 16 or not MIX:
+                    for a, z in cuts(0, NW, HW):
+                        tt(big(nm_, k0 * NW + 4 * a, k0 * NW + 4 * z), egs(k0, a, z), pb[:, 4 * a:4 * z], o, keg(k0) + allp(b), [(nm_, c, k0, a)], 4 * (z - a))
+                    sums[nm_, k0] = ([term(wj, k, spread(nm_, k, REP)) for k in range(k0, k0 + G)], [(nm_, c, k0, a) for a, _ in cuts(0, NW, HW)] + [kterm(wj)])
+            if TA < 16:
                 seq = [("tb", k0) for k0 in range(0, 16, G)] + [("ta", k0) for k0 in range(0, 16, G)]
             else:
                 seq = [(nm_, k0) for k0 in range(0, 16, G) for nm_ in ("tb", "ta")]
+            fw_ = 8.0 if FALLA else 16.0
             if TW:
-                mm([(turned, asl, wt("I16"), True, False, 128), (turned, S("fall"), wt("I8" if FALLA else "I16"), False, False, 128)],
-                   [kz, K("fall"), kxn, K("qq"), "I16", "I8"], [kwq], (BA, gid, False))
-                for j, z in enumerate(seq):
-                    it, r = sums[z]; e = j == len(seq) - 1
-                    mm([(o, a, b, False, e and i == len(it) - 1, n) for i, (o, a, b, n) in enumerate(it)], r, [kwq], (BA, gid, e))
-                act(back, turned, AF.Copy, 0.0, 1.0, [kwq], [K("tr")], 128)
+                (wa, ka_), (wb, kb_) = times("I", 16.0), times("I", fw_)
+                run([([(tu, asl, wa, 128), (tu, S("fall"), wb, 128)], [kz, K("fall"), kxn, K("qq"), ka_, kb_])] + [sums[z] for z in seq], [kwq], "wq")
+                act(back, tu, AF.Copy, 0.0, 1.0, [kwq], [K("tr")], 128)
                 if WQB is None:
-                    mm(acc(wq, [(wt("IU"), ct(6 + t)), (wf(0), nf, 1), (back, sq("IU"))], NW), [kn, K("tr"), "wf0", "IU", "cD%d" % t], [kwq])
+                    lsum("wq", [("I", U, ct(6 + t, NW), "cD%d" % t), (wf(0), "wf0", nf, kn), (back, K("tr")[0], sq(U)[0], K("tr"))])
                 else:
-                    wq, kwq = pt(WQB, 0)
-                    mm([(wq, wt("IU"), ct(6 + t), True, False, NW), (wq, wf(0), nf, False, False, 4 * NW)], [kn, "wf0", "IU", "cD%d" % t], [kwq], (WQB, gid, False))
-                    mm([(wq, back, sq("IU"), False, True, NW)], [K("tr"), "IU"], [kwq], (WQB, gid, True))
+                    wq, kwq = T["pb%d" % WQB][:, 0:NW], ("P", WQB, 0); wu, ku_ = times("I", U)
+                    run([([(wq, wu, ct(6 + t, NW), NW), (wq, wf(0), nf, 4 * NW)], [kn, "wf0", ku_, "cD%d" % t]), ([(wq, back, sq(U)[0], NW)], [K("tr")])], [kwq], "wq")
             else:
-                for j, z in enumerate(seq):
-                    it, r = sums[z]
-                    mm([(o, a, b, j == 0 and i == 0, False, n) for i, (o, a, b, n) in enumerate(it)], r + ([kxn, K("qq")] if j == 0 else []), [kwq], (BA, gid, False))
-                    if j == 0:
-                        mm([(wq, wt("IU"), ct(6 + t), False, False, NW), (wq, wf(0), nf, False, False, 4 * NW)],
-                           [kn, "wf0", "IU", "cD%d" % t], [kwq], (BA, gid, False))
-                mm([(wq, wt("IV16"), asl, False, False, NW), (wq, wt("IU16"), S("fall"), False, True, NW)],
-                   [kz, K("fall"), "IU16", "IV16"], [kwq], (BA, gid, True))
-            u0, ku0 = pt(BS, 0); v2, kv2 = pt(BS, 1); dy, kdy = pt(BS, 2); sn, ksn = pt(BS, 3); ud = pt(BS, 3, ND)[0]
-            mm(acc(ud, [(sw(5, r), T.xs[:, x2 + r:x2 + NW:16]) for r in range(16)], ND), [kxn, "sw5"], [ksn])
-            mm(acc(u0, [(wt("H16"), xn)], NW), [kxn, "H16"], [ku0])
-            dsl = slice(w0 // 16, w0 // 16 + ND)
-            ts(T.cd0[:, dsl], ud, 241.0, None, A.mult, None, [ksn], [K("cd0")], ND)
+                (wu, ku_), (wa, ka_), (wb, kb_) = times("I", U), times("I", 16 * U), times("I", fw_ * U)
+                gs = [sums[z] for z in seq]
+                gs[0] = (gs[0][0], gs[0][1] + [kxn, K("qq")])
+                gs[1:1] = [([(wq, wu, ct(6 + t, NW), NW), (wq, wf(0), nf, 4 * NW)], [kn, "wf0", ku_, "cD%d" % t])]
+                run(gs + [([(wq, wa, asl, NW), (wq, wb, S("fall"), NW)], [kz, K("fall"), ka_, kb_])], [kwq], "wq")
+            txn = ("I", -1.0, xn, kxn); th16 = ("H16", 1.0, xn, kxn)
+            ud, kud = lsum("ud", [(sw(5, r), "sw5", T.xs[:, x2 + r:x2 + NW:16], kxn) for r in range(16)], ND)
+            u0, ku0 = lsum("u0", [th16])
+            ts(T.cd0[:, dsl], ud, 241.0, None, A.mult, None, [kud], [K("cd0")], ND)
             ts(T.cd[:, dsl], T.cd0[:, dsl], 6, 1023, A.logical_shift_right, A.bitwise_and, [K("cd0")], [K("cd")], ND)
-            cu = T.cu[:, dsl]
+            cu = T.cu[:, d2:d2 + ND]
             cp(cu, T.cd[:, dsl], [K("cd")], [K("cu")], ND)
             act(S("hi"), u0, AF.Identity, 159.5 + 1.0 / 2048, 1.0 / 64, [ku0], [K("hi")], NW)
-            mm(acc(v2, [(wt("H16"), xn), (rows(23, 3), T.ct[0:3, 0:NW]), (wt("In64"), S("hi"))], NW), [kxn, K("hi"), "H16", "CW", "ones", "In64"], [kv2])
+            v2, kv2 = lsum("v2", [th16, (rows("CW", 3), "CW", ones(3), "ones"), ("I", -64.0, S("hi"), K("hi"))])
             tt(S("pp"), v2, nf, A.mult, [kv2, kn], [K("pp")], NW)
+            ss, kss = u0, ku0
             if SSP:
-                mm(acc(u0, [(rows(25, 3), T.ct[0:3, 0:NW]), (wf(1), nf, 1), (wf(0), S("pp"), 1)], NW), [kn, K("pp"), "CS", "ones", "wf0", "wf1"], [ku0])
+                lsum("u0", [(rows("CS", 3), "CS", ones(3), "ones"), (wf(1), "wf1", nf, kn), (wf(0), "wf0", S("pp"), K("pp"))])
             else:
                 act(u0, nf, AF.Identity, col(4), 33.0, [kn, "c4"], [ku0], NW)
-                tt(u0, u0, S("pp"), A.add, [ku0, K("pp")], [ku0], NW)
+                if AAP:
+                    ss, kss = S("ss"), K("ss")
+                tt(ss, u0, S("pp"), A.add, [ku0, K("pp")], [kss], NW)
             act(S("yq"), T.st[:].indirect(cu), AF.Abs, 0.0, 2.0 ** -21, ["st", K("cu")], [K("yq")], NW, GR)
             act(S("wg"), T.st[:].indirect(cu), AF.Copy, 0.0, 1.0, ["st", K("cu")], [K("wg")], NW, GR)
-            mm(acc(dy, [(wt("nI"), xn), (wt("I"), S("yq"))], NW), [kxn, K("yq"), "nI", "I"], [kdy])
+            tyq = ("I", 1.0, S("yq"), K("yq"))
+            dy, kdy = lsum("dy", [txn, tyq])
             act(S("ad"), dy, AF.Abs, -Y0, 1.0, [kdy], [K("ad")], NW)
-            mm(acc(sn, [(wt("BOn"), ct(5)), (wt("BOn"), S("ad"))], NW), [K("ad"), "BOn", "cT"], [ksn])
-            tt(S("aa"), sn, S("wg"), A.min, [ksn, K("wg")], [K("aa")], NW)
+            sn, ksn = lsum("sn", [("BO", -2.0 ** 30, ct(5, NW), "cT1"), ("BO", -2.0 ** 30, S("ad"), K("ad"))])
             act(fo, sn, AF.Sign, 0.0, 1.0, [ksn], [kfo], NW)
+            if AAP:
+                ap, kap = lsum("ap", [(wf(0), "wf0", S("wg"), K("wg")), ("I", -2.0 ** 29, T.one[:, 0:NW], "ones"), ("I", 2.0 ** 29, fo, kfo)])
+                tt(S("m0"), ap, ss, A.max, [kap, kss], [K("m0")], NW)
+            else:
+                tt(S("aa"), sn, S("wg"), A.min, [ksn, K("wg")], [K("aa")], NW)
+                tt(S("m0"), ss, S("aa"), A.max, [kss, K("aa")], [K("m0")], NW)
             if t < 3:
                 send(0, t, c, T.lx[:, x2 + 512:x2 + 512 + 2 * NW], T.xs[:, x2:x2 + 2 * NW], [kxn, kfo], [("lx", t + 1, c)])
-            tt(S("m0"), u0, S("aa"), A.max, [ku0, K("aa")], [K("m0")], NW)
             tt(S("mi"), wq, S("m0"), A.max, [kwq, K("m0")], [K("mi")], NW)
             ts(S("fi"), S("mi"), 8191 * 32, None, A.bitwise_and, None, [K("mi")], [K("fi")], NW)
             zo, uo = T.zs[:, s4], T.us[:, s4]; kzo, kuo = ("zs", t, c), ("us", t, c)
@@ -623,50 +709,54 @@ def build(T, dst, eng):
             if t < 3:
                 ts(uo, S("fi"), 1.0 / 32, None, A.mult, None, [K("fi")], [kuo], NW)
                 send(1, t, c, T.lu[:, n4:n4 + NW], uo, [kuo], [("lu", t + 1, c)])
-            ka, kka = pt(BA, 1); sg, ksg = pt(BA, 2); zp, kzp = pt(BA, 3)
-            tt(ka, wq, nf, A.min, [kwq, kn], [kka], NW)
+            if KAP:
+                act(S("sa"), wq, AF.Sign, 0.0, 1.0, [kwq], [K("sa")], NW)
+                ka, kka = lsum("ka", [(wf(0), "wf0", nf, kn), ("I", -2.0 ** 20, T.one[:, 0:NW], "ones"), ("I", 2.0 ** 20, S("sa"), K("sa"))])
+            else:
+                ka, kka = ps("ka")
+                tt(ka, wq, nf, A.min, [kwq, kn], [kka], NW)
             tt(zo, ka, S("fi"), A.is_equal, [kka, K("fi")], [kzo], NW)
             if t < 3:
                 send(2, t, c, T.lz[:, n4:n4 + NW], zo, [kzo], [("lz", t + 1, c)])
             else:
                 ts(S("yn"), S("fi"), 1.0 / 32, None, A.mult, None, [K("fi")], [K("yn")], NW)
-                mm(acc(zp, [(wt("I8192"), zo)], NW), [kzo, "I8192"], [kzp])
+                zp, kzp = lsum("zp", [("I", 8192.0, zo, kzo)])
                 tt(S("yts"), zp, S("yn"), A.add, [kzp, K("yn")], [K("yts")], NW)
                 dma("sp", T.yt[:, sl], S("yts"), [K("yts")], [], 0.3)
                 dma("sp", T.yx[:, sl], xn, [kxn], [], 0.3)
             stage[0] = ENT + STP * t
-            ts(T.cdh[:, dsl], T.cd[:, dsl], 1.0, None, A.add, None, [K("cd")], [K("cdh")], ND)
             if SEA:
                 act(S("se"), S("wg"), AF.Sign, 0.0, 1.0, [K("wg")], [K("se")], NW)
-                mm(acc(sg, [(wt("I"), S("se")), (wt("nI"), fo), (wt("I4"), zo)], NW), [K("se"), kfo, kzo, "I", "nI", "I4"], [ksg])
-            else:
-                mm(acc(sg, [(wf(2), S("wg"), 1), (wt("nI"), fo), (wt("I4"), zo)], NW), [K("wg"), kfo, kzo, "wf2", "nI", "I4"], [ksg])
+            sg, ksg = lsum("sg", [("I", 1.0, S("se"), K("se")) if SEA else (wf(2), "wf2", S("wg"), K("wg")), ("I", -1.0, fo, kfo), ("I", 4.0, zo, kzo)])
             act(S("sg"), sg, AF.Sign, -3.0, 1.0, [ksg], [K("sg")], NW)
-            mm(acc(dy, [(wt("nI"), xn), (wt("I"), S("yq")), (wt("I32"), fo)], NW), [kxn, K("yq"), kfo, "nI", "I", "I32"], [kdy])
-            act(S("hd"), dy, AF.Relu, -Y0, 1.0, [kdy], [K("hd")], NW)
-            terms = [(wt("I21"), xn), (wt("In25"), fo), (wt("I21"), S("hd"))]
+            e2, ke2 = lsum("d2", [txn, tyq, ("I", 32.0, fo, kfo)])
+            act(S("hd"), e2, AF.Relu, -Y0, 1.0, [ke2], [K("hd")], NW)
+            terms = [("I", 2.0 ** 21, xn, kxn), ("I", -2.0 ** 25, fo, kfo), ("I", 2.0 ** 21, S("hd"), K("hd"))]
             if VP:
-                mm(acc(v2, terms + [(wf(0), nf, 1)], NW), [kxn, kfo, K("hd"), kn, "I21", "In25", "wf0"], [kv2])
-                act(S("vv"), v2, AF.Identity, (Y0 - 16) * 2 ** 21, 1.0, [kv2], [K("vv")], NW)
+                vv, kvv = lsum("vv", terms + [(wf(0), "wf0", nf, kn)])
+                act(S("vv"), vv, AF.Identity, (Y0 - 16) * 2 ** 21, 1.0, [kvv], [K("vv")], NW)
             else:
-                mm(acc(v2, terms + [(wt("I21"), ct(1))], NW), [kxn, kfo, K("hd"), "I21", "In25", "c176"], [kv2])
-                tt(S("vv"), v2, nf, A.add, [kv2, kn], [K("vv")], NW)
+                vv, kvv = lsum("vv", terms + [("I", 2.0 ** 21, ct(1, NW), "c176")])
+                tt(S("vv"), vv, nf, A.add, [kvv, kn], [K("vv")], NW)
+        part[:] = ["s", {}, 2 * t + 1]
         for cs in ([[c] for c in range(C)] if t >= SPLIT else [list(range(C))]):
             al = lambda s: [(s, c) for c in cs]
             a, n = sum(NWS[:cs[0]]) // 16, sum(NWS[c] for c in cs) // 16; ws = slice(16 * a, 16 * (a + n))
             if t >= SPLIT:
                 stage[0] = OFF * cs[0] + STP * t
-            b = 3 if TA == 16 else 2; pb = T["pb%d" % b]
-            mm([(pb[:, r:16 * n:16], dm(r), T.cdh[:, a:a + n], True, True, n) for r in range(16)], al("cdh") + ["dm%d" % r for r in range(16)], allp(b))
-            ts(T.eq[:, ws], pb[:, 0:16 * n], 0.0, None, A.is_equal, None, allp(b), al("eq"), 16 * n)
+            pb = T["pb%d" % DB]; w2, k2 = times("I", 2048.0)
+            ts(T.cdh[:, a:a + n], T.cd[:, a:a + n], 1.0, None, A.add, None, al("cd"), al("cdh"), n)
+            mm([(pb[:, r:16 * n:16], dm(r), T.cdh[:, a:a + n], True, True, n) for r in range(16)], al("cdh") + ["dm%d" % r for r in range(16)], allp(DB))
+            ts(T.eq[:, ws], pb[:, 0:16 * n], 0.0, None, A.is_equal, None, allp(DB), al("eq"), 16 * n)
             lo = pb[:, 0:n]
-            mm(acc(lo, [(dm(0), T.cdh[:, a:a + n])] + [(wt("I2048"), T.eq[:, 16 * a + r:16 * (a + n):16]) for r in range(1, 16)], n),
-               al("eq") + al("cdh") + ["dm0", "I2048"], allp(b))
-            ts(T.off[:, 2 * a:2 * (a + n):2], lo, -1.0, col(6), A.add, A.min, allp(b) + ["c6"], al("off"), n)
+            mm(acc(lo, [(dm(0), T.cdh[:, a:a + n])] + [(w2, T.eq[:, 16 * a + r:16 * (a + n):16]) for r in range(1, 16)], n),
+               al("eq") + al("cdh") + ["dm0", k2], allp(DB))
+            ts(T.off[:, 2 * a:2 * (a + n):2], lo, -1.0, col(6), A.add, A.min, allp(DB) + ["c6"], al("off"), n)
         for b in range(16):
             c = max(j for j in range(C) if sum(NWS[:j]) <= 16 * b)
             tt(T.st[:].indirect(T.off[:, 2 * b:2 * b + 1]), T.vv[:, 16 * b:16 * b + 16], T.sg[:, 16 * b:16 * b + 16], A.mult,
                [("off", c), ("vv", c), ("sg", c)], ["st"], 16, SC)
+    part[:] = ["z", {}, 8]
     for h in range(4):
         hs = slice(h * 256, h * 256 + 256); k = lambda s: (s, "o", h)
         ts(T.wi[:, hs], T.st[:, hs], 2.0 ** 18, None, A.max, None, ["st"], [k("wi")], 256)

import math
import numpy as np
from concourse.bass import DstId, RemoteDMATransfer
from concourse.mybir import AluOpType as A, ActivationFunctionType as AF

NWS = [128, 128]
CMAX = 4
REP = 2
REPG = 1
KA = 0
TA = 8
DERD = 8
GD = 0
G0 = 8
GS, ES = 4, 2
GSD, ESD = 1, 1
EGA = False
FALLA = False
SSP = False
VP = True
SEA = True
AAP = False
KAP = False
TG, TW = True, True
F3, HG, LED, WQB = False, 1, False, None
SPLIT = 3
BANKS = "chunk"
GB, TB, KB, THB, DB = (0, 1), (0, 1), 2, 3, 2
CY, PC, FV, FA, FP, LAT, LSELF, GR, SC = 0.83e-3, 0.42e-3, 0.05, 0.065, 0.005, 0.12, 0.06, 1.56, 3.8
COMM, TAB, ROUNDS = 3.0, 6.0, 6
OFF, STP, ENT = 3.0, 6.0, 6.0
MOVES, HEAT, SEED, KEPT = 40000, 0.2, 1, {}
REPG, HG, LED, ESD, ES, REP, HW = 4, 2, True, 1, 2, 4, 1
U = 80.0 * 2 ** 18
Y0 = 192.0
HB = 2033
PLACES = {
    "chunk": dict(cn=("A", 0), xp=("S", 2), mp=("A", 1), pr=("A", 2), ix=("A", 1), dl=("S", 2), ds=("A", 1), d0=("A", 2), au=("A", 3), wq=("A", 0), xa=("S", 0),
                  ka=("A", 1), zp=("A", 3), u0=("S", 0), ud=("S", 3), v2=("S", 1), dy=("S", 2), sn=("S", 3), ap=("S", 2), sg=("A", 2), d2=("S", 2), vv=("S", 1)),
    "phase": dict(cn=(4, 0), xp=(3, 2), mp=(5, 0), pr=(5, 1), ix=(5, 2), dl=(5, 3), ds=(5, 0), d0=(5, 1), au=(5, 2), wq=(6, 0),
                  ka=(6, 1), zp=(6, 2), u0=(7, 0), ud=(7, 3), v2=(7, 1), dy=(7, 2), sn=(7, 3), ap=(7, 2), sg=(3, 0), d2=(3, 1), vv=(3, 0)),
}

BF, F32, I32, U16, F16 = "bfloat16", "float32", "int32", "uint16", "float16"
SCRATCH = {
    "ftab": ("sbuf", [128, 8192], BF), "eg": ("sbuf", [128, 4096 + 16 * CMAX], BF), "fg": ("sbuf", [128, 4096 + 16 * CMAX], BF),
    "zg": ("sbuf", [128, 4096], BF), "ta": ("sbuf", [128, 4096], BF), "tb": ("sbuf", [128, 4096], BF),
    "st": ("sbuf", [128, 1040], F32), "kin": ("sbuf", [128, 1024], I32), "yin": ("sbuf", [128, 1024], BF),
    "w1": ("sbuf", [128, 1024], F32), "wi": ("sbuf", [128, 1024], I32), "wj": ("sbuf", [128, 1024], I32),
    "yo": ("sbuf", [128, 1024], BF), "ys": ("sbuf", [128, 1024], BF), "one": ("sbuf", [128, 512], BF),
    "tin": ("sbuf", [128, 256], I32), "tnm": ("sbuf", [128, 256], I32), "xin": ("sbuf", [128, 256], BF),
    "din": ("sbuf", [128, 8], I32), "hin": ("sbuf", [128, 8], I32), "thin": ("sbuf", [128, 8], I32),
    "xs": ("sbuf", [128, 4 * 512], BF), "us": ("sbuf", [128, 4 * 256], U16), "zs": ("sbuf", [128, 4 * 256], BF),
    "lx": ("sbuf", [128, 4 * 512], BF), "lu": ("sbuf", [128, 4 * 256], U16), "lz": ("sbuf", [128, 4 * 256], BF),
    "cj": ("sbuf", [128, 512], F32), "cf": ("sbuf", [128, 160], F32), "col": ("sbuf", [128, 48], F32),
    "coli": ("sbuf", [128, 8], I32), "dm": ("sbuf", [128, 16 * 128], F16), "sw": ("sbuf", [128, 6 * 144], BF), "swi": ("sbuf", [128, 144], F16),
    "wt": ("sbuf", [128, 36 * 128], BF), "tr": ("sbuf", [128, 128 * CMAX], BF), "wf": ("sbuf", [128, 4 * 128], F32),
    "ct": ("sbuf", [128, 12 * 128], BF), "iu": ("sbuf", [128, 32], U16), "cu": ("sbuf", [128, 32], U16),
    "cd": ("sbuf", [128, 16], I32), "cd0": ("sbuf", [128, 16], I32), "cdh": ("sbuf", [128, 16], F16), "off": ("sbuf", [128, 32], U16),
    "go": ("sbuf", [128, 256], F16),
}
for _n in ("cand", "r2", "fall", "ee", "za", "zc", "le", "qq", "hi", "yq", "ad", "hd", "eq", "se", "sa"):
    SCRATCH[_n] = ("sbuf", [128, 256], BF)
for _n in ("nf", "pp", "ss", "wg", "aa", "m0", "sg", "vv", "yn", "yts"):
    SCRATCH[_n] = ("sbuf", [128, 256], F32)
for _n in ("mi", "fi"):
    SCRATCH[_n] = ("sbuf", [128, 256], I32)
for _b in range(8):
    SCRATCH["pb%d" % _b] = ("psum", [128, 512], F32)
SEMAPHORES = ["pe", "dve", "act", "pool", "sent"] + ["d%d" % i for i in range(28)] + \
    ["a%d_%d_%d" % (k, t, c) for k in range(3) for t in range(1, 4) for c in range(CMAX)]


def place(ops, before, key):
    n = len(ops); start = [0.0] * n; busy = {}; left = [len(b) for b in before]; after = [[] for _ in range(n)]
    for i, b in enumerate(before):
        for d, _ in b:
            after[d].append(i)
    ready = [i for i in range(n) if left[i] == 0]
    while ready:
        i = min(ready, key=lambda j: key[j]); ready.remove(i)
        o = ops[i]; e = o["eng"]; dur = o["dur"]
        t = max([start[d] + ops[d]["dur"] + w for d, w in before[i]] + [0.0])
        if e is not None:
            lines = [(busy.setdefault(e, []), 0.0)] + [(v, LAT + 0.05) for b in o["banks"] for f, v in busy.setdefault(b, {}).items() if f != e]
            moved = True
            while moved:
                moved = False
                for v, gap in lines:
                    lo, hi = 0, len(v)
                    while lo < hi:
                        m = (lo + hi) // 2
                        if v[m][1] + gap <= t + 1e-9:
                            lo = m + 1
                        else:
                            hi = m
                    while lo < len(v) and v[lo][0] - gap < t + dur - 1e-9:
                        t = v[lo][1] + gap; lo += 1; moved = True
            for v in [busy[e]] + [busy[b].setdefault(e, []) for b in o["banks"]]:
                v.append((t, t + dur)); v.sort()
        start[i] = t
        for j in after[i]:
            left[j] -= 1
            if left[j] == 0:
                ready.append(j)
    return start


def tighten(ops, before, order):
    n = len(ops); E = {"pe": 0, "dve": 1, "act": 2, "pool": 3, "sp": 4, None: 5}
    eng = [E[o["eng"]] for o in ops]; dur = [o["dur"] for o in ops]; lat = [o["lat"] for o in ops]; bk = [o["banks"] for o in ops]
    fw = [[(d, w + dur[d]) for d, w in b] for b in before]; gap = LAT + 0.05
    pre = [set(d for d, _ in f) for f in fw]; suc = [set() for _ in range(n)]
    for i in range(n):
        for d in pre[i]:
            suc[d].add(i)

    def times(pi):
        s = [0.0] * n; why = [-1] * n; res = [False] * n
        fe = [0.0] * 6; le = [-1] * 6; bt = [[-9.0] * 3 for _ in range(8)]; bo = [[-1] * 3 for _ in range(8)]
        end = 0.0; last = -1
        for i in pi:
            t = 0.0; y = -1; r = False
            for d, w in fw[i]:
                v = s[d] + w
                if v > t:
                    t = v; y = d
            e = eng[i]
            if e != 5:
                if fe[e] > t + 1e-9:
                    t = fe[e]; y = le[e]; r = True
                for b in bk[i]:
                    for f in range(3):
                        if f != e and bt[b][f] > t + 1e-9:
                            t = bt[b][f]; y = bo[b][f]; r = True
                x = t + dur[i]; fe[e] = x; le[e] = i
                for b in bk[i]:
                    bt[b][e] = x + gap; bo[b][e] = i
            s[i] = t; why[i] = y; res[i] = r
            v = t + dur[i] + lat[i]
            if v > end:
                end = v; last = i
        return end, s, why, res, last
    z = [SEED]

    def rnd():
        z[0] = (z[0] * 1103515245 + 12345) % 2147483648
        return z[0] / 2147483648.0
    pi = list(order); cur = times(pi); best = cur
    for it in range(MOVES):
        _, s, why, res, i = cur; pairs = []
        while i >= 0:
            if res[i] and why[i] not in pre[i]:
                pairs.append((why[i], i))
            i = why[i]
        v, u = pairs[int(rnd() * len(pairs))]; a, b = pi.index(v), pi.index(u)
        far = int(rnd() * 12) if rnd() < 0.3 else 0; mv = []; rest = []
        if rnd() < 0.5:
            a = max(0, a - far); need = {u}
            for x in reversed(pi[a:b + 1]):
                if x in need:
                    mv.append(x); need |= pre[x]
                else:
                    rest.append(x)
            new = pi[:a] + mv[::-1] + rest[::-1] + pi[b + 1:]
        else:
            b = min(n - 1, b + far); need = {v}
            for x in pi[a:b + 1]:
                if x in need:
                    mv.append(x); need |= suc[x]
                else:
                    rest.append(x)
            new = pi[:a] + rest + mv + pi[b + 1:]
        if u in mv and v in mv:
            continue
        c = times(new)
        if c[0] - cur[0] <= -HEAT * (0.1 ** (it / MOVES)) * math.log(1.0 - rnd()):
            pi, cur = new, c
            if it % 32 == 0:
                pi.sort(key=lambda x: c[1][x]); cur = times(pi)
            if cur[0] < best[0]:
                best = cur
    return sorted(range(n), key=lambda i: (best[1][i], i)), best[1]


def plan(ops):
    n = len(ops); fw = [[] for _ in range(n)]; bw = [[] for _ in range(n)]
    for i, o in enumerate(ops):
        for d in o["deps"] | o["soft"]:
            w = 0.0 if d in o["chain"] else ops[d]["lat"] + (LSELF if ops[d]["eng"] == o["eng"] else LAT)
            fw[i].append((d, w)); bw[d].append((i, w))
    pr = [0.0] * n
    for i in range(n - 1, -1, -1):
        pr[i] = ops[i]["dur"] + max([pr[j] + w for j, w in bw[i]] + [ops[i]["lat"]])
    key = [ops[i]["stage"] - pr[i] for i in range(n)]
    end = lambda s: max(s[i] + ops[i]["dur"] + ops[i]["lat"] for i in range(n))
    tail = dict(eng=None, dur=0.0, banks=())
    best = None
    for _ in range(ROUNDS):
        s = place(ops, fw, key)
        if best is None or end(s) < end(best):
            best = s
        r = place(ops + [tail], [b or [(n, ops[i]["lat"])] for i, b in enumerate(bw)] + [[]], [-s[i] - ops[i]["dur"] for i in range(n)] + [0.0])
        key = [-r[i] - ops[i]["dur"] for i in range(n)]
    if KEPT.get("n") != n:
        KEPT["n"] = n; KEPT["plan"] = tighten(ops, fw, sorted(range(n), key=lambda i: (best[i], i)))
    order, best = KEPT["plan"]; bank = {}
    for i in order:
        o = ops[i]; o["t"] = best[i]
        for b in o["banks"]:
            for e, j in bank.get(b, {}).items():
                if e != o["eng"]:
                    o["deps"].add(j)
            bank.setdefault(b, {})[o["eng"]] = i
    return order, end(best)


def emit(g, T, ops, order):
    Q = {"pe": g.tensor, "dve": g.vector, "act": g.scalar, "pool": g, "sp": g.sync}
    pos = {}; cnt = {}
    for i in order:
        o = ops[i]
        if o["sem"] is None:
            cnt[o["eng"]] = cnt.get(o["eng"], 0) + 1; pos[i] = (o["eng"], cnt[o["eng"]])
        else:
            pos[i] = (o["sem"][0], 1)
    clock = {}; known = {e: {} for e in Q}; waits = {}; needed = set()
    for i in order:
        o = ops[i]
        if o["eng"] is None:
            clock[i] = {pos[i][0]: 1}
            continue
        k = known[o["eng"]]; w = []
        for d in sorted(o["deps"] - o["chain"], key=lambda z: -ops[z]["t"]):
            s, v = pos[d]
            if k.get(s, 0) >= v:
                continue
            w.append(d); needed.add(d)
            for s2, v2 in clock[d].items():
                k[s2] = max(k.get(s2, 0), v2)
        waits[i] = w
        clock[i] = dict(k); clock[i][pos[i][0]] = pos[i][1]
    last = {}
    for i in order:
        if ops[i]["sem"] is None and ops[i]["fin"]:
            last[ops[i]["eng"]] = i
    needed |= set(last.values())
    val = {}; tot = {}
    for i in order:
        o = ops[i]
        if o["sem"] is not None:
            val[i] = o["sem"]; tot[o["sem"][0]] = o["sem"][1]
        elif i in needed:
            tot[o["eng"]] = tot.get(o["eng"], 0) + 1; val[i] = (o["eng"], tot[o["eng"]])
    seen = set()
    for i in order:
        o = ops[i]
        if o["eng"] is None:
            continue
        q = Q[o["eng"]]
        for d in waits[i]:
            q.wait_ge(T.sem[val[d][0]], val[d][1]); seen.add(val[d])
        ins = o["fn"](q)
        if o["sem"] is not None:
            ins.then_inc(T.sem[o["sem"][0]], 16)
        elif i in needed:
            ins.then_inc(T.sem[o["eng"]], 1)
    return [(s, v) for s, v in tot.items() if (s, v) not in seen]


def build(T, dst, eng):
    ops = []; lw = {}; rd = {}; nd = [0]; sent = [0]; stage = [0]; sums_in = {}; part = ["c", 0, 0]
    C = len(NWS)

    def op(e, fn, r, w, dur, banks=(), sem=None, lat=0.0, soft=(), fin=True):
        i = len(ops); deps = set(); chain = set()
        for k in r:
            if k in lw:
                deps.add(lw[k])
        for k in w:
            if k in lw:
                deps.add(lw[k])
                if e == "pe" and ops[lw[k]]["eng"] == "pe":
                    chain.add(lw[k])
            deps |= set(rd.get(k, []))
        for k in r:
            rd.setdefault(k, []).append(i)
        for k in w:
            lw[k] = i; rd[k] = []
        deps.discard(i)
        k = w[0] if w else r[0]
        if part[0] == "c" or (isinstance(k, str) and k != "st"):
            kind = ("c", i); half = 0
        else:
            nm = "%s:%s" % (e, k if k == "st" else k[0] if k[0] != "P" else "P%s%d" % ("AASS"[k[1] - 4] if k[1] >= 4 else k[1], k[2]))
            part[1][nm] = part[1].get(nm, -1) + 1; kind = (part[0], nm, part[1][nm]); half = part[2]
        ops.append(dict(eng=e, fn=fn, deps=deps, chain=chain, soft=set(soft), dur=dur, banks=tuple(banks), sem=sem,
                        lat=lat, fin=fin, stage=stage[0], kind=kind, half=half, tag=str(e) + str(w[0] if w else r[0])))
        return i

    def bk(keys):
        return sorted(set(k[1] for k in keys if isinstance(k, tuple) and k[0] == "P"))

    def dma(q, out, in_, r, w, us):
        s = "d%d" % nd[0]; nd[0] += 1
        return op(q, lambda h: h.dma_start(out, in_), r, w, 0.05, sem=(s, 16), lat=2.0 + us)

    def ts(out, in0, s1, s2, o0, o1, r, w, n, rate=1.0):
        if o1 is None:
            f = lambda h: h.tensor_scalar(out, in0, s1, None, o0)
        else:
            f = lambda h: h.tensor_scalar(out, in0, s1, s2, o0, o1)
        return op("dve", f, r, w, FV + CY * max(64, n * rate), bk(r + w))

    def tt(out, in0, in1, o, r, w, n, rate=1.0):
        return op("dve", lambda h: h.tensor_tensor(out, in0, in1, o), r, w, FV + CY * max(64, n * rate), bk(r + w))

    def cp(out, in_, r, w, n, rate=1.0):
        return op("dve", lambda h: h.tensor_copy(out, in_), r, w, FV + CY * max(64, n * rate), bk(r + w))

    def ms(ap, v, w, n=64):
        return op("dve", lambda h: h.memset(ap, v), [], w, FV + CY * max(64, n))

    def act(out, in_, f, bias, scale, r, w, n, rate=1.0):
        if f == AF.Copy:
            fn = lambda h: h.activation(out, in_, f)
        else:
            fn = lambda h: h.activation(out, in_, f, bias=bias, scale=scale)
        return op("act", fn, r, w, FA + CY * max(64, n * rate), bk(r + w))

    def mm(items, r, w, grp=None):
        def f(h):
            for it in items:
                ins = h.matmul(it[0], it[1], it[2], it[3], it[4])
            return ins
        i = op("pe", f, r, w, sum(FP + PC * max(64, it[5]) for it in items), bk(w), lat=0.05)
        z = sums_in.setdefault(w[0][1], dict(open=None, shut=[], ones=[])); first = []
        if grp is None:
            assert z["open"] is None
            first = z["shut"]; z["ones"].append(i)
        elif z["open"] is None:
            first = z["shut"] + z["ones"]; z["open"] = grp[0]; z["ones"] = []
        if grp is not None and grp[1]:
            z["open"] = None; z["shut"] = [i]
        ops[i]["chain"] |= set(first) - ops[i]["deps"]; ops[i]["deps"] |= set(first)
        return i

    def acc(out, terms, n):
        return [(out, z[0], z[1], j == 0, j == len(terms) - 1, max(64, n) * (4 if len(z) > 2 else 1)) for j, z in enumerate(terms)]

    def run(groups, w, name):
        for j, (it, r) in enumerate(groups):
            e = j == len(groups) - 1
            mm([(o, a, b, j == 0 and i == 0, e and i == len(it) - 1, n) for i, (o, a, b, n) in enumerate(it)], r, w, (name, e))

    def iota(out, pat, base, cm, w, flag=True):
        f = (lambda h: h.iota(out, pat, base, cm, allow_small_or_imprecise_dtypes=True)) if flag else (lambda h: h.iota(out, pat, base, cm))
        return op("pool", f, [], w, 0.13 + 2 * CY * int(np.prod([p[1] for p in pat])))

    allp = lambda b: [("P", b, s) for s in range(4)]

    dma("sp", T.ftab[:], T.fx[:], [], ["ftab"], TAB)
    dma("act", T.tin[:], T.t0[:], [], ["tin"], 0.6)
    dma("act", T.xin[:], T.x0[:], [], ["xin"], 0.6)
    dma("act", T.din[:, 0:4], T.dw[:], [], ["din"], 0.6)
    dma("act", T.hin[:, 0:1], T.hw[:], [], ["hin"], 0.6)
    dma("act", T.thin[:, 0:1], T.th[:], [], ["thin"], 0.6)
    dma("sp", T.kin[:], T.k0[:], [], ["kin"], TAB + 1.5)
    dma("sp", T.yin[:], T.y0[:], [], ["yin"], TAB + 2.3)

    col = lambda j: T.col[:, j:j + 1]
    lin = lambda j, a, b: act(col(j), col(1), AF.Identity, b, a, ["c1"], ["c%d" % j], 1)
    iota(T.coli[:, 0:1], [[1, 1]], 0, 1, ["p"], False)
    iota(col(0), [[1, 1]], 0, 1, ["c0"])
    iota(T.cf[:, 0:144], [[1, 144]], 0, 0, ["cf"])
    iota(T.cj[:, 0:128], [[0, 32], [2, 4]], -64, 0, ["cj"])
    iota(T.cj[:, 128:136], [[256, 8]], 0, 0, ["cj2"])
    ts(T.coli[:, 1:2], T.coli[:, 0:1], 15, None, A.bitwise_and, None, ["p"], ["pk"], 1)
    cp(col(1), T.coli[:, 1:2], ["pk"], ["c1"], 1)
    tt(col(2), col(0), col(1), A.subtract, ["c0", "c1"], ["c2"], 1)
    act(col(3), col(2), AF.Identity, 15.0, 1.0, ["c2"], ["c3"], 1)
    for j, a, b in ((4, 1184.0, -2.0 ** 24), (5, 1.0, 50.0), (6, 1.0, 1024.0), (7, 16.0, 0.0), (18, 1.0, float(HB)), (24, -1.0, 0.0)):
        lin(j, a, b)
    ts(T.coli[:, 2:3], T.coli[:, 0:1], 3, None, A.bitwise_and, None, ["p"], ["pq"], 1)
    cp(col(8), T.hin[:, 0:1], ["hin"], ["c8"], 1)
    act(col(9), col(8), AF.Identity, 0.0, 1.0 / 16, ["c8"], ["c9"], 1)
    ts(col(23), T.coli[:, 2:3], TA / 4, -8.0, A.is_lt, A.mult, ["pq"], ["c23"], 1)
    ts(T.col[:, 10:14], T.din[:, 0:4], -8.875 if FALLA else -16.875, col(23), A.add, A.add, ["din", "c23"], ["c10"], 4)
    ts(col(14), T.thin[:, 0:1], -1.0, None, A.mult, None, ["thin"], ["c14"], 1)
    ts(col(15), col(1), 0.0, col(14), A.is_equal, A.mult, ["c1", "c14"], ["c15"], 1)
    ts(col(16), col(1), 1.0, -0.5, A.is_equal, A.mult, ["c1"], ["c16"], 1)
    wn = {}

    def wt(name):
        wn.setdefault(name, len(wn))
        assert len(wn) <= 36
        return T.wt[:, wn[name] * 128:wn[name] * 128 + 128]
    wf = lambda j: T.wf[:, j * 128:j * 128 + 128]
    cm = T.cf[:, 0:128]
    made = set()

    def times(base, v):
        name = "%s*%r" % (base, v)
        if v == 1.0:
            return wt(base), base
        if name not in made:
            made.add(name); keep = stage[0]; stage[0] = 0
            act(wt(name), wt(base), AF.Identity, 0.0, v, [base], [name], 128); stage[0] = keep
        return wt(name), name
    ts(wt("I"), cm, col(0), None, A.is_equal, None, ["cf", "c0"], ["I"], 128)
    for j, v, use in ((0, 1.0, True), (1, 33.0, SSP), (2, 0.75 * 2.0 ** -28, not SEA)):
        if use:
            act(wf(j), wt("I"), AF.Identity, 0.0, v, ["I"], ["wf%d" % j], 128)
    ts(wt("ge"), cm, col(2), None, A.is_ge, None, ["cf", "c2"], ["ge"], 128)
    ts(wt("le"), cm, col(3), None, A.is_le, None, ["cf", "c3"], ["lew"], 128)
    tt(wt("BO"), wt("ge"), wt("le"), A.mult, ["ge", "lew"], ["BO"], 128, 2)
    act(wt("H16"), wt("BO"), AF.Identity, 0.0, col(9), ["BO", "c9"], ["H16"], 128)
    act(wt("sd"), cm, AF.Sign, col(0), -1.0, ["cf", "c0"], ["sd"], 128)
    tt(wt("sb"), wt("sd"), wt("BO"), A.mult, ["sd", "BO"], ["sb"], 128, 2)
    ts(wt("gt"), wt("sb"), 0.0, None, A.min, None, ["sb"], ["gt"], 64)
    tt(wt("TRI"), wt("gt"), times("I", 64.0)[0], A.add, ["gt", "I*64.0"], ["TRI"], 128, 2)
    ts(wt("ge"), wt("sb"), 0.0, -1.0, A.max, A.mult, ["sb", "BO"], ["ge"], 64)
    tt(wt("le"), wt("ge"), wt("I"), A.add, ["I", "ge", "BO"], ["lew"], 128, 2)
    sw = lambda j, k: T.sw[:, j * 144 + 15 - k:j * 144 + 143 - k]
    swf = lambda j: T.sw[:, j * 144:j * 144 + 144]
    ts(swf(0), T.cf[:, 0:144], col(3), None, A.is_equal, None, ["cf", "c3"], ["sw0"], 144)
    for j, v, use in ((1, -16.0, not TG), (2, U, not TW), (3, -U, not TW), (4, -U / 2, not TW)):
        if use:
            act(swf(j), swf(0), AF.Identity, 0.0, v, ["sw0"], ["sw%d" % j], 144)
    ts(T.swi[:], swf(0), col(18), None, A.mult, None, ["sw0", "c18"], ["swi"], 144, 0.5)
    act(swf(5), swf(0), AF.Identity, 0.0, col(8), ["sw0", "c8"], ["sw5"], 144)

    def rows(name, n):
        wt(name)
        return T.wt[0:n, wn[name] * 128:wn[name] * 128 + 128]
    for name, vals in (("CW", (10240.0, -32.0, 1.0 / 32)), ("CX", (2304.0, 7.5)), ("CY", (Y0 * 2 ** 21,))):
        for n in range(len(vals), 0, -1):
            ms(rows(name, n), vals[n - 1], [name])
    if SSP:
        iota(T.cj[:, 256:384], [[0, 8], [1, 16]], 0, 0, ["cj3"])
        ts(col(19), col(0), 1.0, 1024.0, A.is_equal, A.mult, ["c0"], ["c19"], 1)
        ts(col(20), col(0), 2.0, 160.0, A.is_equal, A.mult, ["c0"], ["c20"], 1)
        tt(col(21), col(19), col(20), A.add, ["c19", "c20"], ["c21"], 1)
        ts(col(22), col(0), 0.0, -2.0 ** 24, A.is_equal, A.mult, ["c0"], ["c22"], 1)
        ts(rows("CS", 128), T.cj[:, 256:384], col(21), col(22), A.mult, A.add, ["cj3", "c21", "c22"], ["CS"], 128)
    ct = lambda j, n: T.ct[:, j * 128:j * 128 + n]
    ms(T.one[:], 1.0, ["ones"], 256); ms(ct(2, 128), 144.0, ["c128"]); ms(ct(3, 128), -1.0, ["neg"])
    if not VP:
        ms(ct(1, 128), Y0 - 16, ["c176"])
    for c in range(C):
        b0 = sum(NWS[:c]) + c
        ms(T.eg[:, 16 * b0:16 * b0 + 16], 144.0, [("pad", c)])
    act(ct(4, 128), T.cj[:, 0:128], AF.Identity, col(24), 1.0, ["cj", "c24"], ["cP"], 128)
    act(ct(5, 128), T.one[:, 0:128], AF.Identity, col(16), col(15), ["ones", "c15", "c16"], ["cT1"], 128)
    for t in range(4):
        act(ct(6 + t, 128), T.one[:, 0:128], AF.Identity, 0.0, col(10 + t), ["ones", "c10"], ["cD%d" % t], 128)
    act(ct(11, 8), T.cj[:, 128:136], AF.Identity, col(7), 1.0, ["cj2", "c7"], ["cI"], 8)
    ts(T.cf[:, 144:160], T.cf[:, 0:16], col(1), -1.0, A.is_equal, A.mult, ["cf", "c1"], ["dmc"], 16)
    dm = lambda r: T.dm[:, r * 128:r * 128 + 128]
    cp(dm(0), wt("I"), ["I"], ["dm0"], 64)
    for r in range(1, 16):
        ts(dm(r), wt("le"), T.cf[:, 144 + r:145 + r], None, A.max, None, ["lew", "dmc"], ["dm%d" % r], 64)
    stage[0] = 1
    ms(T.st[:, 1024:1040], 0.0, ["st"])
    for h, s, b in ((0, "a", 2), (1, "b", 3)):
        hs = slice(h * 512, h * 512 + 512)
        ts(T.w1[:, hs], T.kin[:, hs], 32.0, None, A.mult, None, ["kin"], ["w1" + s], 512)
        act(T.ys[:, hs], T.w1[:, hs], AF.Sign, 2.0 ** 18 - 16, -1.0, ["w1" + s], ["ys" + s], 512)
        w21, k21 = times("I", 2.0 ** 21)
        mm(acc(T["pb%d" % b][:], [(wf(0), T.w1[:, hs], 1), (w21, T.yin[:, hs]), (rows("CY", 1), T.one[0:1, :])], 512), ["w1" + s, "yin", "wf0", k21, "CY", "ones"], allp(b))
        tt(T.st[:, hs], T["pb%d" % b][:], T.ys[:, hs], A.mult, allp(b) + ["ys" + s], ["st"], 512)
    stage[0] = 0
    ts(T.tnm[:], T.tin[:], 8191, None, A.bitwise_and, None, ["tin"], ["tnm"], 256)
    cp(T.lu[:, 0:256], T.tnm[:], ["tnm"], [("lu", 0, c) for c in range(C)], 256)
    ts(T.lz[:, 0:256], T.tin[:], 8192.0, None, A.is_ge, None, ["tin"], [("lz", 0, c) for c in range(C)], 256)

    def mask(es):
        return sum(1 << e for e in es)

    def send(kind, t, c, to, frm, r, w):
        s = "a%d_%d_%d" % (kind, t + 1, c)
        i = op("pool", lambda h: h.remote_dma(to, frm, T.sem[s], T.sem.sent, dst[1], dst[0], mask(eng)), r, [], 0.3, fin=False)
        sent[0] += len(eng)
        op(None, None, [], w, 0.0, sem=(s, len(eng)), lat=COMM, soft=[i])
    G = 4
    for t in range(4):
        for c in range(C):
            NW = NWS[c]; ND = NW // 16
            w0 = sum(NWS[:c]); sl = slice(w0, w0 + NW); s4 = slice(t * 256 + w0, t * 256 + w0 + NW)
            stage[0] = OFF * c + STP * t; part[:] = ["w", {}, 2 * t + c]
            K = lambda s: (s, c)
            S = lambda s: T[s][:, sl]

            def where(name):
                b, s = PLACES[BANKS][name]
                return {"A": 4 + c % 2, "S": 6 + c % 2}.get(b, b), s

            def ps(name, n=NW):
                b, s = where(name)
                return T["pb%d" % b][:, s * 128:s * 128 + n], ("P", b, s)

            def lsum(name, terms, n=NW):
                o, ko = ps(name, n); it = []; r = []
                for base, v, data, kd in terms:
                    if data is None:
                        r.append(kd); continue
                    if isinstance(base, str):
                        w, kw = times(base, v); it.append((w, data))
                    else:
                        w, kw = base, v; it.append((w, data, 1) if kw.startswith("wf") else (w, data))
                    r += [kw, kd]
                mm(acc(o, it, n), r, [ko])
                return o, ko
            ones = lambda n: T.one[0:n, 0:NW]
            x2 = t * 512 + 2 * w0
            if t == 0:
                x, fl, kx, kf = T.xin[:, sl], ct(3, NW), "xin", "neg"
            else:
                x, fl, kx = T.lx[:, x2:x2 + NW], T.lx[:, x2 + NW:x2 + 2 * NW], ("lx", t, c); kf = kx
            nu, asl = T.lu[:, s4], T.lz[:, s4]
            ku, kz = ("lu", t, c), ("lz", t, c)
            nf, kn = S("nf"), K("nf")
            ts(nf, nu, 32.0, None, A.mult, None, [ku], [kn], NW)
            xn, fo, kxn, kfo = T.xs[:, x2:x2 + NW], T.xs[:, x2 + NW:x2 + 2 * NW], ("xn", t, c), ("fo", t, c)
            big = lambda s, a, b: T[s][:, 16 * w0 + a:16 * w0 + b]
            r0 = w0 + c + 1; f0 = 16 * r0
            row = lambda q: q // 4 + 4 * (q % 4)
            fgs = lambda a, b, s="fg": T[s][:, f0 + 16 * a:f0 + 16 * b]
            fk = lambda q, s="fg": T[s][:, f0 + row(q):f0 + 16 * NW:16]
            four = lambda s, q0, a, b: T[s][:, f0 + 16 * a + q0 // 4:f0 + 16 * b:4]
            spread = lambda s, k, n: T[s][:, 16 * w0 + (k - k % n) * NW + k % n:16 * w0 + (k - k % n + n) * NW:n]
            first = t == 0 and c == 0
            wg = NW * (G0 if first else GD) // 16 // 4 * 4; n0 = t * 256 + w0
            cuts = lambda a, b, n: [z for z in [(a + (b - a) * j // n // 4 * 4, a + (b - a) * (j + 1) // n // 4 * 4 if j < n - 1 else b) for j in range(n)] if z[1] > z[0]]
            under = lambda s, a, b: [(s, c, j) for j in range(a, b, 4)]
            for a, b in cuts(0, wg, GSD):
                cp(fgs(a, b), T.ftab[:].indirect(T.lu[:, n0 + a:n0 + b]), ["ftab", ku], under("fg", a, b), 16 * (b - a), GR)
            for a, b in cuts(wg, NW, GS):
                act(fgs(a, b), T.ftab[:].indirect(T.lu[:, n0 + a:n0 + b]), AF.Copy, 0, 1, ["ftab", ku], under("fg", a, b), 16 * (b - a), GR)
            wd = NW * (16 if first else DERD) // 16 // 4 * 4
            for a, b in cuts(0, wd, ESD):
                ts(fgs(a, b, "eg"), fgs(a, b), 1.0 / 16, 143.53125, A.mult, A.add, under("fg", a, b), under("eg", a, b), 16 * (b - a), 0.5)
            for a, b in cuts(wd, NW, ES):
                act(fgs(a, b, "eg"), fgs(a, b), AF.Identity, 143.53125, 1.0 / 16, under("fg", a, b), under("eg", a, b), 16 * (b - a))
            egs = lambda q0, a, b: four("eg", q0, a, b)
            egk = lambda q: fk(q, "eg")
            keg = lambda q0, a=0, b=NW: under("eg", a, b)
            kfg = under("fg", 0, NW); ke = under("eg", 0, NW)
            act(S("za"), x, AF.Relu, 16.0, -16.0, [kx], [K("za")], NW)
            wI, wN = wt("I"), times("I", -1.0)[0]; kI = ["I", "I*-1.0"]
            zk = {}; kzg = lambda k0: [("zg", c, k, a) for k in range(k0, k0 + G) for a, _ in cuts(0, NW, HG)]
            for k0 in range(0, KA, G):
                b = GB[k0 // G % len(GB)]; it = []
                for j in range(G):
                    it += acc(T["pb%d" % b][:, j * NW:(j + 1) * NW], [(wI, fk(k0 + j)), (wN, x)], NW)
                    zk[k0 + j] = spread("zg", k0 + j, 1)
                mm(it, kfg + [kx] + kI, allp(b))
                act(big("zg", k0 * NW, (k0 + G) * NW), T["pb%d" % b][:, 0:G * NW], AF.Identity, 2311.5, 1.0, allp(b), kzg(k0), G * NW)
            if KA < 16:
                b, s = where("xp"); R = REPG * NW; s = min(s, 4 - (R + 127) // 128); kxp = [("P", b, s + j) for j in range((R + 127) // 128)]; it = []
                for j in range(REPG):
                    it += acc(T["pb%d" % b][:, s * 128 + j:s * 128 + R:REPG], [(wN, x), (rows("CX", 2), ones(2))], NW)
                mm(it, [kx, "CX", "ones"] + kI, kxp)
                for a, z in cuts(0, NW, HG):
                    for k0 in range(KA, 16, REPG):
                        tt(big("zg", k0 * NW + a * REPG, k0 * NW + z * REPG), four("fg", k0, a, z),
                           T["pb%d" % b][:, s * 128 + a * REPG:s * 128 + z * REPG], A.add, under("fg", a, z) + kxp, [("zg", c, k0 + j, a) for j in range(REPG)], (z - a) * REPG)
                for k in range(KA, 16):
                    zk[k] = spread("zg", k, REPG)

            def turned(name):
                b, s = where(name)
                return T["pb%d" % b][0:NW, s * 128:s * 128 + 128], lambda q: T["pb%d" % b][0:NW, s * 128 + row(q):s * 128 + 128:16]

            def bg(v):
                kw = times("BO", v)[1]
                return T.wt[:, wn[kw] * 128:wn[kw] * 128 + 128:16], kw

            def sq(v):
                kw = times("I", v)[1]
                return T.wt[0:NW, wn[kw] * 128:wn[kw] * 128 + NW], kw
            back = T.tr[0:NW, 128 * c:128 * c + 128]
            cn, kcn = ps("cn"); w8, k8 = times("I", 8.0); w512, k512 = times("I", 512.0)
            if TG:
                tu, tk = turned("cn")
                sums = [([(tk(k), zk[k], bg(1.0)[0], 8) for k in range(k0, k0 + G)], kzg(k0) + ["BO"]) for k0 in range(0, 16, G)]
                sums[0:0] = [([(tu, fl, w8, 128)] * (k0 == 0) + [(tk(k), egk(k), bg(-16.0)[0], 8) for k in range(k0, k0 + 4)], keg(k0) + [kf, bg(-16.0)[1], k8]) for k0 in range(0, 16, 4)]
                sums[-1:-1] = [([(tu, asl, w512, 128)], [kz, k512])]
            else:
                sums = [([(cn, sw(0, row(k)), zk[k], NW) for k in range(k0, k0 + G)], kzg(k0) + ["sw0"]) for k0 in range(0, 16, G)]
                sums[1:1] = [([(cn, sw(1, row(k)), egk(k), NW) for k in range(k0, k0 + 4)], keg(k0) + ["sw1"]) for k0 in range(0, 16, 4)]
                sums[-1:-1] = [([(cn, w8, fl, NW), (cn, w512, asl, NW)], [kf, kz, k8, k512])]
            run(sums, [kcn], "cn")
            if TG:
                act(back, tu, AF.Copy, 0.0, 1.0, [kcn], [K("tr")], 128)
                mm(acc(cn, [(back, sq(1.0)[0])], NW), [K("tr"), "I"], [kcn])
            act(S("cand"), cn, AF.Sign, 108.0, -1.0, [kcn], [K("cand")], NW)
            cP = ("I", 1.0, ct(4, NW), "cP"); tri = ("TRI", 1.0, S("cand"), K("cand"))
            (mp, kmp), (pr, kpr) = ps("mp"), ps("pr"); wb, kb = times("BO", -1.0)
            mm(acc(mp, [(wI, ct(4, NW)), (wb, S("cand"))], NW) + acc(pr, [(wI, ct(4, NW)), (wt("TRI"), S("cand"))], NW), ["I", "cP", "TRI", kb, K("cand")], [kmp, kpr])
            act(S("r2"), mp, AF.Relu, col(5), 1.0, [kmp, "c5"], [K("r2")], NW)
            tt(S("go"), pr, S("r2"), A.is_equal, [kpr, K("r2")], [K("go")], NW)
            if FALLA:
                dl, kdl = lsum("dl", [cP, tri, ("I", -1.0, S("r2"), K("r2"))])
                act(S("fall"), dl, AF.Sign, -1.0, 1.0, [kdl], [K("fall")], NW)
            else:
                tt(S("fall"), pr, S("r2"), A.is_gt, [kpr, K("r2")], [K("fall")], NW)
            ix, kix = lsum("ix", [("I", 1.0, ct(11, ND), "cI")] + [(T.swi[:, 15 - r:143 - r], "swi", T.go[:, w0 + r:w0 + NW:16], K("go")) for r in range(16)], ND)
            dsl = slice(w0 // 16, w0 // 16 + ND); d2 = 8 * c
            iu = T.iu[:, d2:d2 + ND]
            ts(iu, ix, 16.0 - HB, None, A.add, None, [kix], [K("iu")], ND)
            win = T.eg[:, f0 - 16:f0 + 16 * NW].indirect(iu)
            if EGA:
                act(S("ee"), win, AF.Copy, 0, 1, ke + [K("iu"), ("pad", c)], [K("ee")], NW, GR)
            else:
                cp(S("ee"), win, ke + [K("iu"), ("pad", c)], [K("ee")], NW, GR)
            tx = ("I", 1.0, x, kx); tza = ("I", 1.0, S("za"), K("za")); tee = ("I", -1.0, S("ee"), K("ee"))
            act(S("zc"), S("ee"), AF.Relu, 2320.0, -16.0, [K("ee")], [K("zc")], NW)
            if LED:
                ds, kds = lsum("xa", [tx, tza, ("I", 1.0, ct(2, NW), "c128"), ("I", 0.0, None, kcn)])
                tt(S("le"), ds, S("ee"), A.is_ge, [kds, K("ee")], [K("le")], NW)
            else:
                ds, kds = lsum("ds", [tx, tza, tee])
                act(S("le"), ds, AF.Relu, 145.0, 1.0, [kds], [K("le")], NW)
            d0, kd0 = lsum("d0", [tx, tee])
            au, kau = lsum("au", [("I", 1.0 / 64, x, kx), ("I", 1.0 / 64, S("za"), K("za")), ("I", 1.0 / 64, S("zc"), K("zc"))])
            tt(S("qq"), au, S("le"), A.min, [kau, K("le")], [K("qq")], NW)
            act(xn, d0, AF.Abs, 144.0, 1.0, [kd0], [kxn], NW)
            R = REP * NW
            wq, kwq = ps("wq"); tu, tk = turned("wq"); sums = {}
            term = lambda j, k, ap: (tk(k), ap, bg({2: 1.0, 3: -1.0, 4: -0.5}[j])[0], 8) if TW else (wq, sw(j, row(k)), ap, NW)
            kterm = lambda j: bg({2: 1.0, 3: -1.0, 4: -0.5}[j])[1] if TW else "sw%d" % j
            for k0 in range(0, TA, G):
                b = TB[k0 // G % len(TB)]; it = []
                for j in range(G):
                    it += acc(T["pb%d" % b][:, j * NW:(j + 1) * NW], [(wI, egk(k0 + j)), (times("I", -64.0)[0], S("qq"))], NW)
                mm(it, keg(k0) + [K("qq"), "I", "I*-64.0"], allp(b))
                act(big("ta", k0 * NW, (k0 + G) * NW), T["pb%d" % b][:, 0:G * NW], AF.Sign, -144.5, 1.0, allp(b), [("ta", c, k0, 0)], G * NW)
                sums["ta", k0] = ([term(4, k, spread("ta", k, 1)) for k in range(k0, k0 + G)], [("ta", c, k0, 0), kterm(4)])
            for nm_, b, o, wj, k1, terms in (("tb", KB, A.is_equal, 2, 0, [(S("ee"), K("ee")), (S("le"), K("le"))]),
                                             ("ta", THB, A.is_gt, 3, TA, [(ct(2, NW), "c128"), (S("qq"), K("qq"))])):
                if k1 == 16:
                    continue
                it = []; pb = T["pb%d" % b]
                for j in range(REP):
                    it += acc(pb[:, j:R:REP], [(wI, terms[0][0]), (wt("I*64.0"), terms[1][0])], NW)
                mm(it, [k for _, k in terms] + ["I", "I*64.0"], allp(b))
                for k0 in range(k1, 16, G):
                    for a, z in cuts(0, NW, HW):
                        tt(big(nm_, k0 * NW + 4 * a, k0 * NW + 4 * z), egs(k0, a, z), pb[:, 4 * a:4 * z], o, keg(k0) + allp(b), [(nm_, c, k0, a)], 4 * (z - a))
                    sums[nm_, k0] = ([term(wj, k, spread(nm_, k, REP)) for k in range(k0, k0 + G)], [(nm_, c, k0, a) for a, _ in cuts(0, NW, HW)] + [kterm(wj)])
            if TA < 16:
                seq = [("tb", k0) for k0 in range(0, 16, G)] + [("ta", k0) for k0 in range(0, 16, G)]
            else:
                seq = [(nm_, k0) for k0 in range(0, 16, G) for nm_ in ("tb", "ta")]
            fw_ = 8.0 if FALLA else 16.0
            if TW:
                (wa, ka_), (wb, kb_) = times("I", 16.0), times("I", fw_)
                run([([(tu, asl, wa, 128), (tu, S("fall"), wb, 128)], [kz, K("fall"), kxn, K("qq"), ka_, kb_])] + [sums[z] for z in seq], [kwq], "wq")
                act(back, tu, AF.Copy, 0.0, 1.0, [kwq], [K("tr")], 128)
                if WQB is None:
                    lsum("wq", [("I", U, ct(6 + t, NW), "cD%d" % t), (wf(0), "wf0", nf, kn), (back, K("tr")[0], sq(U)[0], K("tr"))])
                else:
                    wq, kwq = T["pb%d" % WQB][:, 0:NW], ("P", WQB, 0); wu, ku_ = times("I", U)
                    run([([(wq, wu, ct(6 + t, NW), NW), (wq, wf(0), nf, 4 * NW)], [kn, "wf0", ku_, "cD%d" % t]), ([(wq, back, sq(U)[0], NW)], [K("tr")])], [kwq], "wq")
            else:
                (wu, ku_), (wa, ka_), (wb, kb_) = times("I", U), times("I", 16 * U), times("I", fw_ * U)
                gs = [sums[z] for z in seq]
                gs[0] = (gs[0][0], gs[0][1] + [kxn, K("qq")])
                gs[1:1] = [([(wq, wu, ct(6 + t, NW), NW), (wq, wf(0), nf, 4 * NW)], [kn, "wf0", ku_, "cD%d" % t])]
                run(gs + [([(wq, wa, asl, NW), (wq, wb, S("fall"), NW)], [kz, K("fall"), ka_, kb_])], [kwq], "wq")
            txn = ("I", -1.0, xn, kxn); th16 = ("H16", 1.0, xn, kxn)
            ud, kud = lsum("ud", [(sw(5, r), "sw5", T.xs[:, x2 + r:x2 + NW:16], kxn) for r in range(16)], ND)
            u0, ku0 = lsum("u0", [th16])
            ts(T.cd0[:, dsl], ud, 241.0, None, A.mult, None, [kud], [K("cd0")], ND)
            ts(T.cd[:, dsl], T.cd0[:, dsl], 6, 1023, A.logical_shift_right, A.bitwise_and, [K("cd0")], [K("cd")], ND)
            cu = T.cu[:, d2:d2 + ND]
            cp(cu, T.cd[:, dsl], [K("cd")], [K("cu")], ND)
            act(S("hi"), u0, AF.Identity, 159.5 + 1.0 / 2048, 1.0 / 64, [ku0], [K("hi")], NW)
            v2, kv2 = lsum("v2", [th16, (rows("CW", 3), "CW", ones(3), "ones"), ("I", -64.0, S("hi"), K("hi"))])
            tt(S("pp"), v2, nf, A.mult, [kv2, kn], [K("pp")], NW)
            ss, kss = u0, ku0
            if SSP:
                lsum("u0", [(rows("CS", 3), "CS", ones(3), "ones"), (wf(1), "wf1", nf, kn), (wf(0), "wf0", S("pp"), K("pp"))])
            else:
                act(u0, nf, AF.Identity, col(4), 33.0, [kn, "c4"], [ku0], NW)
                if AAP:
                    ss, kss = S("ss"), K("ss")
                tt(ss, u0, S("pp"), A.add, [ku0, K("pp")], [kss], NW)
            act(S("yq"), T.st[:].indirect(cu), AF.Abs, 0.0, 2.0 ** -21, ["st", K("cu")], [K("yq")], NW, GR)
            act(S("wg"), T.st[:].indirect(cu), AF.Copy, 0.0, 1.0, ["st", K("cu")], [K("wg")], NW, GR)
            tyq = ("I", 1.0, S("yq"), K("yq"))
            dy, kdy = lsum("dy", [txn, tyq])
            act(S("ad"), dy, AF.Abs, -Y0, 1.0, [kdy], [K("ad")], NW)
            sn, ksn = lsum("sn", [("BO", -2.0 ** 30, ct(5, NW), "cT1"), ("BO", -2.0 ** 30, S("ad"), K("ad"))])
            act(fo, sn, AF.Sign, 0.0, 1.0, [ksn], [kfo], NW)
            if AAP:
                ap, kap = lsum("ap", [(wf(0), "wf0", S("wg"), K("wg")), ("I", -2.0 ** 29, T.one[:, 0:NW], "ones"), ("I", 2.0 ** 29, fo, kfo)])
                tt(S("m0"), ap, ss, A.max, [kap, kss], [K("m0")], NW)
            else:
                tt(S("aa"), sn, S("wg"), A.min, [ksn, K("wg")], [K("aa")], NW)
                tt(S("m0"), ss, S("aa"), A.max, [kss, K("aa")], [K("m0")], NW)
            if t < 3:
                send(0, t, c, T.lx[:, x2 + 512:x2 + 512 + 2 * NW], T.xs[:, x2:x2 + 2 * NW], [kxn, kfo], [("lx", t + 1, c)])
            tt(S("mi"), wq, S("m0"), A.max, [kwq, K("m0")], [K("mi")], NW)
            ts(S("fi"), S("mi"), 8191 * 32, None, A.bitwise_and, None, [K("mi")], [K("fi")], NW)
            zo, uo = T.zs[:, s4], T.us[:, s4]; kzo, kuo = ("zs", t, c), ("us", t, c)
            n4 = (t + 1) * 256 + w0
            if t < 3:
                ts(uo, S("fi"), 1.0 / 32, None, A.mult, None, [K("fi")], [kuo], NW)
                send(1, t, c, T.lu[:, n4:n4 + NW], uo, [kuo], [("lu", t + 1, c)])
            if KAP:
                act(S("sa"), wq, AF.Sign, 0.0, 1.0, [kwq], [K("sa")], NW)
                ka, kka = lsum("ka", [(wf(0), "wf0", nf, kn), ("I", -2.0 ** 20, T.one[:, 0:NW], "ones"), ("I", 2.0 ** 20, S("sa"), K("sa"))])
            else:
                ka, kka = ps("ka")
                tt(ka, wq, nf, A.min, [kwq, kn], [kka], NW)
            tt(zo, ka, S("fi"), A.is_equal, [kka, K("fi")], [kzo], NW)
            if t < 3:
                send(2, t, c, T.lz[:, n4:n4 + NW], zo, [kzo], [("lz", t + 1, c)])
            else:
                ts(S("yn"), S("fi"), 1.0 / 32, None, A.mult, None, [K("fi")], [K("yn")], NW)
                zp, kzp = lsum("zp", [("I", 8192.0, zo, kzo)])
                tt(S("yts"), zp, S("yn"), A.add, [kzp, K("yn")], [K("yts")], NW)
                dma("sp", T.yt[:, sl], S("yts"), [K("yts")], [], 0.3)
                dma("sp", T.yx[:, sl], xn, [kxn], [], 0.3)
            stage[0] = ENT + STP * t
            if SEA:
                act(S("se"), S("wg"), AF.Sign, 0.0, 1.0, [K("wg")], [K("se")], NW)
            sg, ksg = lsum("sg", [("I", 1.0, S("se"), K("se")) if SEA else (wf(2), "wf2", S("wg"), K("wg")), ("I", -1.0, fo, kfo), ("I", 4.0, zo, kzo)])
            act(S("sg"), sg, AF.Sign, -3.0, 1.0, [ksg], [K("sg")], NW)
            e2, ke2 = lsum("d2", [txn, tyq, ("I", 32.0, fo, kfo)])
            act(S("hd"), e2, AF.Relu, -Y0, 1.0, [ke2], [K("hd")], NW)
            terms = [("I", 2.0 ** 21, xn, kxn), ("I", -2.0 ** 25, fo, kfo), ("I", 2.0 ** 21, S("hd"), K("hd"))]
            if VP:
                vv, kvv = lsum("vv", terms + [(wf(0), "wf0", nf, kn)])
                act(S("vv"), vv, AF.Identity, (Y0 - 16) * 2 ** 21, 1.0, [kvv], [K("vv")], NW)
            else:
                vv, kvv = lsum("vv", terms + [("I", 2.0 ** 21, ct(1, NW), "c176")])
                tt(S("vv"), vv, nf, A.add, [kvv, kn], [K("vv")], NW)
        part[:] = ["s", {}, 2 * t + 1]
        for cs in ([[c] for c in range(C)] if t >= SPLIT else [list(range(C))]):
            al = lambda s: [(s, c) for c in cs]
            a, n = sum(NWS[:cs[0]]) // 16, sum(NWS[c] for c in cs) // 16; ws = slice(16 * a, 16 * (a + n))
            if t >= SPLIT:
                stage[0] = OFF * cs[0] + STP * t
            pb = T["pb%d" % DB]; w2, k2 = times("I", 2048.0)
            ts(T.cdh[:, a:a + n], T.cd[:, a:a + n], 1.0, None, A.add, None, al("cd"), al("cdh"), n)
            mm([(pb[:, r:16 * n:16], dm(r), T.cdh[:, a:a + n], True, True, n) for r in range(16)], al("cdh") + ["dm%d" % r for r in range(16)], allp(DB))
            ts(T.eq[:, ws], pb[:, 0:16 * n], 0.0, None, A.is_equal, None, allp(DB), al("eq"), 16 * n)
            lo = pb[:, 0:n]
            mm(acc(lo, [(dm(0), T.cdh[:, a:a + n])] + [(w2, T.eq[:, 16 * a + r:16 * (a + n):16]) for r in range(1, 16)], n),
               al("eq") + al("cdh") + ["dm0", k2], allp(DB))
            ts(T.off[:, 2 * a:2 * (a + n):2], lo, -1.0, col(6), A.add, A.min, allp(DB) + ["c6"], al("off"), n)
        for b in range(16):
            c = max(j for j in range(C) if sum(NWS[:j]) <= 16 * b)
            tt(T.st[:].indirect(T.off[:, 2 * b:2 * b + 1]), T.vv[:, 16 * b:16 * b + 16], T.sg[:, 16 * b:16 * b + 16], A.mult,
               [("off", c), ("vv", c), ("sg", c)], ["st"], 16, SC)
    part[:] = ["z", {}, 8]
    for h in range(4):
        hs = slice(h * 256, h * 256 + 256); k = lambda s: (s, "o", h)
        ts(T.wi[:, hs], T.st[:, hs], 2.0 ** 18, None, A.max, None, ["st"], [k("wi")], 256)
        ts(T.wj[:, hs], T.wi[:, hs], 5, 16383, A.logical_shift_right, A.bitwise_and, [k("wi")], [k("wj")], 256)
        cp(T.w1[:, hs], T.wj[:, hs], [k("wj")], [k("w1"), "w1" + "ab"[h // 2]], 256)
        act(T.ys[:, hs], T.st[:, hs], AF.Abs, 0.0, 2.0 ** -21, ["st"], [k("ys"), "ys" + "ab"[h // 2]], 256)
        act(T.yo[:, hs], T.ys[:, hs], AF.Identity, -Y0, 1.0, [k("ys")], [k("yo")], 256)
        dma("sp", T.yk[:, hs], T.w1[:, hs], [k("w1")], [], 0.4)
        if h % 2:
            h2 = slice(h * 256 - 256, h * 256 + 256)
            dma("act", T.yy[:, h2], T.yo[:, h2], [k("yo"), ("yo", "o", h - 1)], [], 0.4)
    return ops, sent[0]


def rank_program(g, core, T, topo):
    rank = T.rank_of(core)
    if rank is None:
        return
    nxt = T.cores[(rank + 1) % len(T.cores)]
    assert topo.may_write(core, nxt)
    ops, sent = build(T, topo.addr(nxt), topo.engines(core, nxt)[:8])
    order, _ = plan(ops)
    for s, v in emit(g, T, ops, order):
        g.wait_ge(T.sem[s], v)
    g.wait_ge(T.sem.sent, sent)
